import numpy as np
import ml_dtypes


def mxq(x, axis, fmt="e4m3"):
    dtype, down = {"e4m3": (ml_dtypes.float8_e4m3fn, 7), "e5m2": (ml_dtypes.float8_e5m2, 14)}[fmt]
    v = np.moveaxis(np.asarray(x, np.float32).astype(ml_dtypes.bfloat16).astype(np.float64), axis, -1)
    blocks = v.reshape(v.shape[:-1] + (-1, 32))
    amax = np.abs(blocks).max(-1, keepdims=True)
    byte = np.maximum(np.where(amax > 0, np.frexp(amax)[1] - 1 + 127, 0) - down, 1)
    scale = np.exp2(byte - 127.0)
    codes = (blocks / scale).astype(np.float32).astype(dtype).astype(np.float64)
    return np.moveaxis((codes * scale).reshape(v.shape), -1, axis)


WIDE = False


def mx_kscale(k):
    if not WIDE:
        return np.ones(k)
    levels = np.array([18, -18])
    if k % 512:
        return np.exp2(np.random.permutation(np.resize(levels, k // 32))).repeat(32)
    a = np.empty((k // 512, 16))
    for p in range(k // 512):
        a[p, :8] = np.random.permutation(np.resize(levels, 8))
        for g in range(8):
            far = levels[np.abs(levels - a[p, g]) >= 10]
            a[p, g + 8] = far[np.random.randint(len(far))]
    return np.exp2(a.ravel()).repeat(32)


def f64(x):
    return np.asarray(x).astype(np.float64)


def striped(idx):
    return np.tile(np.asarray(idx).reshape(-1, 16).T, (8, 1)).astype(np.uint16)


def unstriped(offs):
    return offs[:16].T.reshape(-1).astype(np.int64)


def setup_inputs():
    n = np.random.standard_normal
    uni = np.random.uniform
    idx = np.random.permutation(2048)[:1024]
    bag = np.random.permutation(np.repeat(np.arange(512), 2))
    slot = np.argsort(bag, kind="stable")
    al_ = np.random.dirichlet(np.ones(2), 512).reshape(-1)[np.argsort(np.argsort(bag, kind="stable"), kind="stable")]
    f_m = mx_kscale(512)
    return {
        "eT": (n((512, 2048)) / np.sqrt(512)).astype(np.float32),
        "W": (n((512, 512)) / np.sqrt(512) * f_m[:, None]).astype(np.float32),
        "dz": (n((512, 512)) / f_m[:, None]).astype(np.float32),
        "al": np.tile(al_, (128, 1)).astype(np.float32),
        "offs": striped(idx),
        "bagoffs": striped(bag),
        "slotoffs": striped(slot),
    }


def reference(eT, W, dz, al, offs, bagoffs, slotoffs):
    idx = unstriped(offs)
    bag = unstriped(bagoffs)
    slot = unstriped(slotoffs)
    eT_c = f64(eT)[:, idx]
    u = mxq(f64(W), 0, "e4m3").T @ mxq(f64(dz), 0, "e5m2")
    ub = u[:, bag]
    de = f64(al)[:1] * ub
    out_0 = np.zeros((512, 2048))
    out_0[:, idx] = de
    ubt = ub.T
    et = eT_c.T
    dal = (ubt * et).sum(-1, keepdims=True)
    dar = dal.T
    w = f64(al)[:1] * dar
    wsl = w[:, slot]
    sb = wsl.reshape(1, 512, 2).sum(-1)
    sbc = sb[:, bag]
    out_1 = f64(al)[:1] * (dar - sbc)
    return out_0, out_1

@@ -1,0 +1,188 @@
+from contextlib import ExitStack
+
+import concourse.mybir as mybir
+from concourse.masks import make_identity
+
+F32 = mybir.dt.float32
+BF16 = mybir.dt.bfloat16
+U32 = mybir.dt.uint32
+U16 = mybir.dt.uint16
+U8 = mybir.dt.uint8
+E4M3X4 = mybir.dt.float8_e4m3fn_x4
+E5M2X4 = mybir.dt.float8_e5m2_x4
+MULT = mybir.AluOpType.mult
+ADD = mybir.AluOpType.add
+SUBTRACT = mybir.AluOpType.subtract
+COPY = mybir.ActivationFunctionType.Copy
+
+P = 128
+PACK = 4
+M, D, C, T, X = 512, 512, 1024, 2048, 512
+BLOCKS = D // P
+CHUNKS = C // P
+BANK = 512
+WIDE = C + 16
+HALF = X // 2
+DZ_SPLIT = 160
+
+FLOPS = 2 * M * D * X
+
+
+def interleave(engine_copy, grouped, raw, lo, hi):
+    engine_copy(
+        grouped[:, lo:hi, :].rearrange("p (c i) t -> p c t i", i=4),
+        raw[:, :, lo:hi].rearrange("p t (c i) -> p c t i", i=4),
+    )
+
+
+def tile_attend_gmil_kernel(tc, eT, W, dz, al, offs, bagoffs, slotoffs, out_0, out_1):
+    nc = tc.nc
+    with ExitStack() as ctx:
+        keep = ctx.enter_context(tc.tile_pool(name="keep", bufs=1))
+        psum = ctx.enter_context(tc.psum_pool(name="psum", bufs=1))
+
+        dz_rows = dz.rearrange("(p j) x -> p j x", j=PACK)
+        w_rows = W.rearrange("(p j) d -> p j d", j=PACK)
+
+        dz_a = keep.tile([P, PACK, HALF], F32, name="dz_a")
+        dz_b = keep.tile([P, PACK, HALF], F32, name="dz_b")
+        w_first = keep.tile([P, PACK, P], F32, name="w_first")
+        w_rest = keep.tile([P, PACK, D - P], F32, name="w_rest")
+        alpha = keep.tile([P, C], F32, name="alpha")
+        idx_list = keep.tile([P, C // 16], U16, name="idx_list")
+        bag_list = keep.tile([P, C // 16], U16, name="bag_list")
+        slot_list = keep.tile([P, C // 16], U16, name="slot_list")
+        emb = [keep.tile([P, T], F32, name=f"emb{b}") for b in range(BLOCKS)]
+
+        nc.sync.dma_start(dz_a[:], dz_rows[:, :, :HALF])
+        nc.sync.dma_start(w_first[:], w_rows[:, :, :P])
+        nc.sync.dma_start(dz_b[:], dz_rows[:, :, HALF:])
+        nc.sync.dma_start(bag_list[:], bagoffs)
+        nc.sync.dma_start(alpha[:], al)
+        nc.sync.dma_start(idx_list[:], offs)
+        nc.sync.dma_start(w_rest[:], w_rows[:, :, P:])
+        for b in range(BLOCKS):
+            nc.sync.dma_start(emb[b][:], eT[b * P : (b + 1) * P, :])
+        nc.sync.dma_start(slot_list[:], slotoffs)
+
+        places = [keep.tile([P, T], F32, name=f"places{i}") for i in range(2)]
+        u = [keep.tile([P, WIDE], F32, name=f"u{b}") for b in range(BLOCKS)]
+        bag_sum = keep.tile([P, WIDE], F32, name="bag_sum")
+        nc.vector.memset(u[0][:, X:], 0.0)
+        nc.vector.memset(places[0][:], 0.0)
+        nc.vector.memset(places[1][:], 0.0)
+        for b in range(1, BLOCKS):
+            nc.vector.memset(u[b][:, X:], 0.0)
+        nc.gpsimd.memset(bag_sum[:, X:], 0.0)
+        identity = keep.tile([P, P], F32, name="identity")
+        make_identity(nc, identity[:])
+
+        dz_a16 = keep.tile([P, HALF, PACK], BF16, name="dz_a16", align_bytes=64)
+        dz_b16 = keep.tile([P, HALF, PACK], BF16, name="dz_b16", align_bytes=64)
+        w_first16 = keep.tile([P, P, PACK], BF16, name="w_first16", align_bytes=64)
+        w_rest16 = keep.tile([P, D - P, PACK], BF16, name="w_rest16", align_bytes=64)
+        dz_codes = keep.tile([P, X], U32, name="dz_codes", align_bytes=64)
+        dz_scales = keep.tile([P, X], U8, name="dz_scales", align_bytes=64)
+        w_codes = keep.tile([P, D], U32, name="w_codes", align_bytes=64)
+        w_scales = keep.tile([P, D], U8, name="w_scales", align_bytes=64)
+
+        def quantize(codes, scales, fmt, first, grouped):
+            width = grouped.shape[1]
+            nc.vector.quantize_mx(
+                out=codes[:, first : first + width].bitcast(fmt),
+                scales=scales[:, first : first + width],
+                in_=grouped.rearrange("p c t -> p (c t)"),
+            )
+
+        def product(b, copy_out):
+            acc = psum.tile([P, BANK], F32, name=f"acc{b}")
+            cols = slice(b * P, (b + 1) * P)
+            nc.tensor.matmul_mx(
+                out=acc[:],
+                lhsT=w_codes[:, cols].bitcast(E4M3X4),
+                lhsT_scale=w_scales[:, cols],
+                rhs=dz_codes[:].bitcast(E5M2X4),
+                rhs_scale=dz_scales[:],
+                start=True,
+                stop=True,
+            )
+            copy_out(u[b][:, :X], acc[:])
+
+        interleave(nc.scalar.copy, dz_a16, dz_a, 0, HALF)
+        interleave(nc.vector.tensor_copy, w_first16, w_first, 0, P)
+        quantize(w_codes, w_scales, E4M3X4, 0, w_first16[:])
+        quantize(dz_codes, dz_scales, E5M2X4, 0, dz_a16[:])
+        interleave(nc.vector.tensor_copy, dz_b16, dz_b, 0, DZ_SPLIT)
+        interleave(nc.scalar.copy, dz_b16, dz_b, DZ_SPLIT, HALF)
+        quantize(dz_codes, dz_scales, E5M2X4, HALF, dz_b16[:])
+        product(0, nc.scalar.copy)
+
+        de = [keep.tile([P, C], F32, name=f"de{b}") for b in range(BLOCKS)]
+        prod = [keep.tile([P, C], F32, name=f"prod{b}") for b in range(BLOCKS)]
+
+        def look_up_u(b):
+            nc.vector.tensor_tensor(de[b][:], u[b][:].indirect(bag_list[:]), alpha[:], MULT)
+
+        def look_up_emb(b):
+            nc.vector.tensor_tensor(prod[b][:], emb[b][:].indirect(idx_list[:]), de[b][:], MULT)
+
+        def put(b):
+            window = places[b % 2]
+            nc.vector.tensor_copy(window[:].indirect(idx_list[:]), de[b][:])
+            nc.sync.dma_start(out_0[b * P : (b + 1) * P, :], window[:])
+
+        look_up_u(0)
+        put(0)
+        interleave(nc.scalar.copy, w_rest16, w_rest, 0, D - P)
+        quantize(w_codes, w_scales, E4M3X4, P, w_rest16[:, :P, :])
+        quantize(w_codes, w_scales, E4M3X4, 2 * P, w_rest16[:, P:, :])
+        for b in range(1, BLOCKS):
+            product(b, lambda dst, src: nc.scalar.activation(dst, src, COPY))
+        look_up_emb(0)
+        look_up_u(1)
+        put(1)
+        look_up_emb(1)
+        for b in range(2, BLOCKS):
+            look_up_u(b)
+            look_up_emb(b)
+
+        w_cols = keep.tile([P, CHUNKS], F32, name="w_cols")
+        spent = keep.tile([P, P], F32, name="spent")
+        w_row = keep.tile([P, C], F32, name="w_row")
+        turned = [psum.tile([P, BANK], F32, name=f"turned{h}") for h in range(2)]
+        spread = [psum.tile([P, BANK], F32, name=f"spread{h}") for h in range(2)]
+        for k in range(CHUNKS):
+            dst = turned[k // 4][:, (k % 4) * P : (k % 4 + 1) * P]
+            for b in range(BLOCKS):
+                nc.tensor.matmul(
+                    dst, prod[b][:, k * P : (k + 1) * P], identity[:],
+                    start=(b == 0), stop=(b == BLOCKS - 1), is_transpose=True,
+                )
+        for k in range(CHUNKS):
+            src = turned[k // 4][:, (k % 4) * P : (k % 4 + 1) * P]
+            nc.scalar.activation(spent[:], src, COPY, accum_out=w_cols[:, k : k + 1])
+        for k in range(CHUNKS):
+            nc.tensor.transpose(
+                spread[k // 4][:, (k % 4) * P : (k % 4 + 1) * P],
+                w_cols[:, k : k + 1].to_broadcast([P, P]),
+                identity[:],
+            )
+        for h in range(2):
+            nc.scalar.copy(w_row[:, h * BANK : (h + 1) * BANK], spread[h][:])
+
+        put(2)
+        put(3)
+
+        by_bag = keep.tile([P, X, 2], F32, name="by_bag")
+        by_bag_flat = by_bag[:].rearrange("p x j -> p (x j)")
+        for h in range(2):
+            nc.vector.tensor_copy(
+                by_bag_flat[:, h * BANK : (h + 1) * BANK],
+                w_row[:].indirect(slot_list[:, h * 32 : (h + 1) * 32]),
+            )
+        nc.vector.tensor_tensor(bag_sum[:, :X], by_bag[:, :, 0], by_bag[:, :, 1], ADD)
+        taken = keep.tile([P, C], F32, name="taken")
+        nc.vector.tensor_tensor(taken[:], bag_sum[:].indirect(bag_list[:]), alpha[:], MULT)
+        result = keep.tile([P, C], F32, name="result")
+        nc.vector.tensor_tensor(result[0:1, :], w_row[0:1, :], taken[0:1, :], SUBTRACT)
+        nc.sync.dma_start(out_1, result[0:1, :])

@@ -11,7 +11,6 @@ U8 = mybir.dt.uint8
 E4M3X4 = mybir.dt.float8_e4m3fn_x4
 E5M2X4 = mybir.dt.float8_e5m2_x4
 MULT = mybir.AluOpType.mult
-ADD = mybir.AluOpType.add
 SUBTRACT = mybir.AluOpType.subtract
 COPY = mybir.ActivationFunctionType.Copy
 
@@ -21,7 +20,8 @@ M, D, C, T, X = 512, 512, 1024, 2048, 512
 BLOCKS = D // P
 CHUNKS = C // P
 BANK = 512
-WIDE = C + 16
+U_WINDOW = 1376
+SUM_WINDOW = X + 16
 HALF = X // 2
 DZ_SPLIT = 160
 
@@ -47,7 +47,7 @@ def tile_attend_gmil_kernel(tc, eT, W, dz, al, offs, bagoffs, slotoffs, out_0, o
         dz_a = keep.tile([P, PACK, HALF], F32, name="dz_a")
         dz_b = keep.tile([P, PACK, HALF], F32, name="dz_b")
         w_first = keep.tile([P, PACK, P], F32, name="w_first")
-        w_rest = keep.tile([P, PACK, D - P], F32, name="w_rest")
+        w_rest = keep.tile([P, PACK, D - P], F32, name="w_rest", tag="second_places")
         alpha = keep.tile([P, C], F32, name="alpha")
         idx_list = keep.tile([P, C // 16], U16, name="idx_list")
         bag_list = keep.tile([P, C // 16], U16, name="bag_list")
@@ -65,14 +65,11 @@ def tile_attend_gmil_kernel(tc, eT, W, dz, al, offs, bagoffs, slotoffs, out_0, o
             nc.sync.dma_start(emb[b][:], eT[b * P : (b + 1) * P, :])
         nc.sync.dma_start(slot_list[:], slotoffs)
 
-        places = [keep.tile([P, T], F32, name=f"places{i}") for i in range(2)]
-        u = [keep.tile([P, WIDE], F32, name=f"u{b}") for b in range(BLOCKS)]
-        bag_sum = keep.tile([P, WIDE], F32, name="bag_sum")
-        nc.vector.memset(u[0][:, X:], 0.0)
-        nc.vector.memset(places[0][:], 0.0)
-        nc.vector.memset(places[1][:], 0.0)
-        for b in range(1, BLOCKS):
-            nc.vector.memset(u[b][:, X:], 0.0)
+        first_places = keep.tile([P, T], F32, name="first_places")
+        u = keep.tile([P, (BLOCKS - 1) * X + U_WINDOW], F32, name="u")
+        bag_sum = keep.tile([P, SUM_WINDOW], F32, name="bag_sum")
+        nc.vector.memset(u[:, BLOCKS * X :], 0.0)
+        nc.vector.memset(first_places[:], 0.0)
         nc.gpsimd.memset(bag_sum[:, X:], 0.0)
         identity = keep.tile([P, P], F32, name="identity")
         make_identity(nc, identity[:])
@@ -94,8 +91,14 @@ def tile_attend_gmil_kernel(tc, eT, W, dz, al, offs, bagoffs, slotoffs, out_0, o
                 in_=grouped.rearrange("p c t -> p (c t)"),
             )
 
+        def bank(i, name):
+            return psum.tile([P, BANK], F32, name=name, tag=f"bank{i}")
+
+        def u_first(b):
+            return (BLOCKS - 1 - b) * X
+
         def product(b, copy_out):
-            acc = psum.tile([P, BANK], F32, name=f"acc{b}")
+            acc = bank(b, f"acc{b}")
             cols = slice(b * P, (b + 1) * P)
             nc.tensor.matmul_mx(
                 out=acc[:],
@@ -106,7 +109,7 @@ def tile_attend_gmil_kernel(tc, eT, W, dz, al, offs, bagoffs, slotoffs, out_0, o
                 start=True,
                 stop=True,
             )
-            copy_out(u[b][:, :X], acc[:])
+            copy_out(u[:, u_first(b) : u_first(b) + X], acc[:])
 
         interleave(nc.scalar.copy, dz_a16, dz_a, 0, HALF)
         interleave(nc.vector.tensor_copy, w_first16, w_first, 0, P)
@@ -117,72 +120,107 @@ def tile_attend_gmil_kernel(tc, eT, W, dz, al, offs, bagoffs, slotoffs, out_0, o
         quantize(dz_codes, dz_scales, E5M2X4, HALF, dz_b16[:])
         product(0, nc.scalar.copy)
 
-        de = [keep.tile([P, C], F32, name=f"de{b}") for b in range(BLOCKS)]
+        ub = [keep.tile([P, C], F32, name=f"ub{b}") for b in range(BLOCKS)]
         prod = [keep.tile([P, C], F32, name=f"prod{b}") for b in range(BLOCKS)]
 
         def look_up_u(b):
-            nc.vector.tensor_tensor(de[b][:], u[b][:].indirect(bag_list[:]), alpha[:], MULT)
+            window = u[:, u_first(b) : u_first(b) + U_WINDOW]
+            nc.vector.tensor_copy(ub[b][:], window.indirect(bag_list[:]))
 
-        def look_up_emb(b):
-            nc.vector.tensor_tensor(prod[b][:], emb[b][:].indirect(idx_list[:]), de[b][:], MULT)
-
-        def put(b):
-            window = places[b % 2]
-            nc.vector.tensor_copy(window[:].indirect(idx_list[:]), de[b][:])
+        def put(b, window):
+            nc.vector.tensor_tensor(window[:].indirect(idx_list[:]), ub[b][:], alpha[:], MULT)
             nc.sync.dma_start(out_0[b * P : (b + 1) * P, :], window[:])
 
+        def first_columns(dst, src, count):
+            nc.scalar.copy(dst, src[:].rearrange("p (k q) -> p k q", q=P)[:, :count, 0])
+
+        def spread(dst, column):
+            nc.tensor.transpose(dst, column.to_broadcast([P, P]), identity[:])
+
         look_up_u(0)
-        put(0)
+        put(0, first_places)
         interleave(nc.scalar.copy, w_rest16, w_rest, 0, D - P)
         quantize(w_codes, w_scales, E4M3X4, P, w_rest16[:, :P, :])
         quantize(w_codes, w_scales, E4M3X4, 2 * P, w_rest16[:, P:, :])
         for b in range(1, BLOCKS):
             product(b, lambda dst, src: nc.scalar.activation(dst, src, COPY))
-        look_up_emb(0)
-        look_up_u(1)
-        put(1)
-        look_up_emb(1)
-        for b in range(2, BLOCKS):
-            look_up_u(b)
-            look_up_emb(b)
 
-        w_cols = keep.tile([P, CHUNKS], F32, name="w_cols")
-        spent = keep.tile([P, P], F32, name="spent")
-        w_row = keep.tile([P, C], F32, name="w_row")
-        turned = [psum.tile([P, BANK], F32, name=f"turned{h}") for h in range(2)]
-        spread = [psum.tile([P, BANK], F32, name=f"spread{h}") for h in range(2)]
-        for k in range(CHUNKS):
-            dst = turned[k // 4][:, (k % 4) * P : (k % 4 + 1) * P]
-            for b in range(BLOCKS):
+        alpha_cols = keep.tile([P, CHUNKS], F32, name="alpha_cols")
+        for h in range(2):
+            alpha_turned = bank(BLOCKS + h, f"alpha_turned{h}")
+            for q in range(4):
+                k = 4 * h + q
+                nc.tensor.transpose(alpha_turned[:, q * P : (q + 1) * P], alpha[:, k * P : (k + 1) * P], identity[:])
+            first_columns(alpha_cols[:, 4 * h : 4 * h + 4], alpha_turned, 4)
+
+        turned = [bank(k, f"turned{k}") for k in range(CHUNKS)]
+
+        def look_up_emb(b):
+            nc.vector.tensor_tensor(prod[b][:], emb[b][:].indirect(idx_list[:]), ub[b][:], MULT)
+            for k in range(CHUNKS):
                 nc.tensor.matmul(
-                    dst, prod[b][:, k * P : (k + 1) * P], identity[:],
+                    turned[k][:, :P], prod[b][:, k * P : (k + 1) * P], identity[:],
                     start=(b == 0), stop=(b == BLOCKS - 1), is_transpose=True,
                 )
+
+        look_up_emb(0)
+        look_up_u(1)
+        second_places = keep.tile([P, T], F32, name="second_places", tag="second_places")
+        nc.gpsimd.memset(second_places[:], 0.0)
+        put(1, second_places)
+        look_up_u(2)
+        look_up_u(3)
+        for b in range(1, BLOCKS):
+            look_up_emb(b)
+
+        w_cols = keep.tile([P, CHUNKS], F32, name="w_cols", tag="last_places")
+        spent = keep.tile([P, P], F32, name="spent")
+        w_row = keep.tile([P, C], F32, name="w_row")
         for k in range(CHUNKS):
-            src = turned[k // 4][:, (k % 4) * P : (k % 4 + 1) * P]
-            nc.scalar.activation(spent[:], src, COPY, accum_out=w_cols[:, k : k + 1])
-        for k in range(CHUNKS):
-            nc.tensor.transpose(
-                spread[k // 4][:, (k % 4) * P : (k % 4 + 1) * P],
-                w_cols[:, k : k + 1].to_broadcast([P, P]),
-                identity[:],
+            nc.scalar.activation(
+                spent[:], turned[k][:, :P], COPY, scale=alpha_cols[:, k : k + 1], accum_out=w_cols[:, k : k + 1]
             )
         for h in range(2):
-            nc.scalar.copy(w_row[:, h * BANK : (h + 1) * BANK], spread[h][:])
+            w_spread = bank(h, f"w_spread{h}")
+            for q in range(4):
+                k = 4 * h + q
+                spread(w_spread[:, q * P : (q + 1) * P], w_cols[:, k : k + 1])
+            nc.scalar.copy(w_row[:, h * BANK : (h + 1) * BANK], w_spread[:])
 
-        put(2)
-        put(3)
+        put(2, first_places)
 
-        by_bag = keep.tile([P, X, 2], F32, name="by_bag")
-        by_bag_flat = by_bag[:].rearrange("p x j -> p (x j)")
+        by_bag = keep.tile([P, C], F32, name="by_bag")
         for h in range(2):
             nc.vector.tensor_copy(
-                by_bag_flat[:, h * BANK : (h + 1) * BANK],
+                by_bag[:, h * BANK : (h + 1) * BANK],
                 w_row[:].indirect(slot_list[:, h * 32 : (h + 1) * 32]),
             )
-        nc.vector.tensor_tensor(bag_sum[:, :X], by_bag[:, :, 0], by_bag[:, :, 1], ADD)
+
+        last_places = keep.tile([P, T], F32, name="last_places", tag="last_places")
+        nc.gpsimd.memset(last_places[:], 0.0)
+        put(3, last_places)
+
+        pair_sums = bank(2, "pair_sums")
+        for q in range(4):
+            for j in range(2):
+                nc.tensor.matmul(
+                    pair_sums[:, q * P : (q + 1) * P], by_bag[:, 2 * q * P + j : 2 * (q + 1) * P : 2], identity[:],
+                    start=(j == 0), stop=(j == 1), is_transpose=True,
+                )
+        sum_cols = keep.tile([P, 4], F32, name="sum_cols")
+        first_columns(sum_cols[:], pair_sums, 4)
+        sum_spread = bank(3, "sum_spread")
+        for q in range(4):
+            spread(sum_spread[:, q * P : (q + 1) * P], sum_cols[:, q : q + 1])
+        nc.scalar.copy(bag_sum[:, :X], sum_spread[:])
+
         taken = keep.tile([P, C], F32, name="taken")
-        nc.vector.tensor_tensor(taken[:], bag_sum[:].indirect(bag_list[:]), alpha[:], MULT)
         result = keep.tile([P, C], F32, name="result")
-        nc.vector.tensor_tensor(result[0:1, :], w_row[0:1, :], taken[0:1, :], SUBTRACT)
+        halves = [slice(h * BANK, (h + 1) * BANK) for h in range(2)]
+        for h in range(2):
+            nc.vector.tensor_tensor(
+                taken[:, halves[h]], bag_sum[:].indirect(bag_list[:, h * 32 : (h + 1) * 32]), alpha[:, halves[h]], MULT
+            )
+        for h in range(2):
+            nc.vector.tensor_tensor(result[0:1, halves[h]], w_row[0:1, halves[h]], taken[0:1, halves[h]], SUBTRACT)
         nc.sync.dma_start(out_1, result[0:1, :])

@@ -47,21 +47,23 @@ def tile_attend_gmil_kernel(tc, eT, W, dz, al, offs, bagoffs, slotoffs, out_0, o
         dz_a = keep.tile([P, PACK, HALF], F32, name="dz_a")
         dz_b = keep.tile([P, PACK, HALF], F32, name="dz_b")
         w_first = keep.tile([P, PACK, P], F32, name="w_first")
-        w_rest = keep.tile([P, PACK, D - P], F32, name="w_rest", tag="second_places")
+        w_rest = keep.tile([P, PACK, D - P], F32, name="w_rest")
         alpha = keep.tile([P, C], F32, name="alpha")
         idx_list = keep.tile([P, C // 16], U16, name="idx_list")
         bag_list = keep.tile([P, C // 16], U16, name="bag_list")
         slot_list = keep.tile([P, C // 16], U16, name="slot_list")
-        emb = [keep.tile([P, T], F32, name=f"emb{b}") for b in range(BLOCKS)]
+        emb = [keep.tile([P, T], F32, name=f"emb{b}", tag=f"emb{b}") for b in range(BLOCKS)]
 
         nc.sync.dma_start(dz_a[:], dz_rows[:, :, :HALF])
         nc.sync.dma_start(w_first[:], w_rows[:, :, :P])
         nc.sync.dma_start(dz_b[:], dz_rows[:, :, HALF:])
-        nc.sync.dma_start(bag_list[:], bagoffs)
-        nc.sync.dma_start(alpha[:], al)
         nc.sync.dma_start(idx_list[:], offs)
+        nc.sync.dma_start(emb[0][:], eT[:P, :])
+        nc.sync.dma_start(bag_list[:], bagoffs)
         nc.sync.dma_start(w_rest[:], w_rows[:, :, P:])
-        for b in range(BLOCKS):
+        nc.sync.dma_start(emb[1][:], eT[P : 2 * P, :])
+        nc.sync.dma_start(alpha[:], al)
+        for b in range(2, BLOCKS):
             nc.sync.dma_start(emb[b][:], eT[b * P : (b + 1) * P, :])
         nc.sync.dma_start(slot_list[:], slotoffs)
 
@@ -77,7 +79,7 @@ def tile_attend_gmil_kernel(tc, eT, W, dz, al, offs, bagoffs, slotoffs, out_0, o
         dz_a16 = keep.tile([P, HALF, PACK], BF16, name="dz_a16", align_bytes=64)
         dz_b16 = keep.tile([P, HALF, PACK], BF16, name="dz_b16", align_bytes=64)
         w_first16 = keep.tile([P, P, PACK], BF16, name="w_first16", align_bytes=64)
-        w_rest16 = keep.tile([P, D - P, PACK], BF16, name="w_rest16", align_bytes=64)
+        w_rest16 = keep.tile([P, D - P, PACK], BF16, name="w_rest16", tag="prod0", align_bytes=64)
         dz_codes = keep.tile([P, X], U32, name="dz_codes", align_bytes=64)
         dz_scales = keep.tile([P, X], U8, name="dz_scales", align_bytes=64)
         w_codes = keep.tile([P, D], U32, name="w_codes", align_bytes=64)
@@ -121,14 +123,31 @@ def tile_attend_gmil_kernel(tc, eT, W, dz, al, offs, bagoffs, slotoffs, out_0, o
         product(0, nc.scalar.copy)
 
         ub = [keep.tile([P, C], F32, name=f"ub{b}") for b in range(BLOCKS)]
-        prod = [keep.tile([P, C], F32, name=f"prod{b}") for b in range(BLOCKS)]
+        et = [keep.tile([P, C], F32, name=f"et{b}", tag=f"et{b}") for b in range(BLOCKS)]
+        de = {}
 
         def look_up_u(b):
             window = u[:, u_first(b) : u_first(b) + U_WINDOW]
             nc.vector.tensor_copy(ub[b][:], window.indirect(bag_list[:]))
 
+        def look_up_emb(b):
+            nc.vector.tensor_copy(et[b][:], emb[b][:].indirect(idx_list[:]))
+
+        def weigh(b, tag):
+            de[b] = keep.tile([P, C], F32, name=f"de{b}", tag=tag)
+            nc.gpsimd.tensor_tensor(de[b][:], ub[b][:], alpha[:], MULT)
+
+        def multiply(b):
+            prod = keep.tile([P, C], F32, name=f"prod{b}", tag=f"prod{b}", align_bytes=64)
+            nc.gpsimd.tensor_tensor(prod[:], ub[b][:], et[b][:], MULT)
+            for k in range(CHUNKS):
+                nc.tensor.matmul(
+                    turned[k][:, :P], prod[:, k * P : (k + 1) * P], identity[:],
+                    start=(b == 0), stop=(b == BLOCKS - 1), is_transpose=True,
+                )
+
         def put(b, window):
-            nc.vector.tensor_tensor(window[:].indirect(idx_list[:]), ub[b][:], alpha[:], MULT)
+            nc.vector.tensor_copy(window[:].indirect(idx_list[:]), de[b][:])
             nc.sync.dma_start(out_0[b * P : (b + 1) * P, :], window[:])
 
         def first_columns(dst, src, count):
@@ -137,8 +156,8 @@ def tile_attend_gmil_kernel(tc, eT, W, dz, al, offs, bagoffs, slotoffs, out_0, o
         def spread(dst, column):
             nc.tensor.transpose(dst, column.to_broadcast([P, P]), identity[:])
 
+        look_up_emb(0)
         look_up_u(0)
-        put(0, first_places)
         interleave(nc.scalar.copy, w_rest16, w_rest, 0, D - P)
         quantize(w_codes, w_scales, E4M3X4, P, w_rest16[:, :P, :])
         quantize(w_codes, w_scales, E4M3X4, 2 * P, w_rest16[:, P:, :])
@@ -154,24 +173,24 @@ def tile_attend_gmil_kernel(tc, eT, W, dz, al, offs, bagoffs, slotoffs, out_0, o
             first_columns(alpha_cols[:, 4 * h : 4 * h + 4], alpha_turned, 4)
 
         turned = [bank(k, f"turned{k}") for k in range(CHUNKS)]
-
-        def look_up_emb(b):
-            nc.vector.tensor_tensor(prod[b][:], emb[b][:].indirect(idx_list[:]), ub[b][:], MULT)
-            for k in range(CHUNKS):
-                nc.tensor.matmul(
-                    turned[k][:, :P], prod[b][:, k * P : (k + 1) * P], identity[:],
-                    start=(b == 0), stop=(b == BLOCKS - 1), is_transpose=True,
-                )
-
-        look_up_emb(0)
-        look_up_u(1)
-        second_places = keep.tile([P, T], F32, name="second_places", tag="second_places")
-        nc.gpsimd.memset(second_places[:], 0.0)
-        put(1, second_places)
-        look_up_u(2)
-        look_up_u(3)
+        multiply(0)
         for b in range(1, BLOCKS):
-            look_up_emb(b)
+            look_up_u(b)
+        look_up_emb(1)
+        weigh(0, "emb1")
+        second_places = keep.tile([P, T], F32, name="second_places", tag="et0")
+        nc.gpsimd.memset(second_places[:], 0.0)
+        multiply(1)
+        look_up_emb(2)
+        put(0, first_places)
+        weigh(1, "emb2")
+        multiply(2)
+        look_up_emb(3)
+        put(1, second_places)
+        multiply(3)
+        weigh(2, "emb3")
+        weigh(3, "de3")
+        put(2, first_places)
 
         w_cols = keep.tile([P, CHUNKS], F32, name="w_cols", tag="last_places")
         spent = keep.tile([P, P], F32, name="spent")
@@ -186,8 +205,6 @@ def tile_attend_gmil_kernel(tc, eT, W, dz, al, offs, bagoffs, slotoffs, out_0, o
                 k = 4 * h + q
                 spread(w_spread[:, q * P : (q + 1) * P], w_cols[:, k : k + 1])
             nc.scalar.copy(w_row[:, h * BANK : (h + 1) * BANK], w_spread[:])
-
-        put(2, first_places)
 
         by_bag = keep.tile([P, C], F32, name="by_bag")
         for h in range(2):

@@ -22,8 +22,8 @@ CHUNKS = C // P
 BANK = 512
 U_WINDOW = 1376
 SUM_WINDOW = X + 16
-HALF = X // 2
-DZ_SPLIT = 160
+DZ_SPLIT = 336
+LAST_SPLIT = 256
 
 FLOPS = 2 * M * D * X
 
@@ -44,8 +44,7 @@ def tile_attend_gmil_kernel(tc, eT, W, dz, al, offs, bagoffs, slotoffs, out_0, o
         dz_rows = dz.rearrange("(p j) x -> p j x", j=PACK)
         w_rows = W.rearrange("(p j) d -> p j d", j=PACK)
 
-        dz_a = keep.tile([P, PACK, HALF], F32, name="dz_a")
-        dz_b = keep.tile([P, PACK, HALF], F32, name="dz_b")
+        dz_raw = keep.tile([P, PACK, X], F32, name="dz_raw")
         w_first = keep.tile([P, PACK, P], F32, name="w_first")
         w_rest = keep.tile([P, PACK, D - P], F32, name="w_rest")
         alpha = keep.tile([P, C], F32, name="alpha")
@@ -54,9 +53,8 @@ def tile_attend_gmil_kernel(tc, eT, W, dz, al, offs, bagoffs, slotoffs, out_0, o
         slot_list = keep.tile([P, C // 16], U16, name="slot_list")
         emb = [keep.tile([P, T], F32, name=f"emb{b}", tag=f"emb{b}") for b in range(BLOCKS)]
 
-        nc.sync.dma_start(dz_a[:], dz_rows[:, :, :HALF])
+        nc.sync.dma_start(dz_raw[:], dz_rows)
         nc.sync.dma_start(w_first[:], w_rows[:, :, :P])
-        nc.sync.dma_start(dz_b[:], dz_rows[:, :, HALF:])
         nc.sync.dma_start(idx_list[:], offs)
         nc.sync.dma_start(emb[0][:], eT[:P, :])
         nc.sync.dma_start(bag_list[:], bagoffs)
@@ -76,8 +74,7 @@ def tile_attend_gmil_kernel(tc, eT, W, dz, al, offs, bagoffs, slotoffs, out_0, o
         identity = keep.tile([P, P], F32, name="identity")
         make_identity(nc, identity[:])
 
-        dz_a16 = keep.tile([P, HALF, PACK], BF16, name="dz_a16", align_bytes=64)
-        dz_b16 = keep.tile([P, HALF, PACK], BF16, name="dz_b16", align_bytes=64)
+        dz16 = keep.tile([P, X, PACK], BF16, name="dz16", align_bytes=64)
         w_first16 = keep.tile([P, P, PACK], BF16, name="w_first16", align_bytes=64)
         w_rest16 = keep.tile([P, D - P, PACK], BF16, name="w_rest16", tag="prod0", align_bytes=64)
         dz_codes = keep.tile([P, X], U32, name="dz_codes", align_bytes=64)
@@ -113,13 +110,11 @@ def tile_attend_gmil_kernel(tc, eT, W, dz, al, offs, bagoffs, slotoffs, out_0, o
             )
             copy_out(u[:, u_first(b) : u_first(b) + X], acc[:])
 
-        interleave(nc.scalar.copy, dz_a16, dz_a, 0, HALF)
-        interleave(nc.vector.tensor_copy, w_first16, w_first, 0, P)
+        interleave(nc.vector.tensor_copy, dz16, dz_raw, 0, DZ_SPLIT)
+        interleave(nc.scalar.copy, dz16, dz_raw, DZ_SPLIT, X)
+        interleave(nc.scalar.copy, w_first16, w_first, 0, P)
+        quantize(dz_codes, dz_scales, E5M2X4, 0, dz16[:])
         quantize(w_codes, w_scales, E4M3X4, 0, w_first16[:])
-        quantize(dz_codes, dz_scales, E5M2X4, 0, dz_a16[:])
-        interleave(nc.vector.tensor_copy, dz_b16, dz_b, 0, DZ_SPLIT)
-        interleave(nc.scalar.copy, dz_b16, dz_b, DZ_SPLIT, HALF)
-        quantize(dz_codes, dz_scales, E5M2X4, HALF, dz_b16[:])
         product(0, nc.scalar.copy)
 
         ub = [keep.tile([P, C], F32, name=f"ub{b}") for b in range(BLOCKS)]
@@ -199,12 +194,12 @@ def tile_attend_gmil_kernel(tc, eT, W, dz, al, offs, bagoffs, slotoffs, out_0, o
             nc.scalar.activation(
                 spent[:], turned[k][:, :P], COPY, scale=alpha_cols[:, k : k + 1], accum_out=w_cols[:, k : k + 1]
             )
+        w_spread = [bank(h, f"w_spread{h}") for h in range(2)]
         for h in range(2):
-            w_spread = bank(h, f"w_spread{h}")
             for q in range(4):
                 k = 4 * h + q
-                spread(w_spread[:, q * P : (q + 1) * P], w_cols[:, k : k + 1])
-            nc.scalar.copy(w_row[:, h * BANK : (h + 1) * BANK], w_spread[:])
+                spread(w_spread[h][:, q * P : (q + 1) * P], w_cols[:, k : k + 1])
+            nc.scalar.copy(w_row[:, h * BANK : (h + 1) * BANK], w_spread[h][:])
 
         by_bag = keep.tile([P, C], F32, name="by_bag")
         for h in range(2):
@@ -238,6 +233,9 @@ def tile_attend_gmil_kernel(tc, eT, W, dz, al, offs, bagoffs, slotoffs, out_0, o
             nc.vector.tensor_tensor(
                 taken[:, halves[h]], bag_sum[:].indirect(bag_list[:, h * 32 : (h + 1) * 32]), alpha[:, halves[h]], MULT
             )
-        for h in range(2):
-            nc.vector.tensor_tensor(result[0:1, halves[h]], w_row[0:1, halves[h]], taken[0:1, halves[h]], SUBTRACT)
+        nc.gpsimd.tensor_tensor(result[0:1, :LAST_SPLIT], w_row[0:1, :LAST_SPLIT], taken[0:1, :LAST_SPLIT], SUBTRACT)
+        nc.vector.tensor_tensor(
+            result[0:1, LAST_SPLIT:BANK], w_spread[0][0:1, LAST_SPLIT:], taken[0:1, LAST_SPLIT:BANK], SUBTRACT
+        )
+        nc.vector.tensor_tensor(result[0:1, BANK:], w_spread[1][0:1, :], taken[0:1, BANK:], SUBTRACT)
         nc.sync.dma_start(out_1, result[0:1, :])

@@ -23,7 +23,8 @@ BANK = 512
 U_WINDOW = 1376
 SUM_WINDOW = X + 16
 DZ_SPLIT = 336
-LAST_SPLIT = 256
+EARLY = 320
+MIDDLE = 672
 
 FLOPS = 2 * M * D * X
 
@@ -53,16 +54,19 @@ def tile_attend_gmil_kernel(tc, eT, W, dz, al, offs, bagoffs, slotoffs, out_0, o
         slot_list = keep.tile([P, C // 16], U16, name="slot_list")
         emb = [keep.tile([P, T], F32, name=f"emb{b}", tag=f"emb{b}") for b in range(BLOCKS)]
 
+        def load_emb(b):
+            nc.sync.dma_start(emb[b][:], eT[b * P : (b + 1) * P, :])
+
+        load_emb(0)
+        nc.sync.dma_start(idx_list[:], offs)
+        load_emb(1)
         nc.sync.dma_start(dz_raw[:], dz_rows)
         nc.sync.dma_start(w_first[:], w_rows[:, :, :P])
-        nc.sync.dma_start(idx_list[:], offs)
-        nc.sync.dma_start(emb[0][:], eT[:P, :])
+        load_emb(2)
         nc.sync.dma_start(bag_list[:], bagoffs)
         nc.sync.dma_start(w_rest[:], w_rows[:, :, P:])
-        nc.sync.dma_start(emb[1][:], eT[P : 2 * P, :])
+        load_emb(3)
         nc.sync.dma_start(alpha[:], al)
-        for b in range(2, BLOCKS):
-            nc.sync.dma_start(emb[b][:], eT[b * P : (b + 1) * P, :])
         nc.sync.dma_start(slot_list[:], slotoffs)
 
         first_places = keep.tile([P, T], F32, name="first_places")
@@ -70,9 +74,11 @@ def tile_attend_gmil_kernel(tc, eT, W, dz, al, offs, bagoffs, slotoffs, out_0, o
         bag_sum = keep.tile([P, SUM_WINDOW], F32, name="bag_sum")
         nc.vector.memset(u[:, BLOCKS * X :], 0.0)
         nc.vector.memset(first_places[:], 0.0)
+        second_places = keep.tile([P, T], F32, name="second_places")
         nc.gpsimd.memset(bag_sum[:, X:], 0.0)
         identity = keep.tile([P, P], F32, name="identity")
         make_identity(nc, identity[:])
+        nc.gpsimd.memset(second_places[:], 0.0)
 
         dz16 = keep.tile([P, X, PACK], BF16, name="dz16", align_bytes=64)
         w_first16 = keep.tile([P, P, PACK], BF16, name="w_first16", align_bytes=64)
@@ -172,22 +178,18 @@ def tile_attend_gmil_kernel(tc, eT, W, dz, al, offs, bagoffs, slotoffs, out_0, o
         for b in range(1, BLOCKS):
             look_up_u(b)
         look_up_emb(1)
-        weigh(0, "emb1")
-        second_places = keep.tile([P, T], F32, name="second_places", tag="et0")
-        nc.gpsimd.memset(second_places[:], 0.0)
+        weigh(0, "de0")
         multiply(1)
         look_up_emb(2)
         put(0, first_places)
-        weigh(1, "emb2")
+        weigh(1, "de1")
         multiply(2)
         look_up_emb(3)
         put(1, second_places)
         multiply(3)
-        weigh(2, "emb3")
-        weigh(3, "de3")
-        put(2, first_places)
+        weigh(2, "de2")
 
-        w_cols = keep.tile([P, CHUNKS], F32, name="w_cols", tag="last_places")
+        w_cols = keep.tile([P, CHUNKS], F32, name="w_cols", tag="third_places")
         spent = keep.tile([P, P], F32, name="spent")
         w_row = keep.tile([P, C], F32, name="w_row")
         for k in range(CHUNKS):
@@ -208,9 +210,9 @@ def tile_attend_gmil_kernel(tc, eT, W, dz, al, offs, bagoffs, slotoffs, out_0, o
                 w_row[:].indirect(slot_list[:, h * 32 : (h + 1) * 32]),
             )
 
-        last_places = keep.tile([P, T], F32, name="last_places", tag="last_places")
-        nc.gpsimd.memset(last_places[:], 0.0)
-        put(3, last_places)
+        third_places = keep.tile([P, T], F32, name="third_places", tag="third_places")
+        nc.gpsimd.memset(third_places[:], 0.0)
+        put(2, third_places)
 
         pair_sums = bank(2, "pair_sums")
         for q in range(4):
@@ -219,23 +221,30 @@ def tile_attend_gmil_kernel(tc, eT, W, dz, al, offs, bagoffs, slotoffs, out_0, o
                     pair_sums[:, q * P : (q + 1) * P], by_bag[:, 2 * q * P + j : 2 * (q + 1) * P : 2], identity[:],
                     start=(j == 0), stop=(j == 1), is_transpose=True,
                 )
-        sum_cols = keep.tile([P, 4], F32, name="sum_cols")
+        sum_cols = keep.tile([P, 4], F32, name="sum_cols", tag="de3")
         first_columns(sum_cols[:], pair_sums, 4)
         sum_spread = bank(3, "sum_spread")
         for q in range(4):
             spread(sum_spread[:, q * P : (q + 1) * P], sum_cols[:, q : q + 1])
         nc.scalar.copy(bag_sum[:, :X], sum_spread[:])
 
-        taken = keep.tile([P, C], F32, name="taken")
         result = keep.tile([P, C], F32, name="result")
-        halves = [slice(h * BANK, (h + 1) * BANK) for h in range(2)]
-        for h in range(2):
+
+        def look_up_sum(dst, lo, hi):
+            nc.vector.tensor_tensor(dst, bag_sum[:].indirect(bag_list[:, lo // 16 : hi // 16]), alpha[:, lo:hi], MULT)
+
+        early = keep.tile([P, EARLY], F32, name="early", tag="taken")
+        look_up_sum(early[:], 0, EARLY)
+        weigh(3, "de3")
+        nc.gpsimd.tensor_tensor(result[0:1, :EARLY], w_row[0:1, :EARLY], early[0:1, :], SUBTRACT)
+        put(3, first_places)
+
+        late = keep.tile([P, C - EARLY], F32, name="late", tag="taken")
+        look_up_sum(late[:, : MIDDLE - EARLY], EARLY, MIDDLE)
+        look_up_sum(late[:, MIDDLE - EARLY :], MIDDLE, C)
+        nc.gpsimd.tensor_tensor(result[0:1, EARLY:BANK], w_row[0:1, EARLY:BANK], late[0:1, : BANK - EARLY], SUBTRACT)
+        for lo, hi in ((BANK, MIDDLE), (MIDDLE, C)):
             nc.vector.tensor_tensor(
-                taken[:, halves[h]], bag_sum[:].indirect(bag_list[:, h * 32 : (h + 1) * 32]), alpha[:, halves[h]], MULT
+                result[0:1, lo:hi], w_spread[1][0:1, lo - BANK : hi - BANK], late[0:1, lo - EARLY : hi - EARLY], SUBTRACT
             )
-        nc.gpsimd.tensor_tensor(result[0:1, :LAST_SPLIT], w_row[0:1, :LAST_SPLIT], taken[0:1, :LAST_SPLIT], SUBTRACT)
-        nc.vector.tensor_tensor(
-            result[0:1, LAST_SPLIT:BANK], w_spread[0][0:1, LAST_SPLIT:], taken[0:1, LAST_SPLIT:BANK], SUBTRACT
-        )
-        nc.vector.tensor_tensor(result[0:1, BANK:], w_spread[1][0:1, :], taken[0:1, BANK:], SUBTRACT)
-        nc.sync.dma_start(out_1, result[0:1, :])
+        nc.scalar.dma_start(out_1, result[0:1, :])

@@ -24,7 +24,7 @@ U_WINDOW = 1376
 SUM_WINDOW = X + 16
 DZ_SPLIT = 336
 EARLY = 320
-MIDDLE = 672
+MIDDLE = 768
 
 FLOPS = 2 * M * D * X
 
@@ -58,10 +58,10 @@ def tile_attend_gmil_kernel(tc, eT, W, dz, al, offs, bagoffs, slotoffs, out_0, o
             nc.sync.dma_start(emb[b][:], eT[b * P : (b + 1) * P, :])
 
         load_emb(0)
+        nc.scalar.dma_start(w_first[:], w_rows[:, :, :P])
         nc.sync.dma_start(idx_list[:], offs)
         load_emb(1)
         nc.sync.dma_start(dz_raw[:], dz_rows)
-        nc.sync.dma_start(w_first[:], w_rows[:, :, :P])
         load_emb(2)
         nc.sync.dma_start(bag_list[:], bagoffs)
         nc.sync.dma_start(w_rest[:], w_rows[:, :, P:])
@@ -79,6 +79,8 @@ def tile_attend_gmil_kernel(tc, eT, W, dz, al, offs, bagoffs, slotoffs, out_0, o
         identity = keep.tile([P, P], F32, name="identity")
         make_identity(nc, identity[:])
         nc.gpsimd.memset(second_places[:], 0.0)
+        w_row = keep.tile([P, U_WINDOW], F32, name="w_row")
+        nc.gpsimd.memset(w_row[:, C:], 0.0)
 
         dz16 = keep.tile([P, X, PACK], BF16, name="dz16", align_bytes=64)
         w_first16 = keep.tile([P, P, PACK], BF16, name="w_first16", align_bytes=64)
@@ -191,7 +193,6 @@ def tile_attend_gmil_kernel(tc, eT, W, dz, al, offs, bagoffs, slotoffs, out_0, o
 
         w_cols = keep.tile([P, CHUNKS], F32, name="w_cols", tag="third_places")
         spent = keep.tile([P, P], F32, name="spent")
-        w_row = keep.tile([P, C], F32, name="w_row")
         for k in range(CHUNKS):
             nc.scalar.activation(
                 spent[:], turned[k][:, :P], COPY, scale=alpha_cols[:, k : k + 1], accum_out=w_cols[:, k : k + 1]
@@ -204,11 +205,7 @@ def tile_attend_gmil_kernel(tc, eT, W, dz, al, offs, bagoffs, slotoffs, out_0, o
             nc.scalar.copy(w_row[:, h * BANK : (h + 1) * BANK], w_spread[h][:])
 
         by_bag = keep.tile([P, C], F32, name="by_bag")
-        for h in range(2):
-            nc.vector.tensor_copy(
-                by_bag[:, h * BANK : (h + 1) * BANK],
-                w_row[:].indirect(slot_list[:, h * 32 : (h + 1) * 32]),
-            )
+        nc.vector.tensor_copy(by_bag[:], w_row[:].indirect(slot_list[:]))
 
         third_places = keep.tile([P, T], F32, name="third_places", tag="third_places")
         nc.gpsimd.memset(third_places[:], 0.0)

@@ -24,7 +24,7 @@ U_WINDOW = 1376
 SUM_WINDOW = X + 16
 DZ_SPLIT = 336
 EARLY = 320
-MIDDLE = 768
+MIDDLE = 832
 
 FLOPS = 2 * M * D * X
 
@@ -58,10 +58,10 @@ def tile_attend_gmil_kernel(tc, eT, W, dz, al, offs, bagoffs, slotoffs, out_0, o
             nc.sync.dma_start(emb[b][:], eT[b * P : (b + 1) * P, :])
 
         load_emb(0)
-        nc.scalar.dma_start(w_first[:], w_rows[:, :, :P])
         nc.sync.dma_start(idx_list[:], offs)
         load_emb(1)
         nc.sync.dma_start(dz_raw[:], dz_rows)
+        nc.sync.dma_start(w_first[:], w_rows[:, :, :P])
         load_emb(2)
         nc.sync.dma_start(bag_list[:], bagoffs)
         nc.sync.dma_start(w_rest[:], w_rows[:, :, P:])

@@ -23,8 +23,8 @@ BANK = 512
 U_WINDOW = 1376
 SUM_WINDOW = X + 16
 DZ_SPLIT = 336
-EARLY = 320
-MIDDLE = 832
+EARLY = 256
+MIDDLE = 768
 
 FLOPS = 2 * M * D * X
 

@@ -22,7 +22,7 @@ CHUNKS = C // P
 BANK = 512
 U_WINDOW = 1376
 SUM_WINDOW = X + 16
-DZ_SPLIT = 336
+DZ_SPLIT = 288
 EARLY = 256
 MIDDLE = 768
 
@@ -72,12 +72,12 @@ def tile_attend_gmil_kernel(tc, eT, W, dz, al, offs, bagoffs, slotoffs, out_0, o
         first_places = keep.tile([P, T], F32, name="first_places")
         u = keep.tile([P, (BLOCKS - 1) * X + U_WINDOW], F32, name="u")
         bag_sum = keep.tile([P, SUM_WINDOW], F32, name="bag_sum")
-        nc.vector.memset(u[:, BLOCKS * X :], 0.0)
-        nc.vector.memset(first_places[:], 0.0)
         second_places = keep.tile([P, T], F32, name="second_places")
         nc.gpsimd.memset(bag_sum[:, X:], 0.0)
         identity = keep.tile([P, P], F32, name="identity")
         make_identity(nc, identity[:])
+        nc.gpsimd.memset(u[:, BLOCKS * X :], 0.0)
+        nc.gpsimd.memset(first_places[:], 0.0)
         nc.gpsimd.memset(second_places[:], 0.0)
         w_row = keep.tile([P, U_WINDOW], F32, name="w_row")
         nc.gpsimd.memset(w_row[:, C:], 0.0)

@@ -26,6 +26,21 @@ DZ_SPLIT = 288
 EARLY = 256
 MIDDLE = 768
 
+KIB = 1024
+ZONES = (
+    (("emb0", 8), ("emb3", 8), ("dz_raw", 8), ("w_first", 2), ("w_rest", 6), ("first_places", 8), ("w_row", 6)),
+    (("emb1", 8), ("emb2", 8), ("second_places", 8), ("bag_sum", 3), ("dz16", 4), ("w_first16", 1), ("dz_codes", 2),
+     ("w_codes", 2), ("dz_scales", 1), ("w_scales", 1), ("identity", 1), ("alpha_cols", 1), ("spent", 1), ("result", 4),
+     ("taken", 3), ("de0", 4), ("de1", 4), ("de2", 4), ("de3", 4)),
+    tuple((f"{kind}{b}", 4) for kind in ("ub", "et", "prod") for b in range(BLOCKS)) + (("alpha", 4), ("by_bag", 4)),
+    (("u", 12), ("third_places", 8)),
+)
+PLACES = {
+    name: (64 * z + sum(size for other, size in zone[:i])) * KIB
+    for z, zone in enumerate(ZONES)
+    for i, (name, size) in enumerate(zone)
+}
+
 FLOPS = 2 * M * D * X
 
 
@@ -39,20 +54,24 @@ def interleave(engine_copy, grouped, raw, lo, hi):
 def tile_attend_gmil_kernel(tc, eT, W, dz, al, offs, bagoffs, slotoffs, out_0, out_1):
     nc = tc.nc
     with ExitStack() as ctx:
+        lists = ctx.enter_context(tc.tile_pool(name="lists", bufs=1))
         keep = ctx.enter_context(tc.tile_pool(name="keep", bufs=1))
         psum = ctx.enter_context(tc.psum_pool(name="psum", bufs=1))
+
+        def place(shape, dtype, name, tag=None):
+            return keep.tile(shape, dtype, name=name, offset=PLACES[tag or name], align_bytes=64)
 
         dz_rows = dz.rearrange("(p j) x -> p j x", j=PACK)
         w_rows = W.rearrange("(p j) d -> p j d", j=PACK)
 
-        dz_raw = keep.tile([P, PACK, X], F32, name="dz_raw")
-        w_first = keep.tile([P, PACK, P], F32, name="w_first")
-        w_rest = keep.tile([P, PACK, D - P], F32, name="w_rest")
-        alpha = keep.tile([P, C], F32, name="alpha")
-        idx_list = keep.tile([P, C // 16], U16, name="idx_list")
-        bag_list = keep.tile([P, C // 16], U16, name="bag_list")
-        slot_list = keep.tile([P, C // 16], U16, name="slot_list")
-        emb = [keep.tile([P, T], F32, name=f"emb{b}", tag=f"emb{b}") for b in range(BLOCKS)]
+        dz_raw = place([P, PACK, X], F32, "dz_raw")
+        w_first = place([P, PACK, P], F32, "w_first")
+        w_rest = place([P, PACK, D - P], F32, "w_rest")
+        alpha = place([P, C], F32, "alpha")
+        idx_list = lists.tile([P, C // 16], U16, name="idx_list")
+        bag_list = lists.tile([P, C // 16], U16, name="bag_list")
+        slot_list = lists.tile([P, C // 16], U16, name="slot_list")
+        emb = [place([P, T], F32, f"emb{b}", f"emb{b}") for b in range(BLOCKS)]
 
         def load_emb(b):
             nc.sync.dma_start(emb[b][:], eT[b * P : (b + 1) * P, :])
@@ -69,26 +88,26 @@ def tile_attend_gmil_kernel(tc, eT, W, dz, al, offs, bagoffs, slotoffs, out_0, o
         nc.sync.dma_start(alpha[:], al)
         nc.sync.dma_start(slot_list[:], slotoffs)
 
-        first_places = keep.tile([P, T], F32, name="first_places")
-        u = keep.tile([P, (BLOCKS - 1) * X + U_WINDOW], F32, name="u")
-        bag_sum = keep.tile([P, SUM_WINDOW], F32, name="bag_sum")
-        second_places = keep.tile([P, T], F32, name="second_places")
+        first_places = place([P, T], F32, "first_places")
+        u = place([P, (BLOCKS - 1) * X + U_WINDOW], F32, "u")
+        bag_sum = place([P, SUM_WINDOW], F32, "bag_sum")
+        second_places = place([P, T], F32, "second_places")
         nc.gpsimd.memset(bag_sum[:, X:], 0.0)
-        identity = keep.tile([P, P], F32, name="identity")
+        identity = place([P, P], F32, "identity")
         make_identity(nc, identity[:])
         nc.gpsimd.memset(u[:, BLOCKS * X :], 0.0)
         nc.gpsimd.memset(first_places[:], 0.0)
         nc.gpsimd.memset(second_places[:], 0.0)
-        w_row = keep.tile([P, U_WINDOW], F32, name="w_row")
+        w_row = place([P, U_WINDOW], F32, "w_row")
         nc.gpsimd.memset(w_row[:, C:], 0.0)
 
-        dz16 = keep.tile([P, X, PACK], BF16, name="dz16", align_bytes=64)
-        w_first16 = keep.tile([P, P, PACK], BF16, name="w_first16", align_bytes=64)
-        w_rest16 = keep.tile([P, D - P, PACK], BF16, name="w_rest16", tag="prod0", align_bytes=64)
-        dz_codes = keep.tile([P, X], U32, name="dz_codes", align_bytes=64)
-        dz_scales = keep.tile([P, X], U8, name="dz_scales", align_bytes=64)
-        w_codes = keep.tile([P, D], U32, name="w_codes", align_bytes=64)
-        w_scales = keep.tile([P, D], U8, name="w_scales", align_bytes=64)
+        dz16 = place([P, X, PACK], BF16, "dz16")
+        w_first16 = place([P, P, PACK], BF16, "w_first16")
+        w_rest16 = place([P, D - P, PACK], BF16, "w_rest16", "prod0")
+        dz_codes = place([P, X], U32, "dz_codes")
+        dz_scales = place([P, X], U8, "dz_scales")
+        w_codes = place([P, D], U32, "w_codes")
+        w_scales = place([P, D], U8, "w_scales")
 
         def quantize(codes, scales, fmt, first, grouped):
             width = grouped.shape[1]
@@ -125,8 +144,8 @@ def tile_attend_gmil_kernel(tc, eT, W, dz, al, offs, bagoffs, slotoffs, out_0, o
         quantize(w_codes, w_scales, E4M3X4, 0, w_first16[:])
         product(0, nc.scalar.copy)
 
-        ub = [keep.tile([P, C], F32, name=f"ub{b}") for b in range(BLOCKS)]
-        et = [keep.tile([P, C], F32, name=f"et{b}", tag=f"et{b}") for b in range(BLOCKS)]
+        ub = [place([P, C], F32, f"ub{b}") for b in range(BLOCKS)]
+        et = [place([P, C], F32, f"et{b}", f"et{b}") for b in range(BLOCKS)]
         de = {}
 
         def look_up_u(b):
@@ -137,11 +156,11 @@ def tile_attend_gmil_kernel(tc, eT, W, dz, al, offs, bagoffs, slotoffs, out_0, o
             nc.vector.tensor_copy(et[b][:], emb[b][:].indirect(idx_list[:]))
 
         def weigh(b, tag):
-            de[b] = keep.tile([P, C], F32, name=f"de{b}", tag=tag)
+            de[b] = place([P, C], F32, f"de{b}", tag)
             nc.gpsimd.tensor_tensor(de[b][:], ub[b][:], alpha[:], MULT)
 
         def multiply(b):
-            prod = keep.tile([P, C], F32, name=f"prod{b}", tag=f"prod{b}", align_bytes=64)
+            prod = place([P, C], F32, f"prod{b}", f"prod{b}")
             nc.gpsimd.tensor_tensor(prod[:], ub[b][:], et[b][:], MULT)
             for k in range(CHUNKS):
                 nc.tensor.matmul(
@@ -167,7 +186,7 @@ def tile_attend_gmil_kernel(tc, eT, W, dz, al, offs, bagoffs, slotoffs, out_0, o
         for b in range(1, BLOCKS):
             product(b, lambda dst, src: nc.scalar.activation(dst, src, COPY))
 
-        alpha_cols = keep.tile([P, CHUNKS], F32, name="alpha_cols")
+        alpha_cols = place([P, CHUNKS], F32, "alpha_cols")
         for h in range(2):
             alpha_turned = bank(BLOCKS + h, f"alpha_turned{h}")
             for q in range(4):
@@ -191,8 +210,8 @@ def tile_attend_gmil_kernel(tc, eT, W, dz, al, offs, bagoffs, slotoffs, out_0, o
         multiply(3)
         weigh(2, "de2")
 
-        w_cols = keep.tile([P, CHUNKS], F32, name="w_cols", tag="third_places")
-        spent = keep.tile([P, P], F32, name="spent")
+        w_cols = place([P, CHUNKS], F32, "w_cols", "third_places")
+        spent = place([P, P], F32, "spent")
         for k in range(CHUNKS):
             nc.scalar.activation(
                 spent[:], turned[k][:, :P], COPY, scale=alpha_cols[:, k : k + 1], accum_out=w_cols[:, k : k + 1]
@@ -204,10 +223,10 @@ def tile_attend_gmil_kernel(tc, eT, W, dz, al, offs, bagoffs, slotoffs, out_0, o
                 spread(w_spread[h][:, q * P : (q + 1) * P], w_cols[:, k : k + 1])
             nc.scalar.copy(w_row[:, h * BANK : (h + 1) * BANK], w_spread[h][:])
 
-        by_bag = keep.tile([P, C], F32, name="by_bag")
+        by_bag = place([P, C], F32, "by_bag")
         nc.vector.tensor_copy(by_bag[:], w_row[:].indirect(slot_list[:]))
 
-        third_places = keep.tile([P, T], F32, name="third_places", tag="third_places")
+        third_places = place([P, T], F32, "third_places", "third_places")
         nc.gpsimd.memset(third_places[:], 0.0)
         put(2, third_places)
 
@@ -218,25 +237,25 @@ def tile_attend_gmil_kernel(tc, eT, W, dz, al, offs, bagoffs, slotoffs, out_0, o
                     pair_sums[:, q * P : (q + 1) * P], by_bag[:, 2 * q * P + j : 2 * (q + 1) * P : 2], identity[:],
                     start=(j == 0), stop=(j == 1), is_transpose=True,
                 )
-        sum_cols = keep.tile([P, 4], F32, name="sum_cols", tag="de3")
+        sum_cols = place([P, 4], F32, "sum_cols", "de3")
         first_columns(sum_cols[:], pair_sums, 4)
         sum_spread = bank(3, "sum_spread")
         for q in range(4):
             spread(sum_spread[:, q * P : (q + 1) * P], sum_cols[:, q : q + 1])
         nc.scalar.copy(bag_sum[:, :X], sum_spread[:])
 
-        result = keep.tile([P, C], F32, name="result")
+        result = place([P, C], F32, "result")
 
         def look_up_sum(dst, lo, hi):
             nc.vector.tensor_tensor(dst, bag_sum[:].indirect(bag_list[:, lo // 16 : hi // 16]), alpha[:, lo:hi], MULT)
 
-        early = keep.tile([P, EARLY], F32, name="early", tag="taken")
+        early = place([P, EARLY], F32, "early", "taken")
         look_up_sum(early[:], 0, EARLY)
         weigh(3, "de3")
         nc.gpsimd.tensor_tensor(result[0:1, :EARLY], w_row[0:1, :EARLY], early[0:1, :], SUBTRACT)
         put(3, first_places)
 
-        late = keep.tile([P, C - EARLY], F32, name="late", tag="taken")
+        late = place([P, C - EARLY], F32, "late", "taken")
         look_up_sum(late[:, : MIDDLE - EARLY], EARLY, MIDDLE)
         look_up_sum(late[:, MIDDLE - EARLY :], MIDDLE, C)
         nc.gpsimd.tensor_tensor(result[0:1, EARLY:BANK], w_row[0:1, EARLY:BANK], late[0:1, : BANK - EARLY], SUBTRACT)

@@ -27,16 +27,17 @@ EARLY = 256
 MIDDLE = 768
 
 KIB = 1024
+POOL_START = 17
 ZONES = (
-    (("emb0", 8), ("emb3", 8), ("dz_raw", 8), ("w_first", 2), ("w_rest", 6), ("first_places", 8), ("w_row", 6)),
+    (("emb3", 8), ("dz_raw", 8), ("w_first", 2), ("w_rest", 6), ("first_places", 8), ("w_row", 6), ("de2", 4)),
     (("emb1", 8), ("emb2", 8), ("second_places", 8), ("bag_sum", 3), ("dz16", 4), ("w_first16", 1), ("dz_codes", 2),
-     ("w_codes", 2), ("dz_scales", 1), ("w_scales", 1), ("identity", 1), ("alpha_cols", 1), ("spent", 1), ("result", 4),
-     ("taken", 3), ("de0", 4), ("de1", 4), ("de2", 4), ("de3", 4)),
-    tuple((f"{kind}{b}", 4) for kind in ("ub", "et", "prod") for b in range(BLOCKS)) + (("alpha", 4), ("by_bag", 4)),
-    (("u", 12), ("third_places", 8)),
+     ("w_codes", 2), ("dz_scales", 1), ("w_scales", 1), ("de0", 4), ("de3", 4)),
+    tuple((f"{kind}{b}", 4) for kind in ("ub", "et", "prod") for b in range(BLOCKS))
+    + (("alpha", 4), ("by_bag", 4), ("de1", 4), ("identity", 1), ("alpha_cols", 1), ("spent", 1)),
+    (("u", 12), ("third_places", 8), ("emb0", 8), ("result", 4), ("taken", 3)),
 )
 PLACES = {
-    name: (64 * z + sum(size for other, size in zone[:i])) * KIB
+    name: (max(64 * z - POOL_START, 0) + sum(size for other, size in zone[:i])) * KIB
     for z, zone in enumerate(ZONES)
     for i, (name, size) in enumerate(zone)
 }
@@ -59,7 +60,7 @@ def tile_attend_gmil_kernel(tc, eT, W, dz, al, offs, bagoffs, slotoffs, out_0, o
         psum = ctx.enter_context(tc.psum_pool(name="psum", bufs=1))
 
         def place(shape, dtype, name, tag=None):
-            return keep.tile(shape, dtype, name=name, offset=PLACES[tag or name], align_bytes=64)
+            return keep.tile(shape, dtype, name=name, offset=PLACES[tag or name], align_bytes=KIB)
 
         dz_rows = dz.rearrange("(p j) x -> p j x", j=PACK)
         w_rows = W.rearrange("(p j) d -> p j d", j=PACK)

@@ -11,36 +11,23 @@ U8 = mybir.dt.uint8
 E4M3X4 = mybir.dt.float8_e4m3fn_x4
 E5M2X4 = mybir.dt.float8_e5m2_x4
 MULT = mybir.AluOpType.mult
+ADD = mybir.AluOpType.add
 SUBTRACT = mybir.AluOpType.subtract
 COPY = mybir.ActivationFunctionType.Copy
+AXIS_X = mybir.AxisListType.X
 
 P = 128
 PACK = 4
 M, D, C, T, X = 512, 512, 1024, 2048, 512
 BLOCKS = D // P
-CHUNKS = C // P
 BANK = 512
-U_WINDOW = 1376
-SUM_WINDOW = X + 16
-DZ_SPLIT = 288
-EARLY = 256
-MIDDLE = 768
-
-KIB = 1024
-POOL_START = 17
-ZONES = (
-    (("emb3", 8), ("dz_raw", 8), ("w_first", 2), ("w_rest", 6), ("first_places", 8), ("w_row", 6), ("de2", 4)),
-    (("emb1", 8), ("emb2", 8), ("second_places", 8), ("bag_sum", 3), ("dz16", 4), ("w_first16", 1), ("dz_codes", 2),
-     ("w_codes", 2), ("dz_scales", 1), ("w_scales", 1), ("de0", 4), ("de3", 4)),
-    tuple((f"{kind}{b}", 4) for kind in ("ub", "et", "prod") for b in range(BLOCKS))
-    + (("alpha", 4), ("by_bag", 4), ("de1", 4), ("identity", 1), ("alpha_cols", 1), ("spent", 1)),
-    (("u", 12), ("third_places", 8), ("emb0", 8), ("result", 4), ("taken", 3)),
-)
-PLACES = {
-    name: (max(64 * z - POOL_START, 0) + sum(size for other, size in zone[:i])) * KIB
-    for z, zone in enumerate(ZONES)
-    for i, (name, size) in enumerate(zone)
-}
+HALF = C // 2
+BAG_WINDOW = X + 16
+ALIGN = 256
+DZ_SPLIT = 336
+W_SPLIT = 160
+THIRDS = ((0, 384), (384, 768), (768, 1024))
+SHARED = ((0, 384), (384, 704), (704, 1024))
 
 FLOPS = 2 * M * D * X
 
@@ -57,211 +44,183 @@ def tile_attend_gmil_kernel(tc, eT, W, dz, al, offs, bagoffs, slotoffs, out_0, o
     with ExitStack() as ctx:
         lists = ctx.enter_context(tc.tile_pool(name="lists", bufs=1))
         keep = ctx.enter_context(tc.tile_pool(name="keep", bufs=1))
+        pairs = ctx.enter_context(tc.tile_pool(name="pairs", bufs=2))
         psum = ctx.enter_context(tc.psum_pool(name="psum", bufs=1))
 
-        def place(shape, dtype, name, tag=None):
-            return keep.tile(shape, dtype, name=name, offset=PLACES[tag or name], align_bytes=KIB)
-
-        dz_rows = dz.rearrange("(p j) x -> p j x", j=PACK)
-        w_rows = W.rearrange("(p j) d -> p j d", j=PACK)
-
-        dz_raw = place([P, PACK, X], F32, "dz_raw")
-        w_first = place([P, PACK, P], F32, "w_first")
-        w_rest = place([P, PACK, D - P], F32, "w_rest")
-        alpha = place([P, C], F32, "alpha")
-        idx_list = lists.tile([P, C // 16], U16, name="idx_list")
-        bag_list = lists.tile([P, C // 16], U16, name="bag_list")
-        slot_list = lists.tile([P, C // 16], U16, name="slot_list")
-        emb = [place([P, T], F32, f"emb{b}", f"emb{b}") for b in range(BLOCKS)]
-
-        def load_emb(b):
-            nc.sync.dma_start(emb[b][:], eT[b * P : (b + 1) * P, :])
-
-        load_emb(0)
-        nc.sync.dma_start(idx_list[:], offs)
-        load_emb(1)
-        nc.sync.dma_start(dz_raw[:], dz_rows)
-        nc.sync.dma_start(w_first[:], w_rows[:, :, :P])
-        load_emb(2)
-        nc.sync.dma_start(bag_list[:], bagoffs)
-        nc.sync.dma_start(w_rest[:], w_rows[:, :, P:])
-        load_emb(3)
-        nc.sync.dma_start(alpha[:], al)
-        nc.sync.dma_start(slot_list[:], slotoffs)
-
-        first_places = place([P, T], F32, "first_places")
-        u = place([P, (BLOCKS - 1) * X + U_WINDOW], F32, "u")
-        bag_sum = place([P, SUM_WINDOW], F32, "bag_sum")
-        second_places = place([P, T], F32, "second_places")
-        nc.gpsimd.memset(bag_sum[:, X:], 0.0)
-        identity = place([P, P], F32, "identity")
-        make_identity(nc, identity[:])
-        nc.gpsimd.memset(u[:, BLOCKS * X :], 0.0)
-        nc.gpsimd.memset(first_places[:], 0.0)
-        nc.gpsimd.memset(second_places[:], 0.0)
-        w_row = place([P, U_WINDOW], F32, "w_row")
-        nc.gpsimd.memset(w_row[:, C:], 0.0)
-
-        dz16 = place([P, X, PACK], BF16, "dz16")
-        w_first16 = place([P, P, PACK], BF16, "w_first16")
-        w_rest16 = place([P, D - P, PACK], BF16, "w_rest16", "prod0")
-        dz_codes = place([P, X], U32, "dz_codes")
-        dz_scales = place([P, X], U8, "dz_scales")
-        w_codes = place([P, D], U32, "w_codes")
-        w_scales = place([P, D], U8, "w_scales")
-
-        def quantize(codes, scales, fmt, first, grouped):
-            width = grouped.shape[1]
-            nc.vector.quantize_mx(
-                out=codes[:, first : first + width].bitcast(fmt),
-                scales=scales[:, first : first + width],
-                in_=grouped.rearrange("p c t -> p (c t)"),
-            )
+        def held(shape, dtype, name, tag=None):
+            return keep.tile(shape, dtype, name=name, tag=tag or name, align_bytes=ALIGN)
 
         def bank(i, name):
             return psum.tile([P, BANK], F32, name=name, tag=f"bank{i}")
 
-        def u_first(b):
-            return (BLOCKS - 1 - b) * X
+        def scalar_move(dst, src):
+            nc.scalar.activation(dst, src, COPY)
 
-        def product(b, copy_out):
+        def entries(listed, lo, hi):
+            return listed[:, lo // 16 : hi // 16]
+
+        dz_rows = dz.rearrange("(p j) x -> p j x", j=PACK)
+        w_rows = W.rearrange("(p j) d -> p j d", j=PACK)
+
+        dz_raw = held([P, PACK, X], F32, "dz_raw")
+        w_raw = [held([P, PACK, 2 * P], F32, f"w_raw{h}") for h in range(2)]
+        idx_list = lists.tile([P, C // 16], U16, name="idx_list", align_bytes=ALIGN)
+        bag_list = lists.tile([P, C // 16], U16, name="bag_list", align_bytes=ALIGN)
+        slot_list = lists.tile([P, C // 16], U16, name="slot_list", align_bytes=ALIGN)
+        emb = [held([P, T], F32, f"emb{b}") for b in range(BLOCKS)]
+        alpha = held([P, C], F32, "alpha")
+
+        nc.sync.dma_start(dz_raw[:], dz_rows)
+        nc.sync.dma_start(w_raw[0][:], w_rows[:, :, : 2 * P])
+        nc.sync.dma_start(w_raw[1][:], w_rows[:, :, 2 * P :])
+        nc.sync.dma_start(bag_list[:], bagoffs)
+        nc.sync.dma_start(alpha[:], al)
+        nc.sync.dma_start(idx_list[:], offs)
+        for b in range(BLOCKS):
+            nc.sync.dma_start(emb[b][:], eT[b * P : (b + 1) * P, :])
+        nc.sync.dma_start(slot_list[:], slotoffs)
+
+        identity = held([P, P], F32, "identity")
+        make_identity(nc, identity[:])
+        u = [held([P, BAG_WINDOW], F32, f"u{b}") for b in range(BLOCKS)]
+        bag_sum = held([P, BAG_WINDOW], F32, "bag_sum")
+        for padded in u + [bag_sum]:
+            nc.gpsimd.memset(padded[:, X:], 0.0)
+        places = [held([P, T], F32, f"places{i}") for i in range(3)]
+        for window in places:
+            nc.gpsimd.memset(window[:], 0.0)
+
+        dz16 = held([P, X, PACK], BF16, "dz16")
+        w16 = [held([P, 2 * P, PACK], BF16, f"w16_{h}") for h in range(2)]
+        dz_codes = held([P, X], U32, "dz_codes")
+        dz_scales = held([P, X], U8, "dz_scales")
+        w_codes = [held([P, 2 * P], U32, f"w_codes{h}") for h in range(2)]
+        w_scales = [held([P, 2 * P], U8, f"w_scales{h}") for h in range(2)]
+
+        def quantize(codes, scales, fmt, grouped):
+            nc.vector.quantize_mx(
+                out=codes[:].bitcast(fmt), scales=scales[:], in_=grouped[:].rearrange("p c t -> p (c t)")
+            )
+
+        def product(b):
             acc = bank(b, f"acc{b}")
-            cols = slice(b * P, (b + 1) * P)
+            cols = slice((b % 2) * P, (b % 2 + 1) * P)
             nc.tensor.matmul_mx(
                 out=acc[:],
-                lhsT=w_codes[:, cols].bitcast(E4M3X4),
-                lhsT_scale=w_scales[:, cols],
+                lhsT=w_codes[b // 2][:, cols].bitcast(E4M3X4),
+                lhsT_scale=w_scales[b // 2][:, cols],
                 rhs=dz_codes[:].bitcast(E5M2X4),
                 rhs_scale=dz_scales[:],
                 start=True,
                 stop=True,
             )
-            copy_out(u[:, u_first(b) : u_first(b) + X], acc[:])
+            nc.scalar.copy(u[b][:, :X], acc[:])
 
         interleave(nc.vector.tensor_copy, dz16, dz_raw, 0, DZ_SPLIT)
         interleave(nc.scalar.copy, dz16, dz_raw, DZ_SPLIT, X)
-        interleave(nc.scalar.copy, w_first16, w_first, 0, P)
-        quantize(dz_codes, dz_scales, E5M2X4, 0, dz16[:])
-        quantize(w_codes, w_scales, E4M3X4, 0, w_first16[:])
-        product(0, nc.scalar.copy)
+        quantize(dz_codes, dz_scales, E5M2X4, dz16)
+        for h in range(2):
+            interleave(nc.scalar.copy, w16[h], w_raw[h], 0, W_SPLIT)
+            interleave(nc.vector.tensor_copy, w16[h], w_raw[h], W_SPLIT, 2 * P)
+            quantize(w_codes[h], w_scales[h], E4M3X4, w16[h])
+            product(2 * h)
+            if h == 0:
+                ub0 = pairs.tile([P, C], F32, name="ub0", tag="ub", align_bytes=ALIGN)
+                scalar_move(ub0[:, :HALF], u[0][:].indirect(entries(bag_list, 0, HALF)))
+            product(2 * h + 1)
 
-        ub = [place([P, C], F32, f"ub{b}") for b in range(BLOCKS)]
-        et = [place([P, C], F32, f"et{b}", f"et{b}") for b in range(BLOCKS)]
-        de = {}
+        turned = [bank(6 + h, f"turned{h}") for h in range(2)]
+        de = [held([P, C], F32, f"de{b}") for b in range(BLOCKS)]
+        ub = {0: ub0}
+        et = {}
 
-        def look_up_u(b):
-            window = u[:, u_first(b) : u_first(b) + U_WINDOW]
-            nc.vector.tensor_copy(ub[b][:], window.indirect(bag_list[:]))
+        def look_up_u(b, halves):
+            if b not in ub:
+                ub[b] = pairs.tile([P, C], F32, name=f"ub{b}", tag="ub", align_bytes=ALIGN)
+            for h in halves:
+                lo, hi = h * HALF, (h + 1) * HALF
+                nc.vector.tensor_copy(ub[b][:, lo:hi], u[b][:].indirect(entries(bag_list, lo, hi)))
 
         def look_up_emb(b):
-            nc.vector.tensor_copy(et[b][:], emb[b][:].indirect(idx_list[:]))
+            et[b] = pairs.tile([P, C], F32, name=f"et{b}", tag="et", align_bytes=ALIGN)
+            for lo in (0, HALF):
+                nc.vector.tensor_copy(et[b][:, lo : lo + HALF], emb[b][:].indirect(entries(idx_list, lo, lo + HALF)))
 
-        def weigh(b, tag):
-            de[b] = place([P, C], F32, f"de{b}", tag)
-            nc.gpsimd.tensor_tensor(de[b][:], ub[b][:], alpha[:], MULT)
+        def weigh(b, lo, hi):
+            nc.gpsimd.tensor_tensor(de[b][:, lo:hi], ub[b][:, lo:hi], alpha[:, lo:hi], MULT)
 
-        def multiply(b):
-            prod = place([P, C], F32, f"prod{b}", f"prod{b}")
-            nc.gpsimd.tensor_tensor(prod[:], ub[b][:], et[b][:], MULT)
-            for k in range(CHUNKS):
-                nc.tensor.matmul(
-                    turned[k][:, :P], prod[:, k * P : (k + 1) * P], identity[:],
-                    start=(b == 0), stop=(b == BLOCKS - 1), is_transpose=True,
-                )
+        def multiply(b, engine):
+            prod = pairs.tile([P, C], F32, name=f"prod{b}", tag="prod", align_bytes=ALIGN)
+            for h in range(2):
+                cols = slice(h * HALF, (h + 1) * HALF)
+                engine.tensor_tensor(prod[:, cols], ub[b][:, cols], et[b][:, cols], MULT)
+                for q in range(4):
+                    nc.tensor.matmul(
+                        turned[h][:, q * P : (q + 1) * P],
+                        prod[:, h * HALF + q * P : h * HALF + (q + 1) * P],
+                        identity[:],
+                        start=(b == 0 and q == 0),
+                        stop=(b == BLOCKS - 1 and q == 3),
+                        is_transpose=True,
+                    )
 
-        def put(b, window):
-            nc.vector.tensor_copy(window[:].indirect(idx_list[:]), de[b][:])
+        def put(move, b, window, lo, hi):
+            move(window[:].indirect(entries(idx_list, lo, hi)), de[b][:, lo:hi])
+
+        def store(b, window):
             nc.sync.dma_start(out_0[b * P : (b + 1) * P, :], window[:])
 
-        def first_columns(dst, src, count):
-            nc.scalar.copy(dst, src[:].rearrange("p (k q) -> p k q", q=P)[:, :count, 0])
-
-        def spread(dst, column):
-            nc.tensor.transpose(dst, column.to_broadcast([P, P]), identity[:])
-
-        look_up_emb(0)
-        look_up_u(0)
-        interleave(nc.scalar.copy, w_rest16, w_rest, 0, D - P)
-        quantize(w_codes, w_scales, E4M3X4, P, w_rest16[:, :P, :])
-        quantize(w_codes, w_scales, E4M3X4, 2 * P, w_rest16[:, P:, :])
-        for b in range(1, BLOCKS):
-            product(b, lambda dst, src: nc.scalar.activation(dst, src, COPY))
-
-        alpha_cols = place([P, CHUNKS], F32, "alpha_cols")
-        for h in range(2):
-            alpha_turned = bank(BLOCKS + h, f"alpha_turned{h}")
-            for q in range(4):
-                k = 4 * h + q
-                nc.tensor.transpose(alpha_turned[:, q * P : (q + 1) * P], alpha[:, k * P : (k + 1) * P], identity[:])
-            first_columns(alpha_cols[:, 4 * h : 4 * h + 4], alpha_turned, 4)
-
-        turned = [bank(k, f"turned{k}") for k in range(CHUNKS)]
-        multiply(0)
-        for b in range(1, BLOCKS):
-            look_up_u(b)
-        look_up_emb(1)
-        weigh(0, "de0")
-        multiply(1)
+        look_up_u(0, (1,))
+        for b in range(2):
+            for lo, hi in THIRDS:
+                weigh(b, lo, hi)
+                put(scalar_move, b, places[b], lo, hi)
+            store(b, places[b])
+            look_up_emb(b)
+            multiply(b, nc.gpsimd)
+            look_up_u(b + 1, (0, 1))
+        weigh(2, *SHARED[0])
+        put(scalar_move, 2, places[2], *SHARED[0])
         look_up_emb(2)
-        put(0, first_places)
-        weigh(1, "de1")
-        multiply(2)
+        multiply(2, nc.gpsimd)
+        look_up_u(3, (0, 1))
         look_up_emb(3)
-        put(1, second_places)
-        multiply(3)
-        weigh(2, "de2")
+        multiply(3, nc.vector)
 
-        w_cols = place([P, CHUNKS], F32, "w_cols", "third_places")
-        spent = place([P, P], F32, "spent")
-        for k in range(CHUNKS):
-            nc.scalar.activation(
-                spent[:], turned[k][:, :P], COPY, scale=alpha_cols[:, k : k + 1], accum_out=w_cols[:, k : k + 1]
-            )
-        w_spread = [bank(h, f"w_spread{h}") for h in range(2)]
+        dal_cols = held([P, 2, 4], F32, "dal_cols")
+        w_row = held([P, C], F32, "w_row")
         for h in range(2):
+            nc.vector.tensor_reduce(dal_cols[:, h, :], turned[h][:].rearrange("p (q d) -> p q d", d=P), AXIS_X, ADD)
+        for lo, hi in SHARED[1:]:
+            weigh(2, lo, hi)
+        for lo, hi in THIRDS:
+            weigh(3, lo, hi)
+            put(scalar_move, 3, places[0], lo, hi)
+        store(3, places[0])
+        put(nc.vector.tensor_copy, 2, places[2], *SHARED[1])
+        for h in range(2):
+            dal_spread = bank(BLOCKS + h, f"dal_spread{h}")
             for q in range(4):
-                k = 4 * h + q
-                spread(w_spread[h][:, q * P : (q + 1) * P], w_cols[:, k : k + 1])
-            nc.scalar.copy(w_row[:, h * BANK : (h + 1) * BANK], w_spread[h][:])
+                column = dal_cols[:, h, q : q + 1]
+                nc.tensor.transpose(dal_spread[:, q * P : (q + 1) * P], column.to_broadcast([P, P]), identity[:])
+            cols = slice(h * HALF, (h + 1) * HALF)
+            nc.vector.tensor_tensor(w_row[:, cols], dal_spread[:], alpha[:, cols], MULT)
+        put(nc.vector.tensor_copy, 2, places[2], *SHARED[2])
+        store(2, places[2])
 
-        by_bag = place([P, C], F32, "by_bag")
-        nc.vector.tensor_copy(by_bag[:], w_row[:].indirect(slot_list[:]))
+        by_bag = held([P, C], F32, "by_bag")
+        nc.vector.tensor_copy(by_bag[:, :HALF], w_row[:].indirect(entries(slot_list, 0, HALF)))
+        scalar_move(by_bag[:, HALF:], w_row[:].indirect(entries(slot_list, HALF, C)))
+        for h in range(2):
+            slots = by_bag[:, h * HALF : (h + 1) * HALF].rearrange("p (x j) -> p x j", j=2)
+            nc.vector.tensor_tensor(bag_sum[:, h * X // 2 : (h + 1) * X // 2], slots[:, :, 0], slots[:, :, 1], ADD)
 
-        third_places = place([P, T], F32, "third_places", "third_places")
-        nc.gpsimd.memset(third_places[:], 0.0)
-        put(2, third_places)
-
-        pair_sums = bank(2, "pair_sums")
-        for q in range(4):
-            for j in range(2):
-                nc.tensor.matmul(
-                    pair_sums[:, q * P : (q + 1) * P], by_bag[:, 2 * q * P + j : 2 * (q + 1) * P : 2], identity[:],
-                    start=(j == 0), stop=(j == 1), is_transpose=True,
-                )
-        sum_cols = place([P, 4], F32, "sum_cols", "de3")
-        first_columns(sum_cols[:], pair_sums, 4)
-        sum_spread = bank(3, "sum_spread")
-        for q in range(4):
-            spread(sum_spread[:, q * P : (q + 1) * P], sum_cols[:, q : q + 1])
-        nc.scalar.copy(bag_sum[:, :X], sum_spread[:])
-
-        result = place([P, C], F32, "result")
-
-        def look_up_sum(dst, lo, hi):
-            nc.vector.tensor_tensor(dst, bag_sum[:].indirect(bag_list[:, lo // 16 : hi // 16]), alpha[:, lo:hi], MULT)
-
-        early = place([P, EARLY], F32, "early", "taken")
-        look_up_sum(early[:], 0, EARLY)
-        weigh(3, "de3")
-        nc.gpsimd.tensor_tensor(result[0:1, :EARLY], w_row[0:1, :EARLY], early[0:1, :], SUBTRACT)
-        put(3, first_places)
-
-        late = place([P, C - EARLY], F32, "late", "taken")
-        look_up_sum(late[:, : MIDDLE - EARLY], EARLY, MIDDLE)
-        look_up_sum(late[:, MIDDLE - EARLY :], MIDDLE, C)
-        nc.gpsimd.tensor_tensor(result[0:1, EARLY:BANK], w_row[0:1, EARLY:BANK], late[0:1, : BANK - EARLY], SUBTRACT)
-        for lo, hi in ((BANK, MIDDLE), (MIDDLE, C)):
-            nc.vector.tensor_tensor(
-                result[0:1, lo:hi], w_spread[1][0:1, lo - BANK : hi - BANK], late[0:1, lo - EARLY : hi - EARLY], SUBTRACT
-            )
+        taken = held([P, C], F32, "taken")
+        plain = held([P, HALF], F32, "plain")
+        result = held([P, C], F32, "result")
+        scalar_move(plain[:], bag_sum[:].indirect(entries(bag_list, HALF, C)))
+        nc.vector.tensor_tensor(taken[:, :HALF], bag_sum[:].indirect(entries(bag_list, 0, HALF)), alpha[:, :HALF], MULT)
+        nc.vector.tensor_tensor(taken[0:1, HALF:], plain[0:1, :], alpha[0:1, HALF:], MULT)
+        nc.vector.tensor_tensor(result[0:1, :HALF], w_row[0:1, :HALF], taken[0:1, :HALF], SUBTRACT)
+        nc.vector.tensor_tensor(result[0:1, HALF:], w_row[0:1, HALF:], taken[0:1, HALF:], SUBTRACT)
         nc.scalar.dma_start(out_1, result[0:1, :])

@@ -6,6 +6,7 @@ from concourse.masks import make_identity
 F32 = mybir.dt.float32
 BF16 = mybir.dt.bfloat16
 U32 = mybir.dt.uint32
+I32 = mybir.dt.int32
 U16 = mybir.dt.uint16
 U8 = mybir.dt.uint8
 E4M3X4 = mybir.dt.float8_e4m3fn_x4
@@ -24,10 +25,9 @@ BANK = 512
 HALF = C // 2
 BAG_WINDOW = X + 16
 ALIGN = 256
-DZ_SPLIT = 336
-W_SPLIT = 160
+CAST_SPLIT = 176
 THIRDS = ((0, 384), (384, 768), (768, 1024))
-SHARED = ((0, 384), (384, 704), (704, 1024))
+FIRST_AND_REST = ((0, 384), (384, 1024))
 
 FLOPS = 2 * M * D * X
 
@@ -44,7 +44,6 @@ def tile_attend_gmil_kernel(tc, eT, W, dz, al, offs, bagoffs, slotoffs, out_0, o
     with ExitStack() as ctx:
         lists = ctx.enter_context(tc.tile_pool(name="lists", bufs=1))
         keep = ctx.enter_context(tc.tile_pool(name="keep", bufs=1))
-        pairs = ctx.enter_context(tc.tile_pool(name="pairs", bufs=2))
         psum = ctx.enter_context(tc.psum_pool(name="psum", bufs=1))
 
         def held(shape, dtype, name, tag=None):
@@ -62,7 +61,7 @@ def tile_attend_gmil_kernel(tc, eT, W, dz, al, offs, bagoffs, slotoffs, out_0, o
         dz_rows = dz.rearrange("(p j) x -> p j x", j=PACK)
         w_rows = W.rearrange("(p j) d -> p j d", j=PACK)
 
-        dz_raw = held([P, PACK, X], F32, "dz_raw")
+        dz_raw = [held([P, PACK, 2 * P], F32, f"dz_raw{h}") for h in range(2)]
         w_raw = [held([P, PACK, 2 * P], F32, f"w_raw{h}") for h in range(2)]
         idx_list = lists.tile([P, C // 16], U16, name="idx_list", align_bytes=ALIGN)
         bag_list = lists.tile([P, C // 16], U16, name="bag_list", align_bytes=ALIGN)
@@ -70,8 +69,9 @@ def tile_attend_gmil_kernel(tc, eT, W, dz, al, offs, bagoffs, slotoffs, out_0, o
         emb = [held([P, T], F32, f"emb{b}") for b in range(BLOCKS)]
         alpha = held([P, C], F32, "alpha")
 
-        nc.sync.dma_start(dz_raw[:], dz_rows)
         nc.sync.dma_start(w_raw[0][:], w_rows[:, :, : 2 * P])
+        nc.sync.dma_start(dz_raw[0][:], dz_rows[:, :, : 2 * P])
+        nc.sync.dma_start(dz_raw[1][:], dz_rows[:, :, 2 * P :])
         nc.sync.dma_start(w_raw[1][:], w_rows[:, :, 2 * P :])
         nc.sync.dma_start(bag_list[:], bagoffs)
         nc.sync.dma_start(alpha[:], al)
@@ -85,142 +85,136 @@ def tile_attend_gmil_kernel(tc, eT, W, dz, al, offs, bagoffs, slotoffs, out_0, o
         u = [held([P, BAG_WINDOW], F32, f"u{b}") for b in range(BLOCKS)]
         bag_sum = held([P, BAG_WINDOW], F32, "bag_sum")
         for padded in u + [bag_sum]:
-            nc.gpsimd.memset(padded[:, X:], 0.0)
+            nc.vector.memset(padded[:, X:], 0.0)
         places = [held([P, T], F32, f"places{i}") for i in range(3)]
         for window in places:
-            nc.gpsimd.memset(window[:], 0.0)
+            nc.vector.memset(window[:].bitcast(I32), 0)
 
-        dz16 = held([P, X, PACK], BF16, "dz16")
+        dz16 = [held([P, 2 * P, PACK], BF16, f"dz16_{h}") for h in range(2)]
         w16 = [held([P, 2 * P, PACK], BF16, f"w16_{h}") for h in range(2)]
         dz_codes = held([P, X], U32, "dz_codes")
         dz_scales = held([P, X], U8, "dz_scales")
-        w_codes = [held([P, 2 * P], U32, f"w_codes{h}") for h in range(2)]
-        w_scales = [held([P, 2 * P], U8, f"w_scales{h}") for h in range(2)]
+        w_codes = held([P, D], U32, "w_codes")
+        w_scales = held([P, D], U8, "w_scales")
 
-        def quantize(codes, scales, fmt, grouped):
+        def quantize(codes, scales, fmt, grouped, raw, h):
+            interleave(nc.vector.tensor_copy, grouped, raw, 0, CAST_SPLIT)
+            interleave(nc.scalar.copy, grouped, raw, CAST_SPLIT, 2 * P)
+            cols = slice(2 * h * P, 2 * (h + 1) * P)
             nc.vector.quantize_mx(
-                out=codes[:].bitcast(fmt), scales=scales[:], in_=grouped[:].rearrange("p c t -> p (c t)")
+                out=codes[:, cols].bitcast(fmt), scales=scales[:, cols], in_=grouped[:].rearrange("p c t -> p (c t)")
             )
 
-        def product(b):
-            acc = bank(b, f"acc{b}")
-            cols = slice((b % 2) * P, (b % 2 + 1) * P)
+        def product(b, lo, hi, i, copy_out):
+            acc = bank(i, f"acc{b}_{lo}")
+            cols = slice(b * P, (b + 1) * P)
             nc.tensor.matmul_mx(
-                out=acc[:],
-                lhsT=w_codes[b // 2][:, cols].bitcast(E4M3X4),
-                lhsT_scale=w_scales[b // 2][:, cols],
-                rhs=dz_codes[:].bitcast(E5M2X4),
-                rhs_scale=dz_scales[:],
+                out=acc[:, : hi - lo],
+                lhsT=w_codes[:, cols].bitcast(E4M3X4),
+                lhsT_scale=w_scales[:, cols],
+                rhs=dz_codes[:, lo:hi].bitcast(E5M2X4),
+                rhs_scale=dz_scales[:, lo:hi],
                 start=True,
                 stop=True,
             )
-            nc.scalar.copy(u[b][:, :X], acc[:])
+            copy_out(u[b][:, lo:hi], acc[:, : hi - lo])
 
-        interleave(nc.vector.tensor_copy, dz16, dz_raw, 0, DZ_SPLIT)
-        interleave(nc.scalar.copy, dz16, dz_raw, DZ_SPLIT, X)
-        quantize(dz_codes, dz_scales, E5M2X4, dz16)
-        for h in range(2):
-            interleave(nc.scalar.copy, w16[h], w_raw[h], 0, W_SPLIT)
-            interleave(nc.vector.tensor_copy, w16[h], w_raw[h], W_SPLIT, 2 * P)
-            quantize(w_codes[h], w_scales[h], E4M3X4, w16[h])
-            product(2 * h)
-            if h == 0:
-                ub0 = pairs.tile([P, C], F32, name="ub0", tag="ub", align_bytes=ALIGN)
-                scalar_move(ub0[:, :HALF], u[0][:].indirect(entries(bag_list, 0, HALF)))
-            product(2 * h + 1)
+        quantize(w_codes, w_scales, E4M3X4, w16[0], w_raw[0], 0)
+        quantize(dz_codes, dz_scales, E5M2X4, dz16[0], dz_raw[0], 0)
+        quantize(dz_codes, dz_scales, E5M2X4, dz16[1], dz_raw[1], 1)
+        product(0, 0, X // 2, 0, nc.scalar.copy)
+        product(1, 0, X // 2, 1, nc.scalar.copy)
+        product(0, X // 2, X, 2, nc.scalar.copy)
+        product(1, X // 2, X, 3, nc.vector.tensor_copy)
+        quantize(w_codes, w_scales, E4M3X4, w16[1], w_raw[1], 1)
 
         turned = [bank(6 + h, f"turned{h}") for h in range(2)]
-        de = [held([P, C], F32, f"de{b}") for b in range(BLOCKS)]
-        ub = {0: ub0}
-        et = {}
+        ub = [held([P, C], F32, f"ub{b}") for b in range(BLOCKS)]
+        et = [held([P, C], F32, f"et{b}") for b in range(BLOCKS)]
+        de = [held([P, C], F32, f"de{b}") for b in range(BLOCKS - 1)]
 
-        def look_up_u(b, halves):
-            if b not in ub:
-                ub[b] = pairs.tile([P, C], F32, name=f"ub{b}", tag="ub", align_bytes=ALIGN)
-            for h in halves:
-                lo, hi = h * HALF, (h + 1) * HALF
-                nc.vector.tensor_copy(ub[b][:, lo:hi], u[b][:].indirect(entries(bag_list, lo, hi)))
+        def look_up_u(move, b, h):
+            lo, hi = h * HALF, (h + 1) * HALF
+            move(ub[b][:, lo:hi], u[b][:].indirect(entries(bag_list, lo, hi)))
 
         def look_up_emb(b):
-            et[b] = pairs.tile([P, C], F32, name=f"et{b}", tag="et", align_bytes=ALIGN)
-            for lo in (0, HALF):
-                nc.vector.tensor_copy(et[b][:, lo : lo + HALF], emb[b][:].indirect(entries(idx_list, lo, lo + HALF)))
+            nc.vector.tensor_copy(et[b][:], emb[b][:].indirect(idx_list[:]))
 
         def weigh(b, lo, hi):
             nc.gpsimd.tensor_tensor(de[b][:, lo:hi], ub[b][:, lo:hi], alpha[:, lo:hi], MULT)
 
-        def multiply(b, engine):
-            prod = pairs.tile([P, C], F32, name=f"prod{b}", tag="prod", align_bytes=ALIGN)
-            for h in range(2):
-                cols = slice(h * HALF, (h + 1) * HALF)
-                engine.tensor_tensor(prod[:, cols], ub[b][:, cols], et[b][:, cols], MULT)
-                for q in range(4):
+        def multiply(b, engine, pieces):
+            prod = held([P, C], F32, f"prod{b}")
+            for lo, hi in pieces:
+                engine.tensor_tensor(prod[:, lo:hi], ub[b][:, lo:hi], et[b][:, lo:hi], MULT)
+                for first in range(lo, hi, P):
+                    col = first % HALF
                     nc.tensor.matmul(
-                        turned[h][:, q * P : (q + 1) * P],
-                        prod[:, h * HALF + q * P : h * HALF + (q + 1) * P],
+                        turned[first // HALF][:, col : col + P],
+                        prod[:, first : first + P],
                         identity[:],
-                        start=(b == 0 and q == 0),
-                        stop=(b == BLOCKS - 1 and q == 3),
+                        start=(b == 0 and col == 0),
+                        stop=(b == BLOCKS - 1 and col == HALF - P),
                         is_transpose=True,
                     )
 
         def put(move, b, window, lo, hi):
             move(window[:].indirect(entries(idx_list, lo, hi)), de[b][:, lo:hi])
+            if hi == C:
+                nc.sync.dma_start(out_0[b * P : (b + 1) * P, :], window[:])
 
-        def store(b, window):
-            nc.sync.dma_start(out_0[b * P : (b + 1) * P, :], window[:])
-
-        look_up_u(0, (1,))
-        for b in range(2):
-            for lo, hi in THIRDS:
+        whole = ((0, C),)
+        halves = ((0, HALF), (HALF, C))
+        look_up_u(scalar_move, 0, 0)
+        look_up_u(nc.vector.tensor_copy, 0, 1)
+        product(2, 0, X, 4, nc.scalar.copy)
+        product(3, 0, X, 5, nc.scalar.copy)
+        for b in range(1, BLOCKS):
+            for h in range(2):
+                look_up_u(nc.vector.tensor_copy, b, h)
+        for lo, hi in FIRST_AND_REST:
+            for b in range(2):
                 weigh(b, lo, hi)
+        for lo, hi in THIRDS:
+            for b in range(2):
                 put(scalar_move, b, places[b], lo, hi)
-            store(b, places[b])
+        for b in range(BLOCKS):
             look_up_emb(b)
-            multiply(b, nc.gpsimd)
-            look_up_u(b + 1, (0, 1))
-        weigh(2, *SHARED[0])
-        put(scalar_move, 2, places[2], *SHARED[0])
-        look_up_emb(2)
-        multiply(2, nc.gpsimd)
-        look_up_u(3, (0, 1))
-        look_up_emb(3)
-        multiply(3, nc.vector)
+        weigh(2, 0, C)
+        for lo, hi in THIRDS:
+            put(scalar_move, 2, places[2], lo, hi)
+        for b in range(BLOCKS - 1):
+            multiply(b, nc.gpsimd, whole)
+        multiply(3, nc.vector, halves)
 
-        dal_cols = held([P, 2, 4], F32, "dal_cols")
+        dal_cols = [held([P, 4], F32, f"dal_cols{h}") for h in range(2)]
         w_row = held([P, C], F32, "w_row")
         for h in range(2):
-            nc.vector.tensor_reduce(dal_cols[:, h, :], turned[h][:].rearrange("p (q d) -> p q d", d=P), AXIS_X, ADD)
-        for lo, hi in SHARED[1:]:
-            weigh(2, lo, hi)
-        for lo, hi in THIRDS:
-            weigh(3, lo, hi)
-            put(scalar_move, 3, places[0], lo, hi)
-        store(3, places[0])
-        put(nc.vector.tensor_copy, 2, places[2], *SHARED[1])
+            nc.vector.tensor_reduce(dal_cols[h][:], turned[h][:].rearrange("p (q d) -> p q d", d=P), AXIS_X, ADD)
         for h in range(2):
-            dal_spread = bank(BLOCKS + h, f"dal_spread{h}")
+            dal_spread = bank(h, f"dal_spread{h}")
             for q in range(4):
-                column = dal_cols[:, h, q : q + 1]
+                column = dal_cols[h][:, q : q + 1]
                 nc.tensor.transpose(dal_spread[:, q * P : (q + 1) * P], column.to_broadcast([P, P]), identity[:])
             cols = slice(h * HALF, (h + 1) * HALF)
             nc.vector.tensor_tensor(w_row[:, cols], dal_spread[:], alpha[:, cols], MULT)
-        put(nc.vector.tensor_copy, 2, places[2], *SHARED[2])
-        store(2, places[2])
+        de.append(held([P, C], F32, "de3", "dal_cols0"))
+        for lo, hi in FIRST_AND_REST:
+            weigh(3, lo, hi)
+            put(nc.vector.tensor_copy, 3, places[0], lo, hi)
 
-        by_bag = held([P, C], F32, "by_bag")
-        nc.vector.tensor_copy(by_bag[:, :HALF], w_row[:].indirect(entries(slot_list, 0, HALF)))
-        scalar_move(by_bag[:, HALF:], w_row[:].indirect(entries(slot_list, HALF, C)))
-        for h in range(2):
-            slots = by_bag[:, h * HALF : (h + 1) * HALF].rearrange("p (x j) -> p x j", j=2)
-            nc.vector.tensor_tensor(bag_sum[:, h * X // 2 : (h + 1) * X // 2], slots[:, :, 0], slots[:, :, 1], ADD)
+        by_bag = held([P, C], F32, "by_bag", "de2")
+        for h, (lo, hi) in enumerate(halves):
+            scalar_move(by_bag[:, lo:hi], w_row[:].indirect(entries(slot_list, lo, hi)))
+            slots = by_bag[:, lo:hi].rearrange("p (x j) -> p x j", j=2)
+            nc.gpsimd.tensor_tensor(bag_sum[:, lo // 2 : hi // 2], slots[:, :, 0], slots[:, :, 1], ADD)
 
+        looked = held([P, C], F32, "looked")
         taken = held([P, C], F32, "taken")
-        plain = held([P, HALF], F32, "plain")
         result = held([P, C], F32, "result")
-        scalar_move(plain[:], bag_sum[:].indirect(entries(bag_list, HALF, C)))
-        nc.vector.tensor_tensor(taken[:, :HALF], bag_sum[:].indirect(entries(bag_list, 0, HALF)), alpha[:, :HALF], MULT)
-        nc.vector.tensor_tensor(taken[0:1, HALF:], plain[0:1, :], alpha[0:1, HALF:], MULT)
-        nc.vector.tensor_tensor(result[0:1, :HALF], w_row[0:1, :HALF], taken[0:1, :HALF], SUBTRACT)
-        nc.vector.tensor_tensor(result[0:1, HALF:], w_row[0:1, HALF:], taken[0:1, HALF:], SUBTRACT)
+        for lo, hi in halves:
+            scalar_move(looked[:, lo:hi], bag_sum[:].indirect(entries(bag_list, lo, hi)))
+        for lo, hi in halves:
+            nc.vector.tensor_tensor(taken[0:1, lo:hi], looked[0:1, lo:hi], alpha[0:1, lo:hi], MULT)
+            nc.vector.tensor_tensor(result[0:1, lo:hi], w_row[0:1, lo:hi], taken[0:1, lo:hi], SUBTRACT)
         nc.scalar.dma_start(out_1, result[0:1, :])

@@ -25,7 +25,7 @@ BANK = 512
 HALF = C // 2
 BAG_WINDOW = X + 16
 ALIGN = 256
-CAST_SPLIT = 176
+CAST_SPLIT = 128
 THIRDS = ((0, 384), (384, 768), (768, 1024))
 FIRST_AND_REST = ((0, 384), (384, 1024))
 
@@ -74,10 +74,11 @@ def tile_attend_gmil_kernel(tc, eT, W, dz, al, offs, bagoffs, slotoffs, out_0, o
         nc.sync.dma_start(dz_raw[1][:], dz_rows[:, :, 2 * P :])
         nc.sync.dma_start(w_raw[1][:], w_rows[:, :, 2 * P :])
         nc.sync.dma_start(bag_list[:], bagoffs)
-        nc.sync.dma_start(alpha[:], al)
         nc.sync.dma_start(idx_list[:], offs)
         for b in range(BLOCKS):
             nc.sync.dma_start(emb[b][:], eT[b * P : (b + 1) * P, :])
+            if b == 0:
+                nc.sync.dma_start(alpha[:], al)
         nc.sync.dma_start(slot_list[:], slotoffs)
 
         identity = held([P, P], F32, "identity")
@@ -86,9 +87,9 @@ def tile_attend_gmil_kernel(tc, eT, W, dz, al, offs, bagoffs, slotoffs, out_0, o
         bag_sum = held([P, BAG_WINDOW], F32, "bag_sum")
         for padded in u + [bag_sum]:
             nc.vector.memset(padded[:, X:], 0.0)
-        places = [held([P, T], F32, f"places{i}") for i in range(3)]
-        for window in places:
-            nc.vector.memset(window[:].bitcast(I32), 0)
+        places = [held([P, T], F32, f"places{i}") for i in range(2)]
+        nc.vector.memset(places[0][:].bitcast(I32), 0)
+        nc.gpsimd.memset(places[1][:], 0.0)
 
         dz16 = [held([P, 2 * P, PACK], BF16, f"dz16_{h}") for h in range(2)]
         w16 = [held([P, 2 * P, PACK], BF16, f"w16_{h}") for h in range(2)]
@@ -143,8 +144,13 @@ def tile_attend_gmil_kernel(tc, eT, W, dz, al, offs, bagoffs, slotoffs, out_0, o
         def weigh(b, lo, hi):
             nc.gpsimd.tensor_tensor(de[b][:, lo:hi], ub[b][:, lo:hi], alpha[:, lo:hi], MULT)
 
+        def weigh_and_put_last(lo, hi, tag):
+            piece = held([P, hi - lo], F32, f"de3_{lo}", tag)
+            nc.gpsimd.tensor_tensor(piece[:], ub[3][:, lo:hi], alpha[:, lo:hi], MULT)
+            nc.vector.tensor_copy(places[0][:].indirect(entries(idx_list, lo, hi)), piece[:])
+
         def multiply(b, engine, pieces):
-            prod = held([P, C], F32, f"prod{b}")
+            prod = held([P, C], F32, f"prod{b}", "u3" if b == 1 else None)
             for lo, hi in pieces:
                 engine.tensor_tensor(prod[:, lo:hi], ub[b][:, lo:hi], et[b][:, lo:hi], MULT)
                 for first in range(lo, hi, P):
@@ -166,31 +172,35 @@ def tile_attend_gmil_kernel(tc, eT, W, dz, al, offs, bagoffs, slotoffs, out_0, o
         whole = ((0, C),)
         halves = ((0, HALF), (HALF, C))
         look_up_u(scalar_move, 0, 0)
-        look_up_u(nc.vector.tensor_copy, 0, 1)
+        look_up_u(scalar_move, 0, 1)
         product(2, 0, X, 4, nc.scalar.copy)
         product(3, 0, X, 5, nc.scalar.copy)
+        places.append(held([P, T], F32, "places2", "w16_1"))
+        nc.gpsimd.memset(places[2][:], 0.0)
         for b in range(1, BLOCKS):
             for h in range(2):
-                look_up_u(nc.vector.tensor_copy, b, h)
+                look_up_u(scalar_move, b, h)
+        look_up_emb(0)
         for lo, hi in FIRST_AND_REST:
-            for b in range(2):
-                weigh(b, lo, hi)
-        for lo, hi in THIRDS:
-            for b in range(2):
-                put(scalar_move, b, places[b], lo, hi)
-        for b in range(BLOCKS):
+            weigh(0, lo, hi)
+            put(nc.vector.tensor_copy, 0, places[0], lo, hi)
+        for b in range(1, BLOCKS):
             look_up_emb(b)
-        weigh(2, 0, C)
+        for b in (1, 2):
+            weigh(b, 0, C)
         for lo, hi in THIRDS:
-            put(scalar_move, 2, places[2], lo, hi)
+            for b in (1, 2):
+                put(scalar_move, b, places[b], lo, hi)
         for b in range(BLOCKS - 1):
             multiply(b, nc.gpsimd, whole)
         multiply(3, nc.vector, halves)
+        weigh_and_put_last(0, 256, None)
 
         dal_cols = [held([P, 4], F32, f"dal_cols{h}") for h in range(2)]
         w_row = held([P, C], F32, "w_row")
         for h in range(2):
             nc.vector.tensor_reduce(dal_cols[h][:], turned[h][:].rearrange("p (q d) -> p q d", d=P), AXIS_X, ADD)
+        weigh_and_put_last(256, HALF, "prod3")
         for h in range(2):
             dal_spread = bank(h, f"dal_spread{h}")
             for q in range(4):
@@ -198,10 +208,8 @@ def tile_attend_gmil_kernel(tc, eT, W, dz, al, offs, bagoffs, slotoffs, out_0, o
                 nc.tensor.transpose(dal_spread[:, q * P : (q + 1) * P], column.to_broadcast([P, P]), identity[:])
             cols = slice(h * HALF, (h + 1) * HALF)
             nc.vector.tensor_tensor(w_row[:, cols], dal_spread[:], alpha[:, cols], MULT)
-        de.append(held([P, C], F32, "de3", "dal_cols0"))
-        for lo, hi in FIRST_AND_REST:
-            weigh(3, lo, hi)
-            put(nc.vector.tensor_copy, 3, places[0], lo, hi)
+        weigh_and_put_last(HALF, C, "dal_cols1")
+        nc.sync.dma_start(out_0[3 * P :, :], places[0][:])
 
         by_bag = held([P, C], F32, "by_bag", "de2")
         for h, (lo, hi) in enumerate(halves):

@@ -125,8 +125,8 @@ def tile_attend_gmil_kernel(tc, eT, W, dz, al, offs, bagoffs, slotoffs, out_0, o
         quantize(dz_codes, dz_scales, E5M2X4, dz16[1], dz_raw[1], 1)
         product(0, 0, X // 2, 0, nc.scalar.copy)
         product(1, 0, X // 2, 1, nc.scalar.copy)
-        product(0, X // 2, X, 2, nc.scalar.copy)
-        product(1, X // 2, X, 3, nc.vector.tensor_copy)
+        product(0, X // 2, X, 2, nc.vector.tensor_copy)
+        product(1, X // 2, X, 3, nc.scalar.copy)
         quantize(w_codes, w_scales, E4M3X4, w16[1], w_raw[1], 1)
 
         turned = [bank(6 + h, f"turned{h}") for h in range(2)]
@@ -144,11 +144,6 @@ def tile_attend_gmil_kernel(tc, eT, W, dz, al, offs, bagoffs, slotoffs, out_0, o
         def weigh(b, lo, hi):
             nc.gpsimd.tensor_tensor(de[b][:, lo:hi], ub[b][:, lo:hi], alpha[:, lo:hi], MULT)
 
-        def weigh_and_put_last(lo, hi, tag):
-            piece = held([P, hi - lo], F32, f"de3_{lo}", tag)
-            nc.gpsimd.tensor_tensor(piece[:], ub[3][:, lo:hi], alpha[:, lo:hi], MULT)
-            nc.vector.tensor_copy(places[0][:].indirect(entries(idx_list, lo, hi)), piece[:])
-
         def multiply(b, engine, pieces):
             prod = held([P, C], F32, f"prod{b}", "u3" if b == 1 else None)
             for lo, hi in pieces:
@@ -164,20 +159,25 @@ def tile_attend_gmil_kernel(tc, eT, W, dz, al, offs, bagoffs, slotoffs, out_0, o
                         is_transpose=True,
                     )
 
+        early = []
+
         def put(move, b, window, lo, hi):
-            move(window[:].indirect(entries(idx_list, lo, hi)), de[b][:, lo:hi])
+            source = early[0][:] if (b, lo) == (BLOCKS - 1, 0) else de[b][:, lo:hi]
+            move(window[:].indirect(entries(idx_list, lo, hi)), source)
             if hi == C:
                 nc.sync.dma_start(out_0[b * P : (b + 1) * P, :], window[:])
 
         whole = ((0, C),)
         halves = ((0, HALF), (HALF, C))
         look_up_u(scalar_move, 0, 0)
-        look_up_u(scalar_move, 0, 1)
+        look_up_u(nc.vector.tensor_copy, 0, 1)
         product(2, 0, X, 4, nc.scalar.copy)
         product(3, 0, X, 5, nc.scalar.copy)
         places.append(held([P, T], F32, "places2", "w16_1"))
         nc.gpsimd.memset(places[2][:], 0.0)
-        for b in range(1, BLOCKS):
+        look_up_u(nc.vector.tensor_copy, 1, 0)
+        look_up_u(nc.vector.tensor_copy, 1, 1)
+        for b in range(2, BLOCKS):
             for h in range(2):
                 look_up_u(scalar_move, b, h)
         look_up_emb(0)
@@ -191,16 +191,16 @@ def tile_attend_gmil_kernel(tc, eT, W, dz, al, offs, bagoffs, slotoffs, out_0, o
         for lo, hi in THIRDS:
             for b in (1, 2):
                 put(scalar_move, b, places[b], lo, hi)
+        early.append(held([P, THIRDS[0][1]], F32, "early"))
+        nc.gpsimd.tensor_tensor(early[0][:], ub[3][:, : THIRDS[0][1]], alpha[:, : THIRDS[0][1]], MULT)
         for b in range(BLOCKS - 1):
             multiply(b, nc.gpsimd, whole)
         multiply(3, nc.vector, halves)
-        weigh_and_put_last(0, 256, None)
 
         dal_cols = [held([P, 4], F32, f"dal_cols{h}") for h in range(2)]
         w_row = held([P, C], F32, "w_row")
         for h in range(2):
             nc.vector.tensor_reduce(dal_cols[h][:], turned[h][:].rearrange("p (q d) -> p q d", d=P), AXIS_X, ADD)
-        weigh_and_put_last(256, HALF, "prod3")
         for h in range(2):
             dal_spread = bank(h, f"dal_spread{h}")
             for q in range(4):
@@ -208,21 +208,22 @@ def tile_attend_gmil_kernel(tc, eT, W, dz, al, offs, bagoffs, slotoffs, out_0, o
                 nc.tensor.transpose(dal_spread[:, q * P : (q + 1) * P], column.to_broadcast([P, P]), identity[:])
             cols = slice(h * HALF, (h + 1) * HALF)
             nc.vector.tensor_tensor(w_row[:, cols], dal_spread[:], alpha[:, cols], MULT)
-        weigh_and_put_last(HALF, C, "dal_cols1")
-        nc.sync.dma_start(out_0[3 * P :, :], places[0][:])
+        de.append(held([P, C], F32, "de3", "prod3"))
+        weigh(3, *FIRST_AND_REST[1])
+        for lo, hi in THIRDS:
+            put(scalar_move, 3, places[0], lo, hi)
 
-        by_bag = held([P, C], F32, "by_bag", "de2")
-        for h, (lo, hi) in enumerate(halves):
-            scalar_move(by_bag[:, lo:hi], w_row[:].indirect(entries(slot_list, lo, hi)))
+        by_bag = held([P, C], F32, "by_bag")
+        for lo, hi in halves:
+            nc.vector.tensor_copy(by_bag[:, lo:hi], w_row[:].indirect(entries(slot_list, lo, hi)))
+        for lo, hi in halves:
             slots = by_bag[:, lo:hi].rearrange("p (x j) -> p x j", j=2)
-            nc.gpsimd.tensor_tensor(bag_sum[:, lo // 2 : hi // 2], slots[:, :, 0], slots[:, :, 1], ADD)
+            nc.vector.tensor_tensor(bag_sum[:, lo // 2 : hi // 2], slots[:, :, 0], slots[:, :, 1], ADD)
 
-        looked = held([P, C], F32, "looked")
         taken = held([P, C], F32, "taken")
         result = held([P, C], F32, "result")
         for lo, hi in halves:
-            scalar_move(looked[:, lo:hi], bag_sum[:].indirect(entries(bag_list, lo, hi)))
+            nc.vector.tensor_tensor(taken[:, lo:hi], bag_sum[:].indirect(entries(bag_list, lo, hi)), alpha[:, lo:hi], MULT)
         for lo, hi in halves:
-            nc.vector.tensor_tensor(taken[0:1, lo:hi], looked[0:1, lo:hi], alpha[0:1, lo:hi], MULT)
             nc.vector.tensor_tensor(result[0:1, lo:hi], w_row[0:1, lo:hi], taken[0:1, lo:hi], SUBTRACT)
-        nc.scalar.dma_start(out_1, result[0:1, :])
+        nc.sync.dma_start(out_1, result[0:1, :])

@@ -23,6 +23,9 @@ M, D, C, T, X = 512, 512, 1024, 2048, 512
 BLOCKS = D // P
 BANK = 512
 HALF = C // 2
+QUARTERS = 4
+SHARE = 320
+QUARTER = C // QUARTERS
 BAG_WINDOW = X + 16
 ALIGN = 256
 CAST_SPLIT = 128
@@ -74,11 +77,10 @@ def tile_attend_gmil_kernel(tc, eT, W, dz, al, offs, bagoffs, slotoffs, out_0, o
         nc.sync.dma_start(dz_raw[1][:], dz_rows[:, :, 2 * P :])
         nc.sync.dma_start(w_raw[1][:], w_rows[:, :, 2 * P :])
         nc.sync.dma_start(bag_list[:], bagoffs)
+        nc.sync.dma_start(alpha[:], al)
         nc.sync.dma_start(idx_list[:], offs)
         for b in range(BLOCKS):
             nc.sync.dma_start(emb[b][:], eT[b * P : (b + 1) * P, :])
-            if b == 0:
-                nc.sync.dma_start(alpha[:], al)
         nc.sync.dma_start(slot_list[:], slotoffs)
 
         identity = held([P, P], F32, "identity")
@@ -98,9 +100,10 @@ def tile_attend_gmil_kernel(tc, eT, W, dz, al, offs, bagoffs, slotoffs, out_0, o
         w_codes = held([P, D], U32, "w_codes")
         w_scales = held([P, D], U8, "w_scales")
 
-        def quantize(codes, scales, fmt, grouped, raw, h):
-            interleave(nc.vector.tensor_copy, grouped, raw, 0, CAST_SPLIT)
-            interleave(nc.scalar.copy, grouped, raw, CAST_SPLIT, 2 * P)
+        def quantize(codes, scales, fmt, grouped, raw, h, split=CAST_SPLIT):
+            interleave(nc.vector.tensor_copy, grouped, raw, 0, split)
+            if split < 2 * P:
+                interleave(nc.scalar.copy, grouped, raw, split, 2 * P)
             cols = slice(2 * h * P, 2 * (h + 1) * P)
             nc.vector.quantize_mx(
                 out=codes[:, cols].bitcast(fmt), scales=scales[:, cols], in_=grouped[:].rearrange("p c t -> p (c t)")
@@ -127,19 +130,21 @@ def tile_attend_gmil_kernel(tc, eT, W, dz, al, offs, bagoffs, slotoffs, out_0, o
         product(1, 0, X // 2, 1, nc.scalar.copy)
         product(0, X // 2, X, 2, nc.vector.tensor_copy)
         product(1, X // 2, X, 3, nc.scalar.copy)
-        quantize(w_codes, w_scales, E4M3X4, w16[1], w_raw[1], 1)
+        quantize(w_codes, w_scales, E4M3X4, w16[1], w_raw[1], 1, 2 * P)
 
-        turned = [bank(6 + h, f"turned{h}") for h in range(2)]
+        turned = [bank(q, f"turned{q}") for q in range(QUARTERS)]
         ub = [held([P, C], F32, f"ub{b}") for b in range(BLOCKS)]
         et = [held([P, C], F32, f"et{b}") for b in range(BLOCKS)]
         de = [held([P, C], F32, f"de{b}") for b in range(BLOCKS - 1)]
 
-        def look_up_u(move, b, h):
-            lo, hi = h * HALF, (h + 1) * HALF
+        def look_up_u(move, b, h, lo=None, hi=None):
+            if h is not None:
+                lo, hi = h * HALF, (h + 1) * HALF
             move(ub[b][:, lo:hi], u[b][:].indirect(entries(bag_list, lo, hi)))
 
-        def look_up_emb(b):
-            nc.vector.tensor_copy(et[b][:], emb[b][:].indirect(idx_list[:]))
+        def look_up_emb(b, pieces):
+            for lo, hi in pieces:
+                nc.vector.tensor_copy(et[b][:, lo:hi], emb[b][:].indirect(entries(idx_list, lo, hi)))
 
         def weigh(b, lo, hi):
             nc.gpsimd.tensor_tensor(de[b][:, lo:hi], ub[b][:, lo:hi], alpha[:, lo:hi], MULT)
@@ -149,81 +154,84 @@ def tile_attend_gmil_kernel(tc, eT, W, dz, al, offs, bagoffs, slotoffs, out_0, o
             for lo, hi in pieces:
                 engine.tensor_tensor(prod[:, lo:hi], ub[b][:, lo:hi], et[b][:, lo:hi], MULT)
                 for first in range(lo, hi, P):
-                    col = first % HALF
+                    col = first % QUARTER
                     nc.tensor.matmul(
-                        turned[first // HALF][:, col : col + P],
+                        turned[first // QUARTER][:, col : col + P],
                         prod[:, first : first + P],
                         identity[:],
                         start=(b == 0 and col == 0),
-                        stop=(b == BLOCKS - 1 and col == HALF - P),
+                        stop=(b == BLOCKS - 1 and col == QUARTER - P),
                         is_transpose=True,
                     )
 
-        early = []
-
         def put(move, b, window, lo, hi):
-            source = early[0][:] if (b, lo) == (BLOCKS - 1, 0) else de[b][:, lo:hi]
-            move(window[:].indirect(entries(idx_list, lo, hi)), source)
+            move(window[:].indirect(entries(idx_list, lo, hi)), de[b][:, lo:hi])
             if hi == C:
                 nc.sync.dma_start(out_0[b * P : (b + 1) * P, :], window[:])
 
         whole = ((0, C),)
         halves = ((0, HALF), (HALF, C))
+        quarters = tuple((q * QUARTER, (q + 1) * QUARTER) for q in range(QUARTERS))
         look_up_u(scalar_move, 0, 0)
         look_up_u(nc.vector.tensor_copy, 0, 1)
         product(2, 0, X, 4, nc.scalar.copy)
         product(3, 0, X, 5, nc.scalar.copy)
         places.append(held([P, T], F32, "places2", "w16_1"))
         nc.gpsimd.memset(places[2][:], 0.0)
-        look_up_u(nc.vector.tensor_copy, 1, 0)
+        look_up_u(scalar_move, 1, None, 0, SHARE)
+        look_up_u(nc.vector.tensor_copy, 1, None, SHARE, HALF)
         look_up_u(nc.vector.tensor_copy, 1, 1)
         for b in range(2, BLOCKS):
             for h in range(2):
                 look_up_u(scalar_move, b, h)
-        look_up_emb(0)
+        look_up_emb(0, whole)
         for lo, hi in FIRST_AND_REST:
             weigh(0, lo, hi)
             put(nc.vector.tensor_copy, 0, places[0], lo, hi)
         for b in range(1, BLOCKS):
-            look_up_emb(b)
+            look_up_emb(b, halves if b == 2 else whole)
         for b in (1, 2):
             weigh(b, 0, C)
         for lo, hi in THIRDS:
             for b in (1, 2):
                 put(scalar_move, b, places[b], lo, hi)
-        early.append(held([P, THIRDS[0][1]], F32, "early"))
-        nc.gpsimd.tensor_tensor(early[0][:], ub[3][:, : THIRDS[0][1]], alpha[:, : THIRDS[0][1]], MULT)
         for b in range(BLOCKS - 1):
-            multiply(b, nc.gpsimd, whole)
-        multiply(3, nc.vector, halves)
+            multiply(b, nc.gpsimd, halves if b == 2 else whole)
+        multiply(3, nc.vector, quarters)
+        early = held([P, QUARTER], F32, "early", "emb3")
+        nc.vector.tensor_tensor(early[:], ub[3][:, :QUARTER], alpha[:, :QUARTER], MULT)
+        scalar_move(places[0][:].indirect(entries(idx_list, 0, QUARTER)), early[:])
 
-        dal_cols = [held([P, 4], F32, f"dal_cols{h}") for h in range(2)]
+        dal_cols = [held([P, 2], F32, f"dal_cols{q}") for q in range(QUARTERS)]
         w_row = held([P, C], F32, "w_row")
-        for h in range(2):
-            nc.vector.tensor_reduce(dal_cols[h][:], turned[h][:].rearrange("p (q d) -> p q d", d=P), AXIS_X, ADD)
-        for h in range(2):
-            dal_spread = bank(h, f"dal_spread{h}")
-            for q in range(4):
-                column = dal_cols[h][:, q : q + 1]
-                nc.tensor.transpose(dal_spread[:, q * P : (q + 1) * P], column.to_broadcast([P, P]), identity[:])
-            cols = slice(h * HALF, (h + 1) * HALF)
-            nc.vector.tensor_tensor(w_row[:, cols], dal_spread[:], alpha[:, cols], MULT)
+        for q in range(QUARTERS):
+            sums = turned[q][:, :QUARTER].rearrange("p (k d) -> p k d", d=P)
+            nc.vector.tensor_reduce(dal_cols[q][:], sums, AXIS_X, ADD)
+        for q, (lo, hi) in enumerate(quarters):
+            dal_spread = bank(QUARTERS + q, f"dal_spread{q}")
+            for k in range(2):
+                column = dal_cols[q][:, k : k + 1]
+                nc.tensor.transpose(dal_spread[:, k * P : (k + 1) * P], column.to_broadcast([P, P]), identity[:])
+            nc.vector.tensor_tensor(w_row[:, lo:hi], dal_spread[:, :QUARTER], alpha[:, lo:hi], MULT)
         de.append(held([P, C], F32, "de3", "prod3"))
-        weigh(3, *FIRST_AND_REST[1])
-        for lo, hi in THIRDS:
+        for lo, hi in ((QUARTER, 640), (640, C)):
+            weigh(3, lo, hi)
             put(scalar_move, 3, places[0], lo, hi)
 
         by_bag = held([P, C], F32, "by_bag")
         for lo, hi in halves:
             nc.vector.tensor_copy(by_bag[:, lo:hi], w_row[:].indirect(entries(slot_list, lo, hi)))
-        for lo, hi in halves:
+        for engine, (lo, hi) in zip((nc.gpsimd, nc.vector), halves):
             slots = by_bag[:, lo:hi].rearrange("p (x j) -> p x j", j=2)
-            nc.vector.tensor_tensor(bag_sum[:, lo // 2 : hi // 2], slots[:, :, 0], slots[:, :, 1], ADD)
+            engine.tensor_tensor(bag_sum[:, lo // 2 : hi // 2], slots[:, :, 0], slots[:, :, 1], ADD)
 
+        looked = held([P, C], F32, "looked")
         taken = held([P, C], F32, "taken")
         result = held([P, C], F32, "result")
         for lo, hi in halves:
-            nc.vector.tensor_tensor(taken[:, lo:hi], bag_sum[:].indirect(entries(bag_list, lo, hi)), alpha[:, lo:hi], MULT)
+            nc.vector.tensor_copy(looked[:, lo:hi], bag_sum[:].indirect(entries(bag_list, lo, hi)))
+        for engine, (lo, hi) in zip((nc.gpsimd, nc.vector), halves):
+            engine.tensor_tensor(taken[0:1, lo:hi], looked[0:1, lo:hi], alpha[0:1, lo:hi], MULT)
         for lo, hi in halves:
             nc.vector.tensor_tensor(result[0:1, lo:hi], w_row[0:1, lo:hi], taken[0:1, lo:hi], SUBTRACT)
         nc.sync.dma_start(out_1, result[0:1, :])

@@ -24,7 +24,6 @@ BLOCKS = D // P
 BANK = 512
 HALF = C // 2
 QUARTERS = 4
-SHARE = 320
 QUARTER = C // QUARTERS
 BAG_WINDOW = X + 16
 ALIGN = 256
@@ -137,9 +136,8 @@ def tile_attend_gmil_kernel(tc, eT, W, dz, al, offs, bagoffs, slotoffs, out_0, o
         et = [held([P, C], F32, f"et{b}") for b in range(BLOCKS)]
         de = [held([P, C], F32, f"de{b}") for b in range(BLOCKS - 1)]
 
-        def look_up_u(move, b, h, lo=None, hi=None):
-            if h is not None:
-                lo, hi = h * HALF, (h + 1) * HALF
+        def look_up_u(move, b, h):
+            lo, hi = h * HALF, (h + 1) * HALF
             move(ub[b][:, lo:hi], u[b][:].indirect(entries(bag_list, lo, hi)))
 
         def look_up_emb(b, pieces):
@@ -178,8 +176,7 @@ def tile_attend_gmil_kernel(tc, eT, W, dz, al, offs, bagoffs, slotoffs, out_0, o
         product(3, 0, X, 5, nc.scalar.copy)
         places.append(held([P, T], F32, "places2", "w16_1"))
         nc.gpsimd.memset(places[2][:], 0.0)
-        look_up_u(scalar_move, 1, None, 0, SHARE)
-        look_up_u(nc.vector.tensor_copy, 1, None, SHARE, HALF)
+        look_up_u(nc.vector.tensor_copy, 1, 0)
         look_up_u(nc.vector.tensor_copy, 1, 1)
         for b in range(2, BLOCKS):
             for h in range(2):
@@ -195,12 +192,13 @@ def tile_attend_gmil_kernel(tc, eT, W, dz, al, offs, bagoffs, slotoffs, out_0, o
         for lo, hi in THIRDS:
             for b in (1, 2):
                 put(scalar_move, b, places[b], lo, hi)
+        lo, hi = THIRDS[0]
+        early = held([P, hi], F32, "early")
+        nc.gpsimd.tensor_tensor(early[:], ub[3][:, :hi], alpha[:, :hi], MULT)
+        scalar_move(places[0][:].indirect(entries(idx_list, lo, hi)), early[:])
         for b in range(BLOCKS - 1):
             multiply(b, nc.gpsimd, halves if b == 2 else whole)
         multiply(3, nc.vector, quarters)
-        early = held([P, QUARTER], F32, "early", "emb3")
-        nc.vector.tensor_tensor(early[:], ub[3][:, :QUARTER], alpha[:, :QUARTER], MULT)
-        scalar_move(places[0][:].indirect(entries(idx_list, 0, QUARTER)), early[:])
 
         dal_cols = [held([P, 2], F32, f"dal_cols{q}") for q in range(QUARTERS)]
         w_row = held([P, C], F32, "w_row")
@@ -214,7 +212,7 @@ def tile_attend_gmil_kernel(tc, eT, W, dz, al, offs, bagoffs, slotoffs, out_0, o
                 nc.tensor.transpose(dal_spread[:, k * P : (k + 1) * P], column.to_broadcast([P, P]), identity[:])
             nc.vector.tensor_tensor(w_row[:, lo:hi], dal_spread[:, :QUARTER], alpha[:, lo:hi], MULT)
         de.append(held([P, C], F32, "de3", "prod3"))
-        for lo, hi in ((QUARTER, 640), (640, C)):
+        for lo, hi in THIRDS[1:]:
             weigh(3, lo, hi)
             put(scalar_move, 3, places[0], lo, hi)
 

@@ -24,6 +24,7 @@ BLOCKS = D // P
 BANK = 512
 HALF = C // 2
 QUARTERS = 4
+SHARE = 384
 QUARTER = C // QUARTERS
 BAG_WINDOW = X + 16
 ALIGN = 256
@@ -136,8 +137,9 @@ def tile_attend_gmil_kernel(tc, eT, W, dz, al, offs, bagoffs, slotoffs, out_0, o
         et = [held([P, C], F32, f"et{b}") for b in range(BLOCKS)]
         de = [held([P, C], F32, f"de{b}") for b in range(BLOCKS - 1)]
 
-        def look_up_u(move, b, h):
-            lo, hi = h * HALF, (h + 1) * HALF
+        def look_up_u(move, b, h, lo=None, hi=None):
+            if h is not None:
+                lo, hi = h * HALF, (h + 1) * HALF
             move(ub[b][:, lo:hi], u[b][:].indirect(entries(bag_list, lo, hi)))
 
         def look_up_emb(b, pieces):
@@ -176,7 +178,8 @@ def tile_attend_gmil_kernel(tc, eT, W, dz, al, offs, bagoffs, slotoffs, out_0, o
         product(3, 0, X, 5, nc.scalar.copy)
         places.append(held([P, T], F32, "places2", "w16_1"))
         nc.gpsimd.memset(places[2][:], 0.0)
-        look_up_u(nc.vector.tensor_copy, 1, 0)
+        look_up_u(scalar_move, 1, None, 0, SHARE)
+        look_up_u(nc.vector.tensor_copy, 1, None, SHARE, HALF)
         look_up_u(nc.vector.tensor_copy, 1, 1)
         for b in range(2, BLOCKS):
             for h in range(2):
@@ -223,13 +226,10 @@ def tile_attend_gmil_kernel(tc, eT, W, dz, al, offs, bagoffs, slotoffs, out_0, o
             slots = by_bag[:, lo:hi].rearrange("p (x j) -> p x j", j=2)
             engine.tensor_tensor(bag_sum[:, lo // 2 : hi // 2], slots[:, :, 0], slots[:, :, 1], ADD)
 
-        looked = held([P, C], F32, "looked")
         taken = held([P, C], F32, "taken")
         result = held([P, C], F32, "result")
         for lo, hi in halves:
-            nc.vector.tensor_copy(looked[:, lo:hi], bag_sum[:].indirect(entries(bag_list, lo, hi)))
-        for engine, (lo, hi) in zip((nc.gpsimd, nc.vector), halves):
-            engine.tensor_tensor(taken[0:1, lo:hi], looked[0:1, lo:hi], alpha[0:1, lo:hi], MULT)
+            nc.vector.tensor_tensor(taken[:, lo:hi], bag_sum[:].indirect(entries(bag_list, lo, hi)), alpha[:, lo:hi], MULT)
         for lo, hi in halves:
             nc.vector.tensor_tensor(result[0:1, lo:hi], w_row[0:1, lo:hi], taken[0:1, lo:hi], SUBTRACT)
         nc.sync.dma_start(out_1, result[0:1, :])

@@ -6,7 +6,6 @@ from concourse.masks import make_identity
 F32 = mybir.dt.float32
 BF16 = mybir.dt.bfloat16
 U32 = mybir.dt.uint32
-I32 = mybir.dt.int32
 U16 = mybir.dt.uint16
 U8 = mybir.dt.uint8
 E4M3X4 = mybir.dt.float8_e4m3fn_x4
@@ -24,9 +23,9 @@ BLOCKS = D // P
 BANK = 512
 HALF = C // 2
 QUARTERS = 4
-SHARE = 384
+SHARE = 256
 QUARTER = C // QUARTERS
-BAG_WINDOW = X + 16
+BAG_WINDOW = X + 17
 ALIGN = 256
 CAST_SPLIT = 128
 THIRDS = ((0, 384), (384, 768), (768, 1024))
@@ -90,7 +89,8 @@ def tile_attend_gmil_kernel(tc, eT, W, dz, al, offs, bagoffs, slotoffs, out_0, o
         for padded in u + [bag_sum]:
             nc.vector.memset(padded[:, X:], 0.0)
         places = [held([P, T], F32, f"places{i}") for i in range(2)]
-        nc.vector.memset(places[0][:].bitcast(I32), 0)
+        nc.vector.memset(places[0][:, : T // 2 - 1], 0.0)
+        nc.vector.memset(places[0][:, T // 2 - 1 :], 0.0)
         nc.gpsimd.memset(places[1][:], 0.0)
 
         dz16 = [held([P, 2 * P, PACK], BF16, f"dz16_{h}") for h in range(2)]

@@ -23,13 +23,12 @@ BLOCKS = D // P
 BANK = 512
 HALF = C // 2
 QUARTERS = 4
-SHARE = 256
+SHARE = 128
 QUARTER = C // QUARTERS
 BAG_WINDOW = X + 17
 ALIGN = 256
-CAST_SPLIT = 128
+CAST_SPLIT = 160
 THIRDS = ((0, 384), (384, 768), (768, 1024))
-FIRST_AND_REST = ((0, 384), (384, 1024))
 
 FLOPS = 2 * M * D * X
 
@@ -93,14 +92,13 @@ def tile_attend_gmil_kernel(tc, eT, W, dz, al, offs, bagoffs, slotoffs, out_0, o
         nc.vector.memset(places[0][:, T // 2 - 1 :], 0.0)
         nc.gpsimd.memset(places[1][:], 0.0)
 
-        dz16 = [held([P, 2 * P, PACK], BF16, f"dz16_{h}") for h in range(2)]
-        w16 = [held([P, 2 * P, PACK], BF16, f"w16_{h}") for h in range(2)]
         dz_codes = held([P, X], U32, "dz_codes")
         dz_scales = held([P, X], U8, "dz_scales")
         w_codes = held([P, D], U32, "w_codes")
         w_scales = held([P, D], U8, "w_scales")
 
-        def quantize(codes, scales, fmt, grouped, raw, h, split=CAST_SPLIT):
+        def quantize(codes, scales, fmt, name, tag, raw, h, split=CAST_SPLIT):
+            grouped = held([P, 2 * P, PACK], BF16, name, tag)
             interleave(nc.vector.tensor_copy, grouped, raw, 0, split)
             if split < 2 * P:
                 interleave(nc.scalar.copy, grouped, raw, split, 2 * P)
@@ -123,14 +121,14 @@ def tile_attend_gmil_kernel(tc, eT, W, dz, al, offs, bagoffs, slotoffs, out_0, o
             )
             copy_out(u[b][:, lo:hi], acc[:, : hi - lo])
 
-        quantize(w_codes, w_scales, E4M3X4, w16[0], w_raw[0], 0)
-        quantize(dz_codes, dz_scales, E5M2X4, dz16[0], dz_raw[0], 0)
-        quantize(dz_codes, dz_scales, E5M2X4, dz16[1], dz_raw[1], 1)
+        quantize(w_codes, w_scales, E4M3X4, "w16_0", None, w_raw[0], 0)
+        quantize(dz_codes, dz_scales, E5M2X4, "dz16_0", "w_raw0", dz_raw[0], 0)
+        quantize(dz_codes, dz_scales, E5M2X4, "dz16_1", "dz_raw0", dz_raw[1], 1)
         product(0, 0, X // 2, 0, nc.scalar.copy)
         product(1, 0, X // 2, 1, nc.scalar.copy)
-        product(0, X // 2, X, 2, nc.vector.tensor_copy)
+        product(0, X // 2, X, 2, nc.scalar.copy)
         product(1, X // 2, X, 3, nc.scalar.copy)
-        quantize(w_codes, w_scales, E4M3X4, w16[1], w_raw[1], 1, 2 * P)
+        quantize(w_codes, w_scales, E4M3X4, "w16_1", "dz_raw1", w_raw[1], 1, 2 * P)
 
         turned = [bank(q, f"turned{q}") for q in range(QUARTERS)]
         ub = [held([P, C], F32, f"ub{b}") for b in range(BLOCKS)]
@@ -176,7 +174,7 @@ def tile_attend_gmil_kernel(tc, eT, W, dz, al, offs, bagoffs, slotoffs, out_0, o
         look_up_u(nc.vector.tensor_copy, 0, 1)
         product(2, 0, X, 4, nc.scalar.copy)
         product(3, 0, X, 5, nc.scalar.copy)
-        places.append(held([P, T], F32, "places2", "w16_1"))
+        places.append(held([P, T], F32, "places2", "dz_raw1"))
         nc.gpsimd.memset(places[2][:], 0.0)
         look_up_u(scalar_move, 1, None, 0, SHARE)
         look_up_u(nc.vector.tensor_copy, 1, None, SHARE, HALF)
@@ -185,9 +183,8 @@ def tile_attend_gmil_kernel(tc, eT, W, dz, al, offs, bagoffs, slotoffs, out_0, o
             for h in range(2):
                 look_up_u(scalar_move, b, h)
         look_up_emb(0, whole)
-        for lo, hi in FIRST_AND_REST:
-            weigh(0, lo, hi)
-            put(nc.vector.tensor_copy, 0, places[0], lo, hi)
+        weigh(0, 0, C)
+        put(nc.vector.tensor_copy, 0, places[0], 0, C)
         for b in range(1, BLOCKS):
             look_up_emb(b, halves if b == 2 else whole)
         for b in (1, 2):

@@ -23,7 +23,7 @@ BLOCKS = D // P
 BANK = 512
 HALF = C // 2
 QUARTERS = 4
-SHARE = 128
+SHARE = 256
 QUARTER = C // QUARTERS
 BAG_WINDOW = X + 17
 ALIGN = 256
@@ -67,7 +67,8 @@ def tile_attend_gmil_kernel(tc, eT, W, dz, al, offs, bagoffs, slotoffs, out_0, o
         idx_list = lists.tile([P, C // 16], U16, name="idx_list", align_bytes=ALIGN)
         bag_list = lists.tile([P, C // 16], U16, name="bag_list", align_bytes=ALIGN)
         slot_list = lists.tile([P, C // 16], U16, name="slot_list", align_bytes=ALIGN)
-        emb = [held([P, T], F32, f"emb{b}") for b in range(BLOCKS)]
+        emb_pair = held([P, 2, T], F32, "emb_pair")
+        emb = [held([P, T], F32, "emb0")[:], emb_pair[:, 0, :], emb_pair[:, 1, :], held([P, T], F32, "emb3")[:]]
         alpha = held([P, C], F32, "alpha")
 
         nc.sync.dma_start(w_raw[0][:], w_rows[:, :, : 2 * P])
@@ -77,8 +78,9 @@ def tile_attend_gmil_kernel(tc, eT, W, dz, al, offs, bagoffs, slotoffs, out_0, o
         nc.sync.dma_start(bag_list[:], bagoffs)
         nc.sync.dma_start(alpha[:], al)
         nc.sync.dma_start(idx_list[:], offs)
-        for b in range(BLOCKS):
-            nc.sync.dma_start(emb[b][:], eT[b * P : (b + 1) * P, :])
+        nc.sync.dma_start(emb[0], eT[:P, :])
+        nc.sync.dma_start(emb_pair[:], eT[P : 3 * P, :].rearrange("(b p) t -> p b t", p=P))
+        nc.sync.dma_start(emb[3], eT[3 * P :, :])
         nc.sync.dma_start(slot_list[:], slotoffs)
 
         identity = held([P, P], F32, "identity")
@@ -87,10 +89,13 @@ def tile_attend_gmil_kernel(tc, eT, W, dz, al, offs, bagoffs, slotoffs, out_0, o
         bag_sum = held([P, BAG_WINDOW], F32, "bag_sum")
         for padded in u + [bag_sum]:
             nc.vector.memset(padded[:, X:], 0.0)
-        places = [held([P, T], F32, f"places{i}") for i in range(2)]
+        places = [held([P, T], F32, f"places{i}") for i in range(3)]
         nc.vector.memset(places[0][:, : T // 2 - 1], 0.0)
         nc.vector.memset(places[0][:, T // 2 - 1 :], 0.0)
+        nc.vector.memset(places[2][:, : T // 4 - 1], 0.0)
+        nc.vector.memset(places[2][:, T // 4 - 1 : T // 2], 0.0)
         nc.gpsimd.memset(places[1][:], 0.0)
+        nc.gpsimd.memset(places[2][:, T // 2 :], 0.0)
 
         dz_codes = held([P, X], U32, "dz_codes")
         dz_scales = held([P, X], U8, "dz_scales")
@@ -99,7 +104,8 @@ def tile_attend_gmil_kernel(tc, eT, W, dz, al, offs, bagoffs, slotoffs, out_0, o
 
         def quantize(codes, scales, fmt, name, tag, raw, h, split=CAST_SPLIT):
             grouped = held([P, 2 * P, PACK], BF16, name, tag)
-            interleave(nc.vector.tensor_copy, grouped, raw, 0, split)
+            if split > 0:
+                interleave(nc.vector.tensor_copy, grouped, raw, 0, split)
             if split < 2 * P:
                 interleave(nc.scalar.copy, grouped, raw, split, 2 * P)
             cols = slice(2 * h * P, 2 * (h + 1) * P)
@@ -121,8 +127,8 @@ def tile_attend_gmil_kernel(tc, eT, W, dz, al, offs, bagoffs, slotoffs, out_0, o
             )
             copy_out(u[b][:, lo:hi], acc[:, : hi - lo])
 
-        quantize(w_codes, w_scales, E4M3X4, "w16_0", None, w_raw[0], 0)
-        quantize(dz_codes, dz_scales, E5M2X4, "dz16_0", "w_raw0", dz_raw[0], 0)
+        quantize(w_codes, w_scales, E4M3X4, "w16_0", None, w_raw[0], 0, 0)
+        quantize(dz_codes, dz_scales, E5M2X4, "dz16_0", None, dz_raw[0], 0)
         quantize(dz_codes, dz_scales, E5M2X4, "dz16_1", "dz_raw0", dz_raw[1], 1)
         product(0, 0, X // 2, 0, nc.scalar.copy)
         product(1, 0, X // 2, 1, nc.scalar.copy)
@@ -131,26 +137,26 @@ def tile_attend_gmil_kernel(tc, eT, W, dz, al, offs, bagoffs, slotoffs, out_0, o
         quantize(w_codes, w_scales, E4M3X4, "w16_1", "dz_raw1", w_raw[1], 1, 2 * P)
 
         turned = [bank(q, f"turned{q}") for q in range(QUARTERS)]
-        ub = [held([P, C], F32, f"ub{b}") for b in range(BLOCKS)]
-        et = [held([P, C], F32, f"et{b}") for b in range(BLOCKS)]
-        de = [held([P, C], F32, f"de{b}") for b in range(BLOCKS - 1)]
+        ub = [held([P, C], F32, f"ub{b}") for b in range(BLOCKS - 1)]
+        de = {b: held([P, C], F32, f"de{b}") for b in (0, 1, 3)}
 
-        def look_up_u(move, b, h, lo=None, hi=None):
-            if h is not None:
-                lo, hi = h * HALF, (h + 1) * HALF
+        def look_up_u(move, b, lo, hi):
             move(ub[b][:, lo:hi], u[b][:].indirect(entries(bag_list, lo, hi)))
 
-        def look_up_emb(b, pieces):
-            for lo, hi in pieces:
-                nc.vector.tensor_copy(et[b][:, lo:hi], emb[b][:].indirect(entries(idx_list, lo, hi)))
+        def look_up_emb(move, b, lo, hi):
+            looked_up = held([P, hi - lo], F32, f"et{b}_{lo}")
+            move(looked_up[:], emb[b].indirect(entries(idx_list, lo, hi)))
+            return looked_up
+
+        prods = [held([P, C], F32, f"prod{b}") for b in range(BLOCKS)]
 
         def weigh(b, lo, hi):
             nc.gpsimd.tensor_tensor(de[b][:, lo:hi], ub[b][:, lo:hi], alpha[:, lo:hi], MULT)
 
-        def multiply(b, engine, pieces):
-            prod = held([P, C], F32, f"prod{b}", "u3" if b == 1 else None)
+        def multiply(b, engine, et, start, pieces):
+            prod = prods[b]
             for lo, hi in pieces:
-                engine.tensor_tensor(prod[:, lo:hi], ub[b][:, lo:hi], et[b][:, lo:hi], MULT)
+                engine.tensor_tensor(prod[:, lo:hi], ub[b][:, lo:hi], et[:, lo - start : hi - start], MULT)
                 for first in range(lo, hi, P):
                     col = first % QUARTER
                     nc.tensor.matmul(
@@ -162,43 +168,48 @@ def tile_attend_gmil_kernel(tc, eT, W, dz, al, offs, bagoffs, slotoffs, out_0, o
                         is_transpose=True,
                     )
 
-        def put(move, b, window, lo, hi):
-            move(window[:].indirect(entries(idx_list, lo, hi)), de[b][:, lo:hi])
-            if hi == C:
-                nc.sync.dma_start(out_0[b * P : (b + 1) * P, :], window[:])
+        def put(move, b, window, pieces):
+            for lo, hi in pieces:
+                move(window[:].indirect(entries(idx_list, lo, hi)), de[b][:, lo:hi])
+            nc.sync.dma_start(out_0[b * P : (b + 1) * P, :], window[:])
 
         whole = ((0, C),)
         halves = ((0, HALF), (HALF, C))
         quarters = tuple((q * QUARTER, (q + 1) * QUARTER) for q in range(QUARTERS))
-        look_up_u(scalar_move, 0, 0)
-        look_up_u(nc.vector.tensor_copy, 0, 1)
+        look_up_u(scalar_move, 0, 0, HALF)
+        look_up_u(nc.vector.tensor_copy, 0, HALF, C)
+        weigh(0, 0, C)
         product(2, 0, X, 4, nc.scalar.copy)
         product(3, 0, X, 5, nc.scalar.copy)
-        places.append(held([P, T], F32, "places2", "dz_raw1"))
-        nc.gpsimd.memset(places[2][:], 0.0)
-        look_up_u(scalar_move, 1, None, 0, SHARE)
-        look_up_u(nc.vector.tensor_copy, 1, None, SHARE, HALF)
-        look_up_u(nc.vector.tensor_copy, 1, 1)
-        for b in range(2, BLOCKS):
-            for h in range(2):
-                look_up_u(scalar_move, b, h)
-        look_up_emb(0, whole)
-        weigh(0, 0, C)
-        put(nc.vector.tensor_copy, 0, places[0], 0, C)
-        for b in range(1, BLOCKS):
-            look_up_emb(b, halves if b == 2 else whole)
-        for b in (1, 2):
-            weigh(b, 0, C)
-        for lo, hi in THIRDS:
-            for b in (1, 2):
-                put(scalar_move, b, places[b], lo, hi)
+        for lo, hi in halves:
+            look_up_u(nc.vector.tensor_copy, 1, lo, hi)
+        look_up_u(nc.vector.tensor_copy, 2, 0, SHARE)
+        look_up_u(scalar_move, 2, SHARE, HALF)
+        look_up_u(scalar_move, 2, HALF, C)
+        weigh(1, 0, C)
+        for b in range(2):
+            put(nc.vector.tensor_copy, b, places[b], whole)
+        multiply(0, nc.gpsimd, look_up_emb(scalar_move, 0, 0, C), 0, whole)
+        ub.append(held([P, C], F32, "ub3", "emb0"))
+        for lo, hi in halves:
+            look_up_u(scalar_move, 3, lo, hi)
+        weigh(3, *THIRDS[0])
+        early = look_up_emb(scalar_move, 1, 0, QUARTER)
+        late = look_up_emb(scalar_move, 1, QUARTER, C)
+        last = look_up_emb(scalar_move, 2, 0, C)
+        multiply(1, nc.gpsimd, early, 0, quarters[:1])
+        de[2] = held([P, C], F32, "de2", "et1_0")
+        weigh(2, *THIRDS[0])
+        weigh(2, THIRDS[0][1], C)
+        multiply(1, nc.gpsimd, late, QUARTER, ((QUARTER, C),))
+        multiply(2, nc.gpsimd, last, 0, whole)
+        put(scalar_move, 2, places[2], THIRDS)
+        multiply(3, nc.vector, look_up_emb(nc.vector.tensor_copy, 3, 0, C), 0, quarters)
         lo, hi = THIRDS[0]
-        early = held([P, hi], F32, "early")
-        nc.gpsimd.tensor_tensor(early[:], ub[3][:, :hi], alpha[:, :hi], MULT)
-        scalar_move(places[0][:].indirect(entries(idx_list, lo, hi)), early[:])
-        for b in range(BLOCKS - 1):
-            multiply(b, nc.gpsimd, halves if b == 2 else whole)
-        multiply(3, nc.vector, quarters)
+        scalar_move(places[0][:].indirect(entries(idx_list, lo, hi)), de[3][:, lo:hi])
+        de[3] = held([P, C], F32, "de3_rest", "prod3")
+        weigh(3, hi, C)
+        put(scalar_move, 3, places[0], THIRDS[1:])
 
         dal_cols = [held([P, 2], F32, f"dal_cols{q}") for q in range(QUARTERS)]
         w_row = held([P, C], F32, "w_row")
@@ -211,10 +222,6 @@ def tile_attend_gmil_kernel(tc, eT, W, dz, al, offs, bagoffs, slotoffs, out_0, o
                 column = dal_cols[q][:, k : k + 1]
                 nc.tensor.transpose(dal_spread[:, k * P : (k + 1) * P], column.to_broadcast([P, P]), identity[:])
             nc.vector.tensor_tensor(w_row[:, lo:hi], dal_spread[:, :QUARTER], alpha[:, lo:hi], MULT)
-        de.append(held([P, C], F32, "de3", "prod3"))
-        for lo, hi in THIRDS[1:]:
-            weigh(3, lo, hi)
-            put(scalar_move, 3, places[0], lo, hi)
 
         by_bag = held([P, C], F32, "by_bag")
         for lo, hi in halves:

@@ -24,11 +24,13 @@ BANK = 512
 HALF = C // 2
 QUARTERS = 4
 SHARE = 256
+HELP = 384
 QUARTER = C // QUARTERS
 BAG_WINDOW = X + 17
 ALIGN = 256
 CAST_SPLIT = 160
-THIRDS = ((0, 384), (384, 768), (768, 1024))
+THIRD = 384
+THIRDS = ((0, THIRD), (THIRD, 2 * THIRD), (2 * THIRD, C))
 
 FLOPS = 2 * M * D * X
 
@@ -45,6 +47,7 @@ def tile_attend_gmil_kernel(tc, eT, W, dz, al, offs, bagoffs, slotoffs, out_0, o
     with ExitStack() as ctx:
         lists = ctx.enter_context(tc.tile_pool(name="lists", bufs=1))
         keep = ctx.enter_context(tc.tile_pool(name="keep", bufs=1))
+        ring = ctx.enter_context(tc.tile_pool(name="ring", bufs=1))
         psum = ctx.enter_context(tc.psum_pool(name="psum", bufs=1))
 
         def held(shape, dtype, name, tag=None):
@@ -104,14 +107,18 @@ def tile_attend_gmil_kernel(tc, eT, W, dz, al, offs, bagoffs, slotoffs, out_0, o
 
         def quantize(codes, scales, fmt, name, tag, raw, h, split=CAST_SPLIT):
             grouped = held([P, 2 * P, PACK], BF16, name, tag)
-            if split > 0:
-                interleave(nc.vector.tensor_copy, grouped, raw, 0, split)
+            for lo, hi in ((0, min(split, P)), (P, split)):
+                if hi > lo:
+                    interleave(nc.vector.tensor_copy, grouped, raw, lo, hi)
             if split < 2 * P:
                 interleave(nc.scalar.copy, grouped, raw, split, 2 * P)
-            cols = slice(2 * h * P, 2 * (h + 1) * P)
-            nc.vector.quantize_mx(
-                out=codes[:, cols].bitcast(fmt), scales=scales[:, cols], in_=grouped[:].rearrange("p c t -> p (c t)")
-            )
+            for lo in (0, P):
+                cols = slice(2 * h * P + lo, 2 * h * P + lo + P)
+                nc.vector.quantize_mx(
+                    out=codes[:, cols].bitcast(fmt),
+                    scales=scales[:, cols],
+                    in_=grouped[:, lo : lo + P, :].rearrange("p c t -> p (c t)"),
+                )
 
         def product(b, lo, hi, i, copy_out):
             acc = bank(i, f"acc{b}_{lo}")
@@ -138,23 +145,19 @@ def tile_attend_gmil_kernel(tc, eT, W, dz, al, offs, bagoffs, slotoffs, out_0, o
 
         turned = [bank(q, f"turned{q}") for q in range(QUARTERS)]
         ub = [held([P, C], F32, f"ub{b}") for b in range(BLOCKS - 1)]
-        de = {b: held([P, C], F32, f"de{b}") for b in (0, 1, 3)}
 
         def look_up_u(move, b, lo, hi):
             move(ub[b][:, lo:hi], u[b][:].indirect(entries(bag_list, lo, hi)))
 
-        def look_up_emb(move, b, lo, hi):
-            looked_up = held([P, hi - lo], F32, f"et{b}_{lo}")
+        def look_up_emb(move, looked_up, b, lo, hi):
             move(looked_up[:], emb[b].indirect(entries(idx_list, lo, hi)))
             return looked_up
 
-        prods = [held([P, C], F32, f"prod{b}") for b in range(BLOCKS)]
+        def weigh(de, b, lo, hi):
+            nc.gpsimd.tensor_tensor(de[:], ub[b][:, lo:hi], alpha[:, lo:hi], MULT)
+            return de
 
-        def weigh(b, lo, hi):
-            nc.gpsimd.tensor_tensor(de[b][:, lo:hi], ub[b][:, lo:hi], alpha[:, lo:hi], MULT)
-
-        def multiply(b, engine, et, start, pieces):
-            prod = prods[b]
+        def multiply(engine, prod, b, et, start, pieces):
             for lo, hi in pieces:
                 engine.tensor_tensor(prod[:, lo:hi], ub[b][:, lo:hi], et[:, lo - start : hi - start], MULT)
                 for first in range(lo, hi, P):
@@ -168,17 +171,21 @@ def tile_attend_gmil_kernel(tc, eT, W, dz, al, offs, bagoffs, slotoffs, out_0, o
                         is_transpose=True,
                     )
 
-        def put(move, b, window, pieces):
+        def put(move, b, window, de, start, pieces):
             for lo, hi in pieces:
-                move(window[:].indirect(entries(idx_list, lo, hi)), de[b][:, lo:hi])
-            nc.sync.dma_start(out_0[b * P : (b + 1) * P, :], window[:])
+                move(window[:].indirect(entries(idx_list, lo, hi)), de[:, lo - start : hi - start])
+                if hi == C:
+                    nc.sync.dma_start(out_0[b * P : (b + 1) * P, :], window[:])
+
+        def reused(columns, name, offset):
+            return ring.tile([P, columns], F32, name=name, align_bytes=ALIGN, offset=offset)
 
         whole = ((0, C),)
         halves = ((0, HALF), (HALF, C))
         quarters = tuple((q * QUARTER, (q + 1) * QUARTER) for q in range(QUARTERS))
         look_up_u(scalar_move, 0, 0, HALF)
         look_up_u(nc.vector.tensor_copy, 0, HALF, C)
-        weigh(0, 0, C)
+        de0 = weigh(held([P, C], F32, "de0"), 0, 0, C)
         product(2, 0, X, 4, nc.scalar.copy)
         product(3, 0, X, 5, nc.scalar.copy)
         for lo, hi in halves:
@@ -186,30 +193,36 @@ def tile_attend_gmil_kernel(tc, eT, W, dz, al, offs, bagoffs, slotoffs, out_0, o
         look_up_u(nc.vector.tensor_copy, 2, 0, SHARE)
         look_up_u(scalar_move, 2, SHARE, HALF)
         look_up_u(scalar_move, 2, HALF, C)
-        weigh(1, 0, C)
-        for b in range(2):
-            put(nc.vector.tensor_copy, b, places[b], whole)
-        multiply(0, nc.gpsimd, look_up_emb(scalar_move, 0, 0, C), 0, whole)
-        ub.append(held([P, C], F32, "ub3", "emb0"))
+        de1 = weigh(held([P, C], F32, "de1"), 1, 0, C)
+        put(nc.vector.tensor_copy, 0, places[0], de0, 0, whole)
+        put(nc.vector.tensor_copy, 1, places[1], de1, 0, whole)
+
+        et0 = look_up_emb(scalar_move, held([P, C], F32, "et0"), 0, 0, C)
+        multiply(nc.gpsimd, held([P, C], F32, "prod0"), 0, et0, 0, whole)
+        et1_first = look_up_emb(scalar_move, held([P, THIRD], F32, "et1_first"), 1, 0, THIRD)
+        et1_rest = look_up_emb(scalar_move, reused(C - THIRD, "et1_rest", 4 * C - ALIGN), 1, THIRD, C)
+        et2 = look_up_emb(scalar_move, held([P, C], F32, "et2"), 2, 0, C)
+        prod1 = held([P, C], F32, "prod1")
+        multiply(nc.gpsimd, prod1, 1, et1_first, 0, THIRDS[:1])
+        de2_first = weigh(held([P, THIRD], F32, "de2_first", "et1_first"), 2, 0, THIRD)
+        multiply(nc.gpsimd, prod1, 1, et1_rest, THIRD, ((THIRD, C),))
+        put(scalar_move, 2, places[2], de2_first, 0, THIRDS[:1])
+        ub.append(reused(C, "ub3", 0))
         for lo, hi in halves:
             look_up_u(scalar_move, 3, lo, hi)
-        weigh(3, *THIRDS[0])
-        early = look_up_emb(scalar_move, 1, 0, QUARTER)
-        late = look_up_emb(scalar_move, 1, QUARTER, C)
-        last = look_up_emb(scalar_move, 2, 0, C)
-        multiply(1, nc.gpsimd, early, 0, quarters[:1])
-        de[2] = held([P, C], F32, "de2", "et1_0")
-        weigh(2, *THIRDS[0])
-        weigh(2, THIRDS[0][1], C)
-        multiply(1, nc.gpsimd, late, QUARTER, ((QUARTER, C),))
-        multiply(2, nc.gpsimd, last, 0, whole)
-        put(scalar_move, 2, places[2], THIRDS)
-        multiply(3, nc.vector, look_up_emb(nc.vector.tensor_copy, 3, 0, C), 0, quarters)
-        lo, hi = THIRDS[0]
-        scalar_move(places[0][:].indirect(entries(idx_list, lo, hi)), de[3][:, lo:hi])
-        de[3] = held([P, C], F32, "de3_rest", "prod3")
-        weigh(3, hi, C)
-        put(scalar_move, 3, places[0], THIRDS[1:])
+        de2_rest = weigh(reused(C - THIRD, "de2_rest", 4 * C), 2, THIRD, C)
+        multiply(nc.gpsimd, held([P, C], F32, "prod2", "prod1"), 2, et2, 0, whole)
+        put(scalar_move, 2, places[2], de2_rest, THIRD, THIRDS[1:])
+        de3_first = weigh(held([P, THIRD], F32, "de3_first"), 3, 0, THIRD)
+
+        et3_first = look_up_emb(nc.vector.tensor_copy, held([P, HELP], F32, "et3_first"), 3, 0, HELP)
+        et3_rest = look_up_emb(nc.vector.tensor_copy, held([P, C - HELP], F32, "et3_rest"), 3, HELP, C)
+        prod3 = held([P, C], F32, "prod3")
+        multiply(nc.gpsimd, prod3, 3, et3_first, 0, ((0, HELP),))
+        multiply(nc.vector, prod3, 3, et3_rest, HELP, ((HELP, HALF),) + quarters[2:])
+        put(scalar_move, 3, places[0], de3_first, 0, THIRDS[:1])
+        de3_rest = weigh(held([P, C - THIRD], F32, "de3_rest", "prod3"), 3, THIRD, C)
+        put(scalar_move, 3, places[0], de3_rest, THIRD, THIRDS[1:])
 
         dal_cols = [held([P, 2], F32, f"dal_cols{q}") for q in range(QUARTERS)]
         w_row = held([P, C], F32, "w_row")
@@ -224,9 +237,10 @@ def tile_attend_gmil_kernel(tc, eT, W, dz, al, offs, bagoffs, slotoffs, out_0, o
             nc.vector.tensor_tensor(w_row[:, lo:hi], dal_spread[:, :QUARTER], alpha[:, lo:hi], MULT)
 
         by_bag = held([P, C], F32, "by_bag")
-        for lo, hi in halves:
+        uneven = ((0, C - THIRD), (C - THIRD, C))
+        for lo, hi in uneven:
             nc.vector.tensor_copy(by_bag[:, lo:hi], w_row[:].indirect(entries(slot_list, lo, hi)))
-        for engine, (lo, hi) in zip((nc.gpsimd, nc.vector), halves):
+        for engine, (lo, hi) in zip((nc.gpsimd, nc.vector), uneven):
             slots = by_bag[:, lo:hi].rearrange("p (x j) -> p x j", j=2)
             engine.tensor_tensor(bag_sum[:, lo // 2 : hi // 2], slots[:, :, 0], slots[:, :, 1], ADD)
 

@@ -23,8 +23,7 @@ BLOCKS = D // P
 BANK = 512
 HALF = C // 2
 QUARTERS = 4
-SHARE = 256
-HELP = 384
+SHARE = 480
 QUARTER = C // QUARTERS
 BAG_WINDOW = X + 17
 ALIGN = 256
@@ -47,7 +46,6 @@ def tile_attend_gmil_kernel(tc, eT, W, dz, al, offs, bagoffs, slotoffs, out_0, o
     with ExitStack() as ctx:
         lists = ctx.enter_context(tc.tile_pool(name="lists", bufs=1))
         keep = ctx.enter_context(tc.tile_pool(name="keep", bufs=1))
-        ring = ctx.enter_context(tc.tile_pool(name="ring", bufs=1))
         psum = ctx.enter_context(tc.psum_pool(name="psum", bufs=1))
 
         def held(shape, dtype, name, tag=None):
@@ -71,7 +69,7 @@ def tile_attend_gmil_kernel(tc, eT, W, dz, al, offs, bagoffs, slotoffs, out_0, o
         bag_list = lists.tile([P, C // 16], U16, name="bag_list", align_bytes=ALIGN)
         slot_list = lists.tile([P, C // 16], U16, name="slot_list", align_bytes=ALIGN)
         emb_pair = held([P, 2, T], F32, "emb_pair")
-        emb = [held([P, T], F32, "emb0")[:], emb_pair[:, 0, :], emb_pair[:, 1, :], held([P, T], F32, "emb3")[:]]
+        emb = [held([P, T], F32, "emb0")[:], held([P, T], F32, "emb1")[:], emb_pair[:, 0, :], emb_pair[:, 1, :]]
         alpha = held([P, C], F32, "alpha")
 
         nc.sync.dma_start(w_raw[0][:], w_rows[:, :, : 2 * P])
@@ -81,9 +79,9 @@ def tile_attend_gmil_kernel(tc, eT, W, dz, al, offs, bagoffs, slotoffs, out_0, o
         nc.sync.dma_start(bag_list[:], bagoffs)
         nc.sync.dma_start(alpha[:], al)
         nc.sync.dma_start(idx_list[:], offs)
-        nc.sync.dma_start(emb[0], eT[:P, :])
-        nc.sync.dma_start(emb_pair[:], eT[P : 3 * P, :].rearrange("(b p) t -> p b t", p=P))
-        nc.sync.dma_start(emb[3], eT[3 * P :, :])
+        for b in (1, 0):
+            nc.sync.dma_start(emb[b], eT[b * P : (b + 1) * P, :])
+        nc.sync.dma_start(emb_pair[:], eT[2 * P :, :].rearrange("(b p) t -> p b t", p=P))
         nc.sync.dma_start(slot_list[:], slotoffs)
 
         identity = held([P, P], F32, "identity")
@@ -144,7 +142,7 @@ def tile_attend_gmil_kernel(tc, eT, W, dz, al, offs, bagoffs, slotoffs, out_0, o
         quantize(w_codes, w_scales, E4M3X4, "w16_1", "dz_raw1", w_raw[1], 1, 2 * P)
 
         turned = [bank(q, f"turned{q}") for q in range(QUARTERS)]
-        ub = [held([P, C], F32, f"ub{b}") for b in range(BLOCKS - 1)]
+        ub = [held([P, C], F32, f"ub{b}") for b in range(BLOCKS)]
 
         def look_up_u(move, b, lo, hi):
             move(ub[b][:, lo:hi], u[b][:].indirect(entries(bag_list, lo, hi)))
@@ -154,31 +152,32 @@ def tile_attend_gmil_kernel(tc, eT, W, dz, al, offs, bagoffs, slotoffs, out_0, o
             return looked_up
 
         def weigh(de, b, lo, hi):
-            nc.gpsimd.tensor_tensor(de[:], ub[b][:, lo:hi], alpha[:, lo:hi], MULT)
+            nc.gpsimd.tensor_tensor(de[:, :], ub[b][:, lo:hi], alpha[:, lo:hi], MULT)
             return de
+
+        opened = set()
 
         def multiply(engine, prod, b, et, start, pieces):
             for lo, hi in pieces:
-                engine.tensor_tensor(prod[:, lo:hi], ub[b][:, lo:hi], et[:, lo - start : hi - start], MULT)
+                shift = lo if prod.shape[1] < C else 0
+                engine.tensor_tensor(prod[:, lo - shift : hi - shift], ub[b][:, lo:hi], et[:, lo - start : hi - start], MULT)
                 for first in range(lo, hi, P):
                     col = first % QUARTER
                     nc.tensor.matmul(
                         turned[first // QUARTER][:, col : col + P],
-                        prod[:, first : first + P],
+                        prod[:, first - shift : first - shift + P],
                         identity[:],
-                        start=(b == 0 and col == 0),
+                        start=(first // QUARTER not in opened),
                         stop=(b == BLOCKS - 1 and col == QUARTER - P),
                         is_transpose=True,
                     )
+                    opened.add(first // QUARTER)
 
         def put(move, b, window, de, start, pieces):
             for lo, hi in pieces:
                 move(window[:].indirect(entries(idx_list, lo, hi)), de[:, lo - start : hi - start])
                 if hi == C:
                     nc.sync.dma_start(out_0[b * P : (b + 1) * P, :], window[:])
-
-        def reused(columns, name, offset):
-            return ring.tile([P, columns], F32, name=name, align_bytes=ALIGN, offset=offset)
 
         whole = ((0, C),)
         halves = ((0, HALF), (HALF, C))
@@ -190,38 +189,35 @@ def tile_attend_gmil_kernel(tc, eT, W, dz, al, offs, bagoffs, slotoffs, out_0, o
         product(3, 0, X, 5, nc.scalar.copy)
         for lo, hi in halves:
             look_up_u(nc.vector.tensor_copy, 1, lo, hi)
-        look_up_u(nc.vector.tensor_copy, 2, 0, SHARE)
-        look_up_u(scalar_move, 2, SHARE, HALF)
-        look_up_u(scalar_move, 2, HALF, C)
+        look_up_u(scalar_move, 2, 0, THIRD)
+        de2_first = weigh(held([P, THIRD], F32, "de2_first"), 2, 0, THIRD)
+        look_up_u(scalar_move, 2, THIRD, C - SHARE)
+        look_up_u(nc.vector.tensor_copy, 2, C - SHARE, C)
+        for lo, hi in halves:
+            look_up_u(scalar_move, 3, lo, hi)
+        et1 = look_up_emb(nc.vector.tensor_copy, held([P, C], F32, "et1"), 1, 0, C)
         de1 = weigh(held([P, C], F32, "de1"), 1, 0, C)
+        de3_first = weigh(held([P, THIRD], F32, "de3_first"), 3, 0, THIRD)
+        put(scalar_move, 2, places[2], de2_first, 0, THIRDS[:1])
         put(nc.vector.tensor_copy, 0, places[0], de0, 0, whole)
         put(nc.vector.tensor_copy, 1, places[1], de1, 0, whole)
+        multiply(nc.gpsimd, held([P, C], F32, "prod1"), 1, et1, 0, whole)
+        de2_last = weigh(held([P, C - 2 * THIRD], F32, "de2_last"), 2, *THIRDS[2])
 
         et0 = look_up_emb(scalar_move, held([P, C], F32, "et0"), 0, 0, C)
         multiply(nc.gpsimd, held([P, C], F32, "prod0"), 0, et0, 0, whole)
-        et1_first = look_up_emb(scalar_move, held([P, THIRD], F32, "et1_first"), 1, 0, THIRD)
-        et1_rest = look_up_emb(scalar_move, reused(C - THIRD, "et1_rest", 4 * C - ALIGN), 1, THIRD, C)
-        et2 = look_up_emb(scalar_move, held([P, C], F32, "et2"), 2, 0, C)
-        prod1 = held([P, C], F32, "prod1")
-        multiply(nc.gpsimd, prod1, 1, et1_first, 0, THIRDS[:1])
-        de2_first = weigh(held([P, THIRD], F32, "de2_first", "et1_first"), 2, 0, THIRD)
-        multiply(nc.gpsimd, prod1, 1, et1_rest, THIRD, ((THIRD, C),))
-        put(scalar_move, 2, places[2], de2_first, 0, THIRDS[:1])
-        ub.append(reused(C, "ub3", 0))
-        for lo, hi in halves:
-            look_up_u(scalar_move, 3, lo, hi)
-        de2_rest = weigh(reused(C - THIRD, "de2_rest", 4 * C), 2, THIRD, C)
-        multiply(nc.gpsimd, held([P, C], F32, "prod2", "prod1"), 2, et2, 0, whole)
-        put(scalar_move, 2, places[2], de2_rest, THIRD, THIRDS[1:])
-        de3_first = weigh(held([P, THIRD], F32, "de3_first"), 3, 0, THIRD)
-
-        et3_first = look_up_emb(nc.vector.tensor_copy, held([P, HELP], F32, "et3_first"), 3, 0, HELP)
-        et3_rest = look_up_emb(nc.vector.tensor_copy, held([P, C - HELP], F32, "et3_rest"), 3, HELP, C)
-        prod3 = held([P, C], F32, "prod3")
-        multiply(nc.gpsimd, prod3, 3, et3_first, 0, ((0, HELP),))
-        multiply(nc.vector, prod3, 3, et3_rest, HELP, ((HELP, HALF),) + quarters[2:])
+        et2_first = look_up_emb(scalar_move, held([P, QUARTER], F32, "et2_first"), 2, 0, QUARTER)
+        et2_rest = look_up_emb(scalar_move, held([P, C - QUARTER], F32, "et2_rest"), 2, QUARTER, C)
+        et3 = look_up_emb(scalar_move, held([P, C], F32, "et3"), 3, 0, C)
+        prod2 = held([P, C], F32, "prod2")
+        multiply(nc.gpsimd, prod2, 2, et2_first, 0, quarters[:1])
+        de2_mid = weigh(held([P, THIRD], F32, "de2_mid", "et2_first"), 2, *THIRDS[1])
+        multiply(nc.gpsimd, prod2, 2, et2_rest, QUARTER, ((QUARTER, C),))
+        put(scalar_move, 2, places[2], de2_mid, THIRD, THIRDS[1:2])
+        put(scalar_move, 2, places[2], de2_last, 2 * THIRD, THIRDS[2:])
+        multiply(nc.gpsimd, held([P, C], F32, "prod3"), 3, et3, 0, halves)
+        de3_rest = weigh(held([P, C - THIRD], F32, "de3_rest", "et3"), 3, THIRD, C)
         put(scalar_move, 3, places[0], de3_first, 0, THIRDS[:1])
-        de3_rest = weigh(held([P, C - THIRD], F32, "de3_rest", "prod3"), 3, THIRD, C)
         put(scalar_move, 3, places[0], de3_rest, THIRD, THIRDS[1:])
 
         dal_cols = [held([P, 2], F32, f"dal_cols{q}") for q in range(QUARTERS)]
@@ -237,10 +233,10 @@ def tile_attend_gmil_kernel(tc, eT, W, dz, al, offs, bagoffs, slotoffs, out_0, o
             nc.vector.tensor_tensor(w_row[:, lo:hi], dal_spread[:, :QUARTER], alpha[:, lo:hi], MULT)
 
         by_bag = held([P, C], F32, "by_bag")
-        uneven = ((0, C - THIRD), (C - THIRD, C))
+        uneven = ((0, HALF), (HALF, C - P), (C - P, C))
         for lo, hi in uneven:
             nc.vector.tensor_copy(by_bag[:, lo:hi], w_row[:].indirect(entries(slot_list, lo, hi)))
-        for engine, (lo, hi) in zip((nc.gpsimd, nc.vector), uneven):
+        for engine, (lo, hi) in zip((nc.gpsimd, nc.vector, nc.vector), uneven):
             slots = by_bag[:, lo:hi].rearrange("p (x j) -> p x j", j=2)
             engine.tensor_tensor(bag_sum[:, lo // 2 : hi // 2], slots[:, :, 0], slots[:, :, 1], ADD)
 

@@ -23,11 +23,11 @@ BLOCKS = D // P
 BANK = 512
 HALF = C // 2
 QUARTERS = 4
-SHARE = 480
 QUARTER = C // QUARTERS
 BAG_WINDOW = X + 17
 ALIGN = 256
 CAST_SPLIT = 160
+CLEAR_SPLIT = 768
 THIRD = 384
 THIRDS = ((0, THIRD), (THIRD, 2 * THIRD), (2 * THIRD, C))
 
@@ -46,6 +46,7 @@ def tile_attend_gmil_kernel(tc, eT, W, dz, al, offs, bagoffs, slotoffs, out_0, o
     with ExitStack() as ctx:
         lists = ctx.enter_context(tc.tile_pool(name="lists", bufs=1))
         keep = ctx.enter_context(tc.tile_pool(name="keep", bufs=1))
+        ring = ctx.enter_context(tc.tile_pool(name="ring", bufs=1))
         psum = ctx.enter_context(tc.psum_pool(name="psum", bufs=1))
 
         def held(shape, dtype, name, tag=None):
@@ -84,8 +85,6 @@ def tile_attend_gmil_kernel(tc, eT, W, dz, al, offs, bagoffs, slotoffs, out_0, o
         nc.sync.dma_start(emb_pair[:], eT[2 * P :, :].rearrange("(b p) t -> p b t", p=P))
         nc.sync.dma_start(slot_list[:], slotoffs)
 
-        identity = held([P, P], F32, "identity")
-        make_identity(nc, identity[:])
         u = [held([P, BAG_WINDOW], F32, f"u{b}") for b in range(BLOCKS)]
         bag_sum = held([P, BAG_WINDOW], F32, "bag_sum")
         for padded in u + [bag_sum]:
@@ -93,10 +92,10 @@ def tile_attend_gmil_kernel(tc, eT, W, dz, al, offs, bagoffs, slotoffs, out_0, o
         places = [held([P, T], F32, f"places{i}") for i in range(3)]
         nc.vector.memset(places[0][:, : T // 2 - 1], 0.0)
         nc.vector.memset(places[0][:, T // 2 - 1 :], 0.0)
-        nc.vector.memset(places[2][:, : T // 4 - 1], 0.0)
-        nc.vector.memset(places[2][:, T // 4 - 1 : T // 2], 0.0)
+        nc.vector.memset(places[2][:, : CLEAR_SPLIT // 2 - 1], 0.0)
+        nc.vector.memset(places[2][:, CLEAR_SPLIT // 2 - 1 : CLEAR_SPLIT], 0.0)
         nc.gpsimd.memset(places[1][:], 0.0)
-        nc.gpsimd.memset(places[2][:, T // 2 :], 0.0)
+        nc.gpsimd.memset(places[2][:, CLEAR_SPLIT:], 0.0)
 
         dz_codes = held([P, X], U32, "dz_codes")
         dz_scales = held([P, X], U8, "dz_scales")
@@ -141,6 +140,8 @@ def tile_attend_gmil_kernel(tc, eT, W, dz, al, offs, bagoffs, slotoffs, out_0, o
         product(1, X // 2, X, 3, nc.scalar.copy)
         quantize(w_codes, w_scales, E4M3X4, "w16_1", "dz_raw1", w_raw[1], 1, 2 * P)
 
+        identity = held([P, P], F32, "identity", "dz_raw1")
+        make_identity(nc, identity[:])
         turned = [bank(q, f"turned{q}") for q in range(QUARTERS)]
         ub = [held([P, C], F32, f"ub{b}") for b in range(BLOCKS)]
 
@@ -173,11 +174,14 @@ def tile_attend_gmil_kernel(tc, eT, W, dz, al, offs, bagoffs, slotoffs, out_0, o
                     )
                     opened.add(first // QUARTER)
 
-        def put(move, b, window, de, start, pieces):
+        def put(move, b, window, de, start, pieces, last=None):
             for lo, hi in pieces:
                 move(window[:].indirect(entries(idx_list, lo, hi)), de[:, lo - start : hi - start])
-                if hi == C:
+                if (hi == C) if last is None else last:
                     nc.sync.dma_start(out_0[b * P : (b + 1) * P, :], window[:])
+
+        def reused(columns, name, offset):
+            return ring.tile([P, columns], F32, name=name, align_bytes=ALIGN, offset=offset)
 
         whole = ((0, C),)
         halves = ((0, HALF), (HALF, C))
@@ -190,34 +194,34 @@ def tile_attend_gmil_kernel(tc, eT, W, dz, al, offs, bagoffs, slotoffs, out_0, o
         for lo, hi in halves:
             look_up_u(nc.vector.tensor_copy, 1, lo, hi)
         look_up_u(scalar_move, 2, 0, THIRD)
-        de2_first = weigh(held([P, THIRD], F32, "de2_first"), 2, 0, THIRD)
-        look_up_u(scalar_move, 2, THIRD, C - SHARE)
-        look_up_u(nc.vector.tensor_copy, 2, C - SHARE, C)
+        de2_early = weigh(held([P, THIRD], F32, "de2_early"), 2, 0, THIRD)
+        look_up_u(scalar_move, 2, THIRD, C - THIRD)
+        look_up_u(nc.vector.tensor_copy, 2, C - THIRD, C)
         for lo, hi in halves:
             look_up_u(scalar_move, 3, lo, hi)
         et1 = look_up_emb(nc.vector.tensor_copy, held([P, C], F32, "et1"), 1, 0, C)
         de1 = weigh(held([P, C], F32, "de1"), 1, 0, C)
         de3_first = weigh(held([P, THIRD], F32, "de3_first"), 3, 0, THIRD)
-        put(scalar_move, 2, places[2], de2_first, 0, THIRDS[:1])
+        put(scalar_move, 2, places[2], de2_early, 0, THIRDS[:1])
         put(nc.vector.tensor_copy, 0, places[0], de0, 0, whole)
         put(nc.vector.tensor_copy, 1, places[1], de1, 0, whole)
         multiply(nc.gpsimd, held([P, C], F32, "prod1"), 1, et1, 0, whole)
-        de2_last = weigh(held([P, C - 2 * THIRD], F32, "de2_last"), 2, *THIRDS[2])
 
         et0 = look_up_emb(scalar_move, held([P, C], F32, "et0"), 0, 0, C)
         multiply(nc.gpsimd, held([P, C], F32, "prod0"), 0, et0, 0, whole)
-        et2_first = look_up_emb(scalar_move, held([P, QUARTER], F32, "et2_first"), 2, 0, QUARTER)
+        et2_first = look_up_emb(scalar_move, reused(QUARTER, "et2_first", 4 * THIRD - ALIGN), 2, 0, QUARTER)
         et2_rest = look_up_emb(scalar_move, held([P, C - QUARTER], F32, "et2_rest"), 2, QUARTER, C)
         et3 = look_up_emb(scalar_move, held([P, C], F32, "et3"), 3, 0, C)
-        prod2 = held([P, C], F32, "prod2")
-        multiply(nc.gpsimd, prod2, 2, et2_first, 0, quarters[:1])
-        de2_mid = weigh(held([P, THIRD], F32, "de2_mid", "et2_first"), 2, *THIRDS[1])
-        multiply(nc.gpsimd, prod2, 2, et2_rest, QUARTER, ((QUARTER, C),))
-        put(scalar_move, 2, places[2], de2_mid, THIRD, THIRDS[1:2])
-        put(scalar_move, 2, places[2], de2_last, 2 * THIRD, THIRDS[2:])
-        multiply(nc.gpsimd, held([P, C], F32, "prod3"), 3, et3, 0, halves)
-        de3_rest = weigh(held([P, C - THIRD], F32, "de3_rest", "et3"), 3, THIRD, C)
+        multiply(nc.gpsimd, held([P, QUARTER], F32, "prod2_first"), 2, et2_first, 0, quarters[:1])
+        de2_late = weigh(reused(THIRD, "de2_late", 0), 2, C - THIRD, C)
+        multiply(nc.gpsimd, reused(C - QUARTER, "prod2_rest", 4 * THIRD), 2, et2_rest, QUARTER, ((QUARTER, C),))
+        put(scalar_move, 2, places[2], de2_late, C - THIRD, ((C - THIRD, C),), False)
+        multiply(nc.gpsimd, held([P, C], F32, "prod3", "prod2_first"), 3, et3, 0, halves)
+        de_last = held([P, C - 2 * THIRD + C - THIRD], F32, "de_last", "et3")
+        de2_last = weigh(de_last[:, : C - 2 * THIRD], 2, THIRD, C - THIRD)
+        de3_rest = weigh(de_last[:, C - 2 * THIRD :], 3, THIRD, C)
         put(scalar_move, 3, places[0], de3_first, 0, THIRDS[:1])
+        put(scalar_move, 2, places[2], de2_last, THIRD, ((THIRD, C - THIRD),), True)
         put(scalar_move, 3, places[0], de3_rest, THIRD, THIRDS[1:])
 
         dal_cols = [held([P, 2], F32, f"dal_cols{q}") for q in range(QUARTERS)]

@@ -28,6 +28,7 @@ BAG_WINDOW = X + 17
 ALIGN = 256
 CAST_SPLIT = 160
 CLEAR_SPLIT = 768
+W_SHARE = 192
 THIRD = 384
 THIRDS = ((0, THIRD), (THIRD, 2 * THIRD), (2 * THIRD, C))
 
@@ -217,12 +218,12 @@ def tile_attend_gmil_kernel(tc, eT, W, dz, al, offs, bagoffs, slotoffs, out_0, o
         multiply(nc.gpsimd, reused(C - QUARTER, "prod2_rest", 4 * THIRD), 2, et2_rest, QUARTER, ((QUARTER, C),))
         put(scalar_move, 2, places[2], de2_late, C - THIRD, ((C - THIRD, C),), False)
         multiply(nc.gpsimd, held([P, C], F32, "prod3", "prod2_first"), 3, et3, 0, halves)
-        de_last = held([P, C - 2 * THIRD + C - THIRD], F32, "de_last", "et3")
-        de2_last = weigh(de_last[:, : C - 2 * THIRD], 2, THIRD, C - THIRD)
-        de3_rest = weigh(de_last[:, C - 2 * THIRD :], 3, THIRD, C)
+        de_last = held([P, 2, QUARTER], F32, "de_last", "et3")
+        de2_last = weigh(de_last[:, 0, :], 2, THIRD, C - THIRD)
+        de3_mid = weigh(de_last[:, 1, :], 3, THIRD, C - THIRD)
         put(scalar_move, 3, places[0], de3_first, 0, THIRDS[:1])
         put(scalar_move, 2, places[2], de2_last, THIRD, ((THIRD, C - THIRD),), True)
-        put(scalar_move, 3, places[0], de3_rest, THIRD, THIRDS[1:])
+        put(scalar_move, 3, places[0], de3_mid, THIRD, ((THIRD, C - THIRD),))
 
         dal_cols = [held([P, 2], F32, f"dal_cols{q}") for q in range(QUARTERS)]
         w_row = held([P, C], F32, "w_row")
@@ -237,9 +238,11 @@ def tile_attend_gmil_kernel(tc, eT, W, dz, al, offs, bagoffs, slotoffs, out_0, o
             nc.vector.tensor_tensor(w_row[:, lo:hi], dal_spread[:, :QUARTER], alpha[:, lo:hi], MULT)
 
         by_bag = held([P, C], F32, "by_bag")
-        uneven = ((0, HALF), (HALF, C - P), (C - P, C))
-        for lo, hi in uneven:
-            nc.vector.tensor_copy(by_bag[:, lo:hi], w_row[:].indirect(entries(slot_list, lo, hi)))
+        uneven = ((0, HALF), (HALF, C - W_SHARE), (C - W_SHARE, C))
+        for move, (lo, hi) in zip((nc.vector.tensor_copy, nc.vector.tensor_copy, scalar_move), uneven):
+            move(by_bag[:, lo:hi], w_row[:].indirect(entries(slot_list, lo, hi)))
+        de3_last = weigh(held([P, THIRD], F32, "de3_last", "dal_cols3"), 3, C - THIRD, C)
+        put(scalar_move, 3, places[0], de3_last, C - THIRD, ((C - THIRD, C),))
         for engine, (lo, hi) in zip((nc.gpsimd, nc.vector, nc.vector), uneven):
             slots = by_bag[:, lo:hi].rearrange("p (x j) -> p x j", j=2)
             engine.tensor_tensor(bag_sum[:, lo // 2 : hi // 2], slots[:, :, 0], slots[:, :, 1], ADD)

@@ -28,7 +28,6 @@ BAG_WINDOW = X + 17
 ALIGN = 256
 CAST_SPLIT = 160
 CLEAR_SPLIT = 768
-W_SHARE = 192
 THIRD = 384
 THIRDS = ((0, THIRD), (THIRD, 2 * THIRD), (2 * THIRD, C))
 
@@ -144,7 +143,8 @@ def tile_attend_gmil_kernel(tc, eT, W, dz, al, offs, bagoffs, slotoffs, out_0, o
         identity = held([P, P], F32, "identity", "dz_raw1")
         make_identity(nc, identity[:])
         turned = [bank(q, f"turned{q}") for q in range(QUARTERS)]
-        ub = [held([P, C], F32, f"ub{b}") for b in range(BLOCKS)]
+        ub_pair = held([P, 2, C], F32, "ub_pair")
+        ub = [held([P, C], F32, "ub0")[:], held([P, C], F32, "ub1")[:], ub_pair[:, 0, :], ub_pair[:, 1, :]]
 
         def look_up_u(move, b, lo, hi):
             move(ub[b][:, lo:hi], u[b][:].indirect(entries(bag_list, lo, hi)))
@@ -155,6 +155,11 @@ def tile_attend_gmil_kernel(tc, eT, W, dz, al, offs, bagoffs, slotoffs, out_0, o
 
         def weigh(de, b, lo, hi):
             nc.gpsimd.tensor_tensor(de[:, :], ub[b][:, lo:hi], alpha[:, lo:hi], MULT)
+            return de
+
+        def weigh_pair(de, lo, hi):
+            both = alpha[:, lo:hi].unsqueeze(1).to_broadcast([P, 2, hi - lo])
+            nc.gpsimd.tensor_tensor(de[:], ub_pair[:, :, lo:hi], both, MULT)
             return de
 
         opened = set()
@@ -194,36 +199,32 @@ def tile_attend_gmil_kernel(tc, eT, W, dz, al, offs, bagoffs, slotoffs, out_0, o
         product(3, 0, X, 5, nc.scalar.copy)
         for lo, hi in halves:
             look_up_u(nc.vector.tensor_copy, 1, lo, hi)
-        look_up_u(scalar_move, 2, 0, THIRD)
-        de2_early = weigh(held([P, THIRD], F32, "de2_early"), 2, 0, THIRD)
-        look_up_u(scalar_move, 2, THIRD, C - THIRD)
+        for b in (2, 3):
+            look_up_u(scalar_move, b, 0, HALF)
+        look_up_u(scalar_move, 2, HALF, C - THIRD)
         look_up_u(nc.vector.tensor_copy, 2, C - THIRD, C)
-        for lo, hi in halves:
-            look_up_u(scalar_move, 3, lo, hi)
+        look_up_u(scalar_move, 3, HALF, C)
         et1 = look_up_emb(nc.vector.tensor_copy, held([P, C], F32, "et1"), 1, 0, C)
         de1 = weigh(held([P, C], F32, "de1"), 1, 0, C)
-        de3_first = weigh(held([P, THIRD], F32, "de3_first"), 3, 0, THIRD)
-        put(scalar_move, 2, places[2], de2_early, 0, THIRDS[:1])
+        de_first = weigh_pair(held([P, 2, THIRD], F32, "de_first"), 0, THIRD)
         put(nc.vector.tensor_copy, 0, places[0], de0, 0, whole)
         put(nc.vector.tensor_copy, 1, places[1], de1, 0, whole)
         multiply(nc.gpsimd, held([P, C], F32, "prod1"), 1, et1, 0, whole)
 
         et0 = look_up_emb(scalar_move, held([P, C], F32, "et0"), 0, 0, C)
-        multiply(nc.gpsimd, held([P, C], F32, "prod0"), 0, et0, 0, whole)
-        et2_first = look_up_emb(scalar_move, reused(QUARTER, "et2_first", 4 * THIRD - ALIGN), 2, 0, QUARTER)
-        et2_rest = look_up_emb(scalar_move, held([P, C - QUARTER], F32, "et2_rest"), 2, QUARTER, C)
-        et3 = look_up_emb(scalar_move, held([P, C], F32, "et3"), 3, 0, C)
-        multiply(nc.gpsimd, held([P, QUARTER], F32, "prod2_first"), 2, et2_first, 0, quarters[:1])
-        de2_late = weigh(reused(THIRD, "de2_late", 0), 2, C - THIRD, C)
-        multiply(nc.gpsimd, reused(C - QUARTER, "prod2_rest", 4 * THIRD), 2, et2_rest, QUARTER, ((QUARTER, C),))
+        put(scalar_move, 2, places[2], de_first[:, 0, :], 0, THIRDS[:1])
+        et2, et3 = [look_up_emb(scalar_move, held([P, C], F32, f"et{b}"), b, 0, C) for b in (2, 3)]
+        multiply(nc.gpsimd, reused(C, "prod0", 2 * C), 0, et0, 0, whole)
+        de2_late = weigh(held([P, THIRD], F32, "de2_late", "et0"), 2, C - THIRD, C)
+        multiply(nc.gpsimd, reused(C, "prod2", 0), 2, et2, 0, whole)
         put(scalar_move, 2, places[2], de2_late, C - THIRD, ((C - THIRD, C),), False)
-        multiply(nc.gpsimd, held([P, C], F32, "prod3", "prod2_first"), 3, et3, 0, halves)
-        de_last = held([P, 2, QUARTER], F32, "de_last", "et3")
-        de2_last = weigh(de_last[:, 0, :], 2, THIRD, C - THIRD)
-        de3_mid = weigh(de_last[:, 1, :], 3, THIRD, C - THIRD)
-        put(scalar_move, 3, places[0], de3_first, 0, THIRDS[:1])
+        multiply(nc.gpsimd, reused(C, "prod3", 4 * C), 3, et3, 0, halves)
+        de_last = held([P, C - THIRD + C - 2 * THIRD], F32, "de_last", "et3")
+        de2_last = weigh(de_last[:, C - THIRD :], 2, THIRD, C - THIRD)
+        de3_rest = weigh(de_last[:, : C - THIRD], 3, THIRD, C)
+        put(scalar_move, 3, places[0], de_first[:, 1, :], 0, THIRDS[:1])
         put(scalar_move, 2, places[2], de2_last, THIRD, ((THIRD, C - THIRD),), True)
-        put(scalar_move, 3, places[0], de3_mid, THIRD, ((THIRD, C - THIRD),))
+        put(scalar_move, 3, places[0], de3_rest, THIRD, THIRDS[1:])
 
         dal_cols = [held([P, 2], F32, f"dal_cols{q}") for q in range(QUARTERS)]
         w_row = held([P, C], F32, "w_row")
@@ -238,11 +239,9 @@ def tile_attend_gmil_kernel(tc, eT, W, dz, al, offs, bagoffs, slotoffs, out_0, o
             nc.vector.tensor_tensor(w_row[:, lo:hi], dal_spread[:, :QUARTER], alpha[:, lo:hi], MULT)
 
         by_bag = held([P, C], F32, "by_bag")
-        uneven = ((0, HALF), (HALF, C - W_SHARE), (C - W_SHARE, C))
-        for move, (lo, hi) in zip((nc.vector.tensor_copy, nc.vector.tensor_copy, scalar_move), uneven):
-            move(by_bag[:, lo:hi], w_row[:].indirect(entries(slot_list, lo, hi)))
-        de3_last = weigh(held([P, THIRD], F32, "de3_last", "dal_cols3"), 3, C - THIRD, C)
-        put(scalar_move, 3, places[0], de3_last, C - THIRD, ((C - THIRD, C),))
+        uneven = ((0, HALF), (HALF, C - P), (C - P, C))
+        for lo, hi in uneven:
+            nc.vector.tensor_copy(by_bag[:, lo:hi], w_row[:].indirect(entries(slot_list, lo, hi)))
         for engine, (lo, hi) in zip((nc.gpsimd, nc.vector, nc.vector), uneven):
             slots = by_bag[:, lo:hi].rearrange("p (x j) -> p x j", j=2)
             engine.tensor_tensor(bag_sum[:, lo // 2 : hi // 2], slots[:, :, 0], slots[:, :, 1], ADD)

@@ -201,8 +201,8 @@ def tile_attend_gmil_kernel(tc, eT, W, dz, al, offs, bagoffs, slotoffs, out_0, o
             look_up_u(nc.vector.tensor_copy, 1, lo, hi)
         for b in (2, 3):
             look_up_u(scalar_move, b, 0, HALF)
-        look_up_u(scalar_move, 2, HALF, C - THIRD)
-        look_up_u(nc.vector.tensor_copy, 2, C - THIRD, C)
+        look_up_u(scalar_move, 2, HALF, C - QUARTER)
+        look_up_u(nc.vector.tensor_copy, 2, C - QUARTER, C)
         look_up_u(scalar_move, 3, HALF, C)
         et1 = look_up_emb(nc.vector.tensor_copy, held([P, C], F32, "et1"), 1, 0, C)
         de1 = weigh(held([P, C], F32, "de1"), 1, 0, C)

@@ -28,6 +28,7 @@ BAG_WINDOW = X + 17
 ALIGN = 256
 CAST_SPLIT = 160
 CLEAR_SPLIT = 768
+SHARE = 192
 THIRD = 384
 THIRDS = ((0, THIRD), (THIRD, 2 * THIRD), (2 * THIRD, C))
 
@@ -117,18 +118,20 @@ def tile_attend_gmil_kernel(tc, eT, W, dz, al, offs, bagoffs, slotoffs, out_0, o
                     in_=grouped[:, lo : lo + P, :].rearrange("p c t -> p (c t)"),
                 )
 
-        def product(b, lo, hi, i, copy_out):
+        def product(b, lo, hi, i, copy_out, width=BANK):
             acc = bank(i, f"acc{b}_{lo}")
             cols = slice(b * P, (b + 1) * P)
-            nc.tensor.matmul_mx(
-                out=acc[:, : hi - lo],
-                lhsT=w_codes[:, cols].bitcast(E4M3X4),
-                lhsT_scale=w_scales[:, cols],
-                rhs=dz_codes[:, lo:hi].bitcast(E5M2X4),
-                rhs_scale=dz_scales[:, lo:hi],
-                start=True,
-                stop=True,
-            )
+            for first in range(lo, hi, width):
+                last = min(first + width, hi)
+                nc.tensor.matmul_mx(
+                    out=acc[:, first - lo : last - lo],
+                    lhsT=w_codes[:, cols].bitcast(E4M3X4),
+                    lhsT_scale=w_scales[:, cols],
+                    rhs=dz_codes[:, first:last].bitcast(E5M2X4),
+                    rhs_scale=dz_scales[:, first:last],
+                    start=True,
+                    stop=True,
+                )
             copy_out(u[b][:, lo:hi], acc[:, : hi - lo])
 
         quantize(w_codes, w_scales, E4M3X4, "w16_0", None, w_raw[0], 0, 0)
@@ -136,7 +139,7 @@ def tile_attend_gmil_kernel(tc, eT, W, dz, al, offs, bagoffs, slotoffs, out_0, o
         quantize(dz_codes, dz_scales, E5M2X4, "dz16_1", "dz_raw0", dz_raw[1], 1)
         product(0, 0, X // 2, 0, nc.scalar.copy)
         product(1, 0, X // 2, 1, nc.scalar.copy)
-        product(0, X // 2, X, 2, nc.scalar.copy)
+        product(0, X // 2, X, 2, nc.scalar.copy, P)
         product(1, X // 2, X, 3, nc.scalar.copy)
         quantize(w_codes, w_scales, E4M3X4, "w16_1", "dz_raw1", w_raw[1], 1, 2 * P)
 
@@ -201,8 +204,8 @@ def tile_attend_gmil_kernel(tc, eT, W, dz, al, offs, bagoffs, slotoffs, out_0, o
             look_up_u(nc.vector.tensor_copy, 1, lo, hi)
         for b in (2, 3):
             look_up_u(scalar_move, b, 0, HALF)
-        look_up_u(scalar_move, 2, HALF, C - QUARTER)
-        look_up_u(nc.vector.tensor_copy, 2, C - QUARTER, C)
+        look_up_u(scalar_move, 2, HALF, C - SHARE)
+        look_up_u(nc.vector.tensor_copy, 2, C - SHARE, C)
         look_up_u(scalar_move, 3, HALF, C)
         et1 = look_up_emb(nc.vector.tensor_copy, held([P, C], F32, "et1"), 1, 0, C)
         de1 = weigh(held([P, C], F32, "de1"), 1, 0, C)
@@ -211,14 +214,14 @@ def tile_attend_gmil_kernel(tc, eT, W, dz, al, offs, bagoffs, slotoffs, out_0, o
         put(nc.vector.tensor_copy, 1, places[1], de1, 0, whole)
         multiply(nc.gpsimd, held([P, C], F32, "prod1"), 1, et1, 0, whole)
 
-        et0 = look_up_emb(scalar_move, held([P, C], F32, "et0"), 0, 0, C)
+        et0 = look_up_emb(scalar_move, reused(C, "et0", 4 * C - 5 * ALIGN), 0, 0, C)
         put(scalar_move, 2, places[2], de_first[:, 0, :], 0, THIRDS[:1])
         et2, et3 = [look_up_emb(scalar_move, held([P, C], F32, f"et{b}"), b, 0, C) for b in (2, 3)]
-        multiply(nc.gpsimd, reused(C, "prod0", 2 * C), 0, et0, 0, whole)
-        de2_late = weigh(held([P, THIRD], F32, "de2_late", "et0"), 2, C - THIRD, C)
+        multiply(nc.gpsimd, held([P, C], F32, "prod0"), 0, et0, 0, whole)
+        de2_late = weigh(reused(THIRD, "de2_late", 4 * C), 2, C - THIRD, C)
         multiply(nc.gpsimd, reused(C, "prod2", 0), 2, et2, 0, whole)
         put(scalar_move, 2, places[2], de2_late, C - THIRD, ((C - THIRD, C),), False)
-        multiply(nc.gpsimd, reused(C, "prod3", 4 * C), 3, et3, 0, halves)
+        multiply(nc.gpsimd, reused(C, "prod3", 4 * (C + THIRD)), 3, et3, 0, halves)
         de_last = held([P, C - THIRD + C - 2 * THIRD], F32, "de_last", "et3")
         de2_last = weigh(de_last[:, C - THIRD :], 2, THIRD, C - THIRD)
         de3_rest = weigh(de_last[:, : C - THIRD], 3, THIRD, C)

@@ -28,7 +28,7 @@ BAG_WINDOW = X + 17
 ALIGN = 256
 CAST_SPLIT = 160
 CLEAR_SPLIT = 768
-SHARE = 192
+SHARE = 224
 THIRD = 384
 THIRDS = ((0, THIRD), (THIRD, 2 * THIRD), (2 * THIRD, C))
 

@@ -21,16 +21,16 @@ PACK = 4
 M, D, C, T, X = 512, 512, 1024, 2048, 512
 BLOCKS = D // P
 BANK = 512
+WORD = 4
+ALIGN = 256
 HALF = C // 2
 QUARTERS = 4
 QUARTER = C // QUARTERS
+THIRD = 384
 BAG_WINDOW = X + 17
-ALIGN = 256
 CAST_SPLIT = 160
 CLEAR_SPLIT = 768
 SHARE = 224
-THIRD = 384
-THIRDS = ((0, THIRD), (THIRD, 2 * THIRD), (2 * THIRD, C))
 
 FLOPS = 2 * M * D * X
 
@@ -47,11 +47,14 @@ def tile_attend_gmil_kernel(tc, eT, W, dz, al, offs, bagoffs, slotoffs, out_0, o
     with ExitStack() as ctx:
         lists = ctx.enter_context(tc.tile_pool(name="lists", bufs=1))
         keep = ctx.enter_context(tc.tile_pool(name="keep", bufs=1))
-        ring = ctx.enter_context(tc.tile_pool(name="ring", bufs=1))
+        shared = ctx.enter_context(tc.tile_pool(name="shared", bufs=1))
         psum = ctx.enter_context(tc.psum_pool(name="psum", bufs=1))
 
         def held(shape, dtype, name, tag=None):
             return keep.tile(shape, dtype, name=name, tag=tag or name, align_bytes=ALIGN)
+
+        def placed(columns, name, offset):
+            return shared.tile([P, columns], F32, name=name, align_bytes=ALIGN, offset=offset)
 
         def bank(i, name):
             return psum.tile([P, BANK], F32, name=name, tag=f"bank{i}")
@@ -103,13 +106,12 @@ def tile_attend_gmil_kernel(tc, eT, W, dz, al, offs, bagoffs, slotoffs, out_0, o
         w_codes = held([P, D], U32, "w_codes")
         w_scales = held([P, D], U8, "w_scales")
 
-        def quantize(codes, scales, fmt, name, tag, raw, h, split=CAST_SPLIT):
+        def quantize(codes, scales, fmt, name, tag, raw, h, vector_parts, scalar_parts):
             grouped = held([P, 2 * P, PACK], BF16, name, tag)
-            for lo, hi in ((0, min(split, P)), (P, split)):
-                if hi > lo:
-                    interleave(nc.vector.tensor_copy, grouped, raw, lo, hi)
-            if split < 2 * P:
-                interleave(nc.scalar.copy, grouped, raw, split, 2 * P)
+            for lo, hi in vector_parts:
+                interleave(nc.vector.tensor_copy, grouped, raw, lo, hi)
+            for lo, hi in scalar_parts:
+                interleave(nc.scalar.copy, grouped, raw, lo, hi)
             for lo in (0, P):
                 cols = slice(2 * h * P + lo, 2 * h * P + lo + P)
                 nc.vector.quantize_mx(
@@ -118,7 +120,7 @@ def tile_attend_gmil_kernel(tc, eT, W, dz, al, offs, bagoffs, slotoffs, out_0, o
                     in_=grouped[:, lo : lo + P, :].rearrange("p c t -> p (c t)"),
                 )
 
-        def product(b, lo, hi, i, copy_out, width=BANK):
+        def product(b, lo, hi, i, width=BANK):
             acc = bank(i, f"acc{b}_{lo}")
             cols = slice(b * P, (b + 1) * P)
             for first in range(lo, hi, width):
@@ -132,74 +134,66 @@ def tile_attend_gmil_kernel(tc, eT, W, dz, al, offs, bagoffs, slotoffs, out_0, o
                     start=True,
                     stop=True,
                 )
-            copy_out(u[b][:, lo:hi], acc[:, : hi - lo])
+            nc.scalar.copy(u[b][:, lo:hi], acc[:, : hi - lo])
 
-        quantize(w_codes, w_scales, E4M3X4, "w16_0", None, w_raw[0], 0, 0)
-        quantize(dz_codes, dz_scales, E5M2X4, "dz16_0", None, dz_raw[0], 0)
-        quantize(dz_codes, dz_scales, E5M2X4, "dz16_1", "dz_raw0", dz_raw[1], 1)
-        product(0, 0, X // 2, 0, nc.scalar.copy)
-        product(1, 0, X // 2, 1, nc.scalar.copy)
-        product(0, X // 2, X, 2, nc.scalar.copy, P)
-        product(1, X // 2, X, 3, nc.scalar.copy)
-        quantize(w_codes, w_scales, E4M3X4, "w16_1", "dz_raw1", w_raw[1], 1, 2 * P)
+        dz_vector, dz_scalar = ((0, P), (P, CAST_SPLIT)), ((CAST_SPLIT, 2 * P),)
+        quantize(w_codes, w_scales, E4M3X4, "w16_0", None, w_raw[0], 0, (), ((0, 2 * P),))
+        quantize(dz_codes, dz_scales, E5M2X4, "dz16_0", None, dz_raw[0], 0, dz_vector, dz_scalar)
+        quantize(dz_codes, dz_scales, E5M2X4, "dz16_1", "dz_raw0", dz_raw[1], 1, dz_vector, dz_scalar)
+        product(0, 0, X // 2, 0)
+        product(1, 0, X // 2, 1)
+        product(0, X // 2, X, 2, P)
+        product(1, X // 2, X, 3)
+        quantize(w_codes, w_scales, E4M3X4, "w16_1", "dz_raw1", w_raw[1], 1, ((0, P), (P, 2 * P)), ())
 
         identity = held([P, P], F32, "identity", "dz_raw1")
         make_identity(nc, identity[:])
+
         turned = [bank(q, f"turned{q}") for q in range(QUARTERS)]
         ub_pair = held([P, 2, C], F32, "ub_pair")
         ub = [held([P, C], F32, "ub0")[:], held([P, C], F32, "ub1")[:], ub_pair[:, 0, :], ub_pair[:, 1, :]]
+        first_block, last_block = 1, 3
 
         def look_up_u(move, b, lo, hi):
             move(ub[b][:, lo:hi], u[b][:].indirect(entries(bag_list, lo, hi)))
 
-        def look_up_emb(move, looked_up, b, lo, hi):
-            move(looked_up[:], emb[b].indirect(entries(idx_list, lo, hi)))
-            return looked_up
+        def look_up_emb(move, et, b):
+            move(et[:], emb[b].indirect(entries(idx_list, 0, C)))
+            return et
 
         def weigh(de, b, lo, hi):
             nc.gpsimd.tensor_tensor(de[:, :], ub[b][:, lo:hi], alpha[:, lo:hi], MULT)
             return de
 
-        def weigh_pair(de, lo, hi):
-            both = alpha[:, lo:hi].unsqueeze(1).to_broadcast([P, 2, hi - lo])
-            nc.gpsimd.tensor_tensor(de[:], ub_pair[:, :, lo:hi], both, MULT)
-            return de
-
-        opened = set()
-
-        def multiply(engine, prod, b, et, start, pieces):
+        def multiply(prod, b, et, pieces):
             for lo, hi in pieces:
-                shift = lo if prod.shape[1] < C else 0
-                engine.tensor_tensor(prod[:, lo - shift : hi - shift], ub[b][:, lo:hi], et[:, lo - start : hi - start], MULT)
+                nc.gpsimd.tensor_tensor(prod[:, lo:hi], ub[b][:, lo:hi], et[:, lo:hi], MULT)
                 for first in range(lo, hi, P):
                     col = first % QUARTER
                     nc.tensor.matmul(
                         turned[first // QUARTER][:, col : col + P],
-                        prod[:, first - shift : first - shift + P],
+                        prod[:, first : first + P],
                         identity[:],
-                        start=(first // QUARTER not in opened),
-                        stop=(b == BLOCKS - 1 and col == QUARTER - P),
+                        start=(b == first_block and col == 0),
+                        stop=(b == last_block and col == QUARTER - P),
                         is_transpose=True,
                     )
-                    opened.add(first // QUARTER)
 
-        def put(move, b, window, de, start, pieces, last=None):
-            for lo, hi in pieces:
-                move(window[:].indirect(entries(idx_list, lo, hi)), de[:, lo - start : hi - start])
-                if (hi == C) if last is None else last:
-                    nc.sync.dma_start(out_0[b * P : (b + 1) * P, :], window[:])
+        def put(move, window, de, lo, hi):
+            move(window[:].indirect(entries(idx_list, lo, hi)), de)
 
-        def reused(columns, name, offset):
-            return ring.tile([P, columns], F32, name=name, align_bytes=ALIGN, offset=offset)
+        def store(b, window, queue=nc.sync):
+            queue.dma_start(out_0[b * P : (b + 1) * P, :], window[:])
 
         whole = ((0, C),)
         halves = ((0, HALF), (HALF, C))
         quarters = tuple((q * QUARTER, (q + 1) * QUARTER) for q in range(QUARTERS))
+
         look_up_u(scalar_move, 0, 0, HALF)
         look_up_u(nc.vector.tensor_copy, 0, HALF, C)
         de0 = weigh(held([P, C], F32, "de0"), 0, 0, C)
-        product(2, 0, X, 4, nc.scalar.copy)
-        product(3, 0, X, 5, nc.scalar.copy)
+        product(2, 0, X, 4)
+        product(3, 0, X, 5)
         for lo, hi in halves:
             look_up_u(nc.vector.tensor_copy, 1, lo, hi)
         for b in (2, 3):
@@ -207,27 +201,37 @@ def tile_attend_gmil_kernel(tc, eT, W, dz, al, offs, bagoffs, slotoffs, out_0, o
         look_up_u(scalar_move, 2, HALF, C - SHARE)
         look_up_u(nc.vector.tensor_copy, 2, C - SHARE, C)
         look_up_u(scalar_move, 3, HALF, C)
-        et1 = look_up_emb(nc.vector.tensor_copy, held([P, C], F32, "et1"), 1, 0, C)
+        et1 = look_up_emb(nc.vector.tensor_copy, held([P, C], F32, "et1"), 1)
         de1 = weigh(held([P, C], F32, "de1"), 1, 0, C)
-        de_first = weigh_pair(held([P, 2, THIRD], F32, "de_first"), 0, THIRD)
-        put(nc.vector.tensor_copy, 0, places[0], de0, 0, whole)
-        put(nc.vector.tensor_copy, 1, places[1], de1, 0, whole)
-        multiply(nc.gpsimd, held([P, C], F32, "prod1"), 1, et1, 0, whole)
+        de_first = held([P, 2, THIRD], F32, "de_first")
+        alpha_twice = alpha[:, :THIRD].unsqueeze(1).to_broadcast([P, 2, THIRD])
+        nc.gpsimd.tensor_tensor(de_first[:], ub_pair[:, :, :THIRD], alpha_twice, MULT)
+        for b, de in enumerate((de0, de1)):
+            put(nc.vector.tensor_copy, places[b], de[:, :], 0, C)
+            store(b, places[b])
+        multiply(held([P, C], F32, "prod1"), 1, et1, whole)
 
-        et0 = look_up_emb(scalar_move, reused(C, "et0", 4 * C - 5 * ALIGN), 0, 0, C)
-        put(scalar_move, 2, places[2], de_first[:, 0, :], 0, THIRDS[:1])
-        et2, et3 = [look_up_emb(scalar_move, held([P, C], F32, f"et{b}"), b, 0, C) for b in (2, 3)]
-        multiply(nc.gpsimd, held([P, C], F32, "prod0"), 0, et0, 0, whole)
-        de2_late = weigh(reused(THIRD, "de2_late", 4 * C), 2, C - THIRD, C)
-        multiply(nc.gpsimd, reused(C, "prod2", 0), 2, et2, 0, whole)
-        put(scalar_move, 2, places[2], de2_late, C - THIRD, ((C - THIRD, C),), False)
-        multiply(nc.gpsimd, reused(C, "prod3", 4 * (C + THIRD)), 3, et3, 0, halves)
-        de_last = held([P, C - THIRD + C - 2 * THIRD], F32, "de_last", "et3")
+        prod2_at = 0
+        de2_late_at = prod2_at + WORD * C
+        prod3_at = de2_late_at + WORD * THIRD
+        et0_at = de2_late_at - WORD * (C - THIRD) // 2
+        et0 = look_up_emb(scalar_move, placed(C, "et0", et0_at), 0)
+        put(scalar_move, places[2], de_first[:, 0, :], 0, THIRD)
+        et2, et3 = [look_up_emb(scalar_move, held([P, C], F32, f"et{b}"), b) for b in (2, 3)]
+        multiply(held([P, C], F32, "prod0"), 0, et0, whole)
+        de2_late = weigh(placed(THIRD, "de2_late", de2_late_at), 2, C - THIRD, C)
+        multiply(placed(C, "prod2", prod2_at), 2, et2, whole)
+        put(scalar_move, places[2], de2_late[:, :], C - THIRD, C)
+        multiply(placed(C, "prod3", prod3_at), 3, et3, halves)
+        de_last = held([P, C - THIRD + QUARTER], F32, "de_last", "et3")
         de2_last = weigh(de_last[:, C - THIRD :], 2, THIRD, C - THIRD)
         de3_rest = weigh(de_last[:, : C - THIRD], 3, THIRD, C)
-        put(scalar_move, 3, places[0], de_first[:, 1, :], 0, THIRDS[:1])
-        put(scalar_move, 2, places[2], de2_last, THIRD, ((THIRD, C - THIRD),), True)
-        put(scalar_move, 3, places[0], de3_rest, THIRD, THIRDS[1:])
+        put(scalar_move, places[0], de_first[:, 1, :], 0, THIRD)
+        put(scalar_move, places[2], de2_last[:, :], THIRD, C - THIRD)
+        store(2, places[2])
+        put(scalar_move, places[0], de3_rest[:, :THIRD], THIRD, 2 * THIRD)
+        put(scalar_move, places[0], de3_rest[:, THIRD:], 2 * THIRD, C)
+        store(3, places[0], nc.scalar)
 
         dal_cols = [held([P, 2], F32, f"dal_cols{q}") for q in range(QUARTERS)]
         w_row = held([P, C], F32, "w_row")

from contextlib import ExitStack

import concourse.mybir as mybir
from concourse.masks import make_identity

F32 = mybir.dt.float32
BF16 = mybir.dt.bfloat16
U32 = mybir.dt.uint32
U16 = mybir.dt.uint16
U8 = mybir.dt.uint8
E4M3X4 = mybir.dt.float8_e4m3fn_x4
E5M2X4 = mybir.dt.float8_e5m2_x4
MULT = mybir.AluOpType.mult
ADD = mybir.AluOpType.add
SUBTRACT = mybir.AluOpType.subtract
COPY = mybir.ActivationFunctionType.Copy
AXIS_X = mybir.AxisListType.X

P = 128
PACK = 4
M, D, C, T, X = 512, 512, 1024, 2048, 512
BLOCKS = D // P
BANK = 512
WORD = 4
ALIGN = 256
HALF = C // 2
QUARTERS = 4
QUARTER = C // QUARTERS
THIRD = 384
BAG_WINDOW = X + 17
CAST_SPLIT = 160
CLEAR_SPLIT = 768
SHARE = 224

FLOPS = 2 * M * D * X


def interleave(engine_copy, grouped, raw, lo, hi):
    engine_copy(
        grouped[:, lo:hi, :].rearrange("p (c i) t -> p c t i", i=4),
        raw[:, :, lo:hi].rearrange("p t (c i) -> p c t i", i=4),
    )


def tile_attend_gmil_kernel(tc, eT, W, dz, al, offs, bagoffs, slotoffs, out_0, out_1):
    nc = tc.nc
    with ExitStack() as ctx:
        lists = ctx.enter_context(tc.tile_pool(name="lists", bufs=1))
        keep = ctx.enter_context(tc.tile_pool(name="keep", bufs=1))
        shared = ctx.enter_context(tc.tile_pool(name="shared", bufs=1))
        psum = ctx.enter_context(tc.psum_pool(name="psum", bufs=1))

        def held(shape, dtype, name, tag=None):
            return keep.tile(shape, dtype, name=name, tag=tag or name, align_bytes=ALIGN)

        def placed(columns, name, offset):
            return shared.tile([P, columns], F32, name=name, align_bytes=ALIGN, offset=offset)

        def bank(i, name):
            return psum.tile([P, BANK], F32, name=name, tag=f"bank{i}")

        def scalar_move(dst, src):
            nc.scalar.activation(dst, src, COPY)

        def entries(listed, lo, hi):
            return listed[:, lo // 16 : hi // 16]

        dz_rows = dz.rearrange("(p j) x -> p j x", j=PACK)
        w_rows = W.rearrange("(p j) d -> p j d", j=PACK)

        dz_raw = [held([P, PACK, 2 * P], F32, f"dz_raw{h}") for h in range(2)]
        w_raw = [held([P, PACK, 2 * P], F32, f"w_raw{h}") for h in range(2)]
        idx_list = lists.tile([P, C // 16], U16, name="idx_list", align_bytes=ALIGN)
        bag_list = lists.tile([P, C // 16], U16, name="bag_list", align_bytes=ALIGN)
        slot_list = lists.tile([P, C // 16], U16, name="slot_list", align_bytes=ALIGN)
        emb_pair = held([P, 2, T], F32, "emb_pair")
        emb = [held([P, T], F32, "emb0")[:], held([P, T], F32, "emb1")[:], emb_pair[:, 0, :], emb_pair[:, 1, :]]
        alpha = held([P, C], F32, "alpha")

        nc.sync.dma_start(w_raw[0][:], w_rows[:, :, : 2 * P])
        nc.sync.dma_start(dz_raw[0][:], dz_rows[:, :, : 2 * P])
        nc.sync.dma_start(dz_raw[1][:], dz_rows[:, :, 2 * P :])
        nc.sync.dma_start(w_raw[1][:], w_rows[:, :, 2 * P :])
        nc.sync.dma_start(bag_list[:], bagoffs)
        nc.sync.dma_start(alpha[:], al)
        nc.sync.dma_start(idx_list[:], offs)
        for b in (1, 0):
            nc.sync.dma_start(emb[b], eT[b * P : (b + 1) * P, :])
        nc.sync.dma_start(emb_pair[:], eT[2 * P :, :].rearrange("(b p) t -> p b t", p=P))
        nc.sync.dma_start(slot_list[:], slotoffs)

        u = [held([P, BAG_WINDOW], F32, f"u{b}") for b in range(BLOCKS)]
        bag_sum = held([P, BAG_WINDOW], F32, "bag_sum")
        for padded in u + [bag_sum]:
            nc.vector.memset(padded[:, X:], 0.0)
        places = [held([P, T], F32, f"places{i}") for i in range(3)]
        nc.vector.memset(places[0][:, : T // 2 - 1], 0.0)
        nc.vector.memset(places[0][:, T // 2 - 1 :], 0.0)
        nc.vector.memset(places[2][:, : CLEAR_SPLIT // 2 - 1], 0.0)
        nc.vector.memset(places[2][:, CLEAR_SPLIT // 2 - 1 : CLEAR_SPLIT], 0.0)
        nc.gpsimd.memset(places[1][:], 0.0)
        nc.gpsimd.memset(places[2][:, CLEAR_SPLIT:], 0.0)

        dz_codes = held([P, X], U32, "dz_codes")
        dz_scales = held([P, X], U8, "dz_scales")
        w_codes = held([P, D], U32, "w_codes")
        w_scales = held([P, D], U8, "w_scales")

        def quantize(codes, scales, fmt, name, tag, raw, h, vector_parts, scalar_parts):
            grouped = held([P, 2 * P, PACK], BF16, name, tag)
            for lo, hi in vector_parts:
                interleave(nc.vector.tensor_copy, grouped, raw, lo, hi)
            for lo, hi in scalar_parts:
                interleave(nc.scalar.copy, grouped, raw, lo, hi)
            for lo in (0, P):
                cols = slice(2 * h * P + lo, 2 * h * P + lo + P)
                nc.vector.quantize_mx(
                    out=codes[:, cols].bitcast(fmt),
                    scales=scales[:, cols],
                    in_=grouped[:, lo : lo + P, :].rearrange("p c t -> p (c t)"),
                )

        def product(b, lo, hi, i, width=BANK):
            acc = bank(i, f"acc{b}_{lo}")
            cols = slice(b * P, (b + 1) * P)
            for first in range(lo, hi, width):
                last = min(first + width, hi)
                nc.tensor.matmul_mx(
                    out=acc[:, first - lo : last - lo],
                    lhsT=w_codes[:, cols].bitcast(E4M3X4),
                    lhsT_scale=w_scales[:, cols],
                    rhs=dz_codes[:, first:last].bitcast(E5M2X4),
                    rhs_scale=dz_scales[:, first:last],
                    start=True,
                    stop=True,
                )
            nc.scalar.copy(u[b][:, lo:hi], acc[:, : hi - lo])

        dz_vector, dz_scalar = ((0, P), (P, CAST_SPLIT)), ((CAST_SPLIT, 2 * P),)
        quantize(w_codes, w_scales, E4M3X4, "w16_0", None, w_raw[0], 0, (), ((0, 2 * P),))
        quantize(dz_codes, dz_scales, E5M2X4, "dz16_0", None, dz_raw[0], 0, dz_vector, dz_scalar)
        quantize(dz_codes, dz_scales, E5M2X4, "dz16_1", "dz_raw0", dz_raw[1], 1, dz_vector, dz_scalar)
        product(0, 0, X // 2, 0)
        product(1, 0, X // 2, 1)
        product(0, X // 2, X, 2, P)
        product(1, X // 2, X, 3)
        quantize(w_codes, w_scales, E4M3X4, "w16_1", "dz_raw1", w_raw[1], 1, ((0, P), (P, 2 * P)), ())

        identity = held([P, P], F32, "identity", "dz_raw1")
        make_identity(nc, identity[:])

        turned = [bank(q, f"turned{q}") for q in range(QUARTERS)]
        ub_pair = held([P, 2, C], F32, "ub_pair")
        ub = [held([P, C], F32, "ub0")[:], held([P, C], F32, "ub1")[:], ub_pair[:, 0, :], ub_pair[:, 1, :]]
        first_block, last_block = 1, 3

        def look_up_u(move, b, lo, hi):
            move(ub[b][:, lo:hi], u[b][:].indirect(entries(bag_list, lo, hi)))

        def look_up_emb(move, et, b):
            move(et[:], emb[b].indirect(entries(idx_list, 0, C)))
            return et

        def weigh(de, b, lo, hi):
            nc.gpsimd.tensor_tensor(de[:, :], ub[b][:, lo:hi], alpha[:, lo:hi], MULT)
            return de

        def multiply(prod, b, et, pieces):
            for lo, hi in pieces:
                nc.gpsimd.tensor_tensor(prod[:, lo:hi], ub[b][:, lo:hi], et[:, lo:hi], MULT)
                for first in range(lo, hi, P):
                    col = first % QUARTER
                    nc.tensor.matmul(
                        turned[first // QUARTER][:, col : col + P],
                        prod[:, first : first + P],
                        identity[:],
                        start=(b == first_block and col == 0),
                        stop=(b == last_block and col == QUARTER - P),
                        is_transpose=True,
                    )

        def put(move, window, de, lo, hi):
            move(window[:].indirect(entries(idx_list, lo, hi)), de)

        def store(b, window, queue=nc.sync):
            queue.dma_start(out_0[b * P : (b + 1) * P, :], window[:])

        whole = ((0, C),)
        halves = ((0, HALF), (HALF, C))
        quarters = tuple((q * QUARTER, (q + 1) * QUARTER) for q in range(QUARTERS))

        look_up_u(scalar_move, 0, 0, HALF)
        look_up_u(nc.vector.tensor_copy, 0, HALF, C)
        de0 = weigh(held([P, C], F32, "de0"), 0, 0, C)
        product(2, 0, X, 4)
        product(3, 0, X, 5)
        for lo, hi in halves:
            look_up_u(nc.vector.tensor_copy, 1, lo, hi)
        for b in (2, 3):
            look_up_u(scalar_move, b, 0, HALF)
        look_up_u(scalar_move, 2, HALF, C - SHARE)
        look_up_u(nc.vector.tensor_copy, 2, C - SHARE, C)
        look_up_u(scalar_move, 3, HALF, C)
        et1 = look_up_emb(nc.vector.tensor_copy, held([P, C], F32, "et1"), 1)
        de1 = weigh(held([P, C], F32, "de1"), 1, 0, C)
        de_first = held([P, 2, THIRD], F32, "de_first")
        alpha_twice = alpha[:, :THIRD].unsqueeze(1).to_broadcast([P, 2, THIRD])
        nc.gpsimd.tensor_tensor(de_first[:], ub_pair[:, :, :THIRD], alpha_twice, MULT)
        for b, de in enumerate((de0, de1)):
            put(nc.vector.tensor_copy, places[b], de[:, :], 0, C)
            store(b, places[b])
        multiply(held([P, C], F32, "prod1"), 1, et1, whole)

        prod2_at = 0
        de2_late_at = prod2_at + WORD * C
        prod3_at = de2_late_at + WORD * THIRD
        et0_at = de2_late_at - WORD * (C - THIRD) // 2
        et0 = look_up_emb(scalar_move, placed(C, "et0", et0_at), 0)
        put(scalar_move, places[2], de_first[:, 0, :], 0, THIRD)
        et2, et3 = [look_up_emb(scalar_move, held([P, C], F32, f"et{b}"), b) for b in (2, 3)]
        multiply(held([P, C], F32, "prod0"), 0, et0, whole)
        de2_late = weigh(placed(THIRD, "de2_late", de2_late_at), 2, C - THIRD, C)
        multiply(placed(C, "prod2", prod2_at), 2, et2, whole)
        put(scalar_move, places[2], de2_late[:, :], C - THIRD, C)
        multiply(placed(C, "prod3", prod3_at), 3, et3, halves)
        de_last = held([P, C - THIRD + QUARTER], F32, "de_last", "et3")
        de2_last = weigh(de_last[:, C - THIRD :], 2, THIRD, C - THIRD)
        de3_rest = weigh(de_last[:, : C - THIRD], 3, THIRD, C)
        put(scalar_move, places[0], de_first[:, 1, :], 0, THIRD)
        put(scalar_move, places[2], de2_last[:, :], THIRD, C - THIRD)
        store(2, places[2])
        put(scalar_move, places[0], de3_rest[:, :THIRD], THIRD, 2 * THIRD)
        put(scalar_move, places[0], de3_rest[:, THIRD:], 2 * THIRD, C)
        store(3, places[0], nc.scalar)

        dal_cols = [held([P, 2], F32, f"dal_cols{q}") for q in range(QUARTERS)]
        w_row = held([P, C], F32, "w_row")
        for q in range(QUARTERS):
            sums = turned[q][:, :QUARTER].rearrange("p (k d) -> p k d", d=P)
            nc.vector.tensor_reduce(dal_cols[q][:], sums, AXIS_X, ADD)
        for q, (lo, hi) in enumerate(quarters):
            dal_spread = bank(QUARTERS + q, f"dal_spread{q}")
            for k in range(2):
                column = dal_cols[q][:, k : k + 1]
                nc.tensor.transpose(dal_spread[:, k * P : (k + 1) * P], column.to_broadcast([P, P]), identity[:])
            nc.vector.tensor_tensor(w_row[:, lo:hi], dal_spread[:, :QUARTER], alpha[:, lo:hi], MULT)

        by_bag = held([P, C], F32, "by_bag")
        uneven = ((0, HALF), (HALF, C - P), (C - P, C))
        for lo, hi in uneven:
            nc.vector.tensor_copy(by_bag[:, lo:hi], w_row[:].indirect(entries(slot_list, lo, hi)))
        for engine, (lo, hi) in zip((nc.gpsimd, nc.vector, nc.vector), uneven):
            slots = by_bag[:, lo:hi].rearrange("p (x j) -> p x j", j=2)
            engine.tensor_tensor(bag_sum[:, lo // 2 : hi // 2], slots[:, :, 0], slots[:, :, 1], ADD)

        taken = held([P, C], F32, "taken")
        result = held([P, C], F32, "result")
        for lo, hi in halves:
            nc.vector.tensor_tensor(taken[:, lo:hi], bag_sum[:].indirect(entries(bag_list, lo, hi)), alpha[:, lo:hi], MULT)
        for lo, hi in halves:
            nc.vector.tensor_tensor(result[0:1, lo:hi], w_row[0:1, lo:hi], taken[0:1, lo:hi], SUBTRACT)
        nc.sync.dma_start(out_1, result[0:1, :])
